import numpy as np, ml_dtypes
CORES = [10,34,74,98]
N = 4
BF = ml_dtypes.bfloat16
W, L, C, ST, H = 4096, 256, 16, 6, 1
def parts(rng):
    x = rng.integers(0, 256, (N, 8, 16, W)); z = rng.integers(0, 256, (N, 8, 16, L))
    p = rng.integers(0, W, (N, 8, 16, L)); r = rng.integers(0, W, (N, 8, 16, L))
    return x, p, r, z, rng.integers(1000, 1701, (N, 8))
def pack(x, p, r, z, t):
    return {"xt": np.ascontiguousarray(x.reshape(N, 128, W)).astype(np.float32).astype(BF), "pl": np.ascontiguousarray(p.reshape(N, 128, L)).astype(np.int32),
            "pr": np.ascontiguousarray(r.reshape(N, 128, L)).astype(np.int32), "z0": np.ascontiguousarray(z.reshape(N, 128, L)).astype(np.float32).astype(BF),
            "th": np.repeat(t, 16, axis=1).reshape(N, 128, 1).astype(np.int32)}
def setup_inputs(rng):
    return pack(*parts(rng))
def setup_inputs_spread(rng):
    x, p, r, z, t = parts(rng)
    x = np.floor(256 * np.exp2(-8 * rng.random((N, 8, 1, W))) * rng.random((N, 8, 16, W))); z = np.floor(256 * np.exp2(-8 * rng.random((N, 8, 1, L))) * rng.random((N, 8, 16, L)))
    w = []
    for _ in range(2):
        e = rng.choice(np.array([1.0, 2.0, 4.0]), (N, 8, 1, 1)); n = np.minimum(np.floor(W * rng.random((N, 8, 16, L)) ** e), W - 1).astype(np.int64)
        w.append(np.where(rng.random((N, 8, 1, 1)) < 0.5, n, W - 1 - n))
    t = np.minimum(np.floor(4080 * rng.random((N, 8)) ** 3), 4079)
    return pack(np.minimum(x, 255), w[0], w[1], np.minimum(z, 255), t)
def setup_inputs_ends(rng):
    x, p, r, z, t = parts(rng)
    def bits(n):
        v = 255 * rng.integers(0, 2, (N, 8, 16, n)); c = rng.random((N, 8, 1, n))
        return np.where(c < 0.25, 0, np.where(c > 0.75, 255, v))
    x = bits(W); z = bits(L)
    for g in range(8):
        if g in (0, 3, 7): x[:, g, :, 0] = 0
        elif g in (1, 4): x[:, g, :, 0] = 255
        elif g in (2, 5): x[:, g, :, 0] = 0; x[:, g, 15, 0] = 255
        else: x[:, g, :, 0] = 255 * rng.integers(0, 2, (N, 16))
        x[:, g, :, W - 1] = 255 - x[:, g, :, 0]
    p = np.where(rng.random(p.shape) < 0.8, (W - 1) * rng.integers(0, 2, p.shape), p); r = np.where(rng.random(r.shape) < 0.8, (W - 1) * rng.integers(0, 2, r.shape), r)
    t = 4079 * rng.integers(0, 2, (N, 8)); t[:, 0] = 4079; t[:, 7] = 0
    x[:, 7, :, W - 2] = 0; x[:, 7, 15, W - 2] = 255; z[:, 7, :, L - 1] = 0
    r[:, 7, :15, L - 1] = W - 1; r[:, 7, 15, L - 1] = 0; p[:, 7, :15, L - 1] = W - 1; p[:, 7, 15, L - 1] = W - 2
    z[:, 7, :, L - 2] = 0; r[:, 7, :, L - 2] = W - 1; p[:, 7, 0, L - 2] = 0; p[:, 7, 15, L - 2] = W - 1
    z[:, 1, :, 1] = 255; r[:, 1, :, 1] = W - 1; p[:, 1, 0, 1] = 0; p[:, 1, 15, 1] = W - 1
    return pack(x, p, r, z, t)
def setup_inputs_crowd(rng):
    x, p, r, z, t = parts(rng); x[..., 0] = 0; x[..., W - 1] = 255
    q = rng.integers(0, 16, (N, 8, 1, L)); m = (np.arange(16).reshape(1, 1, 16, 1) - q) & 15; lane = np.arange(L)
    b = rng.integers(0, 2, (N, 8, 1, L)); z = np.broadcast_to(255 * b, (N, 8, 16, L))
    far = np.where(rng.random(r.shape) < 0.5, (W - 1) * (1 - b), rng.integers(1, W - 1, r.shape))
    r = np.where(m == 0, (W - 1) * b, far)
    own = (W - 1) * rng.integers(0, 2, (N, 8, 1, L)); e = (m >= 1) & (m < 8)
    e[:, 1::2, :, L - 1] &= m[:, 1::2, :, L - 1] != 7
    e[:, 2] &= (m[:, 2] == 1) & (lane < 32); e[:, 3] &= (m[:, 3] == 1) & (lane < 31); e[:, 6] = False
    p = np.where(e, W - 1 - own, np.where(m < 8, own, p))
    return pack(x, p, r, z, rng.choice(np.array([0, 1000, 1400, 4079]), (N, 8)))
def setup_inputs_ties(rng):
    x, p, r, z, t = parts(rng)
    x = rng.integers(0, 4, x.shape); z = rng.integers(0, 4, z.shape); x[:, 1] += 252; x[:, 6] += 252; z[:, 6] += 252
    same = rng.random((N, 8, 1, L)) < 0.25
    p = np.where(same, np.roll(np.repeat(p[:, :, :4], 4, axis=2), 1, axis=2), p); r = np.where(same, np.tile(r[:, :, :4], (1, 1, 4, 1)), r)
    t = rng.integers(0, 19, (N, 8)); t[:, 3] = 0; near = np.array([3, 5, 7, 9, 19, 21])
    p[:, 3] = W - rng.choice(near, (N, 16, L)); r[:, 3] = W - rng.choice(near, (N, 16, L))
    return pack(x, p, r, z, t)
def setup_inputs_corners(rng):
    x, p, r, z, t = parts(rng); i = np.arange(L).reshape(1, 1, L); j = np.arange(16).reshape(1, 16, 1)
    p[:, 0] = rng.integers(0, W, (N, 16, 1)); r[:, 0] = rng.integers(0, W, (N, 16, 1))
    p[:, 1] = rng.integers(0, W, (N, 1, L)); r[:, 1] = rng.integers(0, W, (N, 1, L))
    p[:, 2] = C * i + (j & (C - 1)); r[:, 2] = C * i + (C - 1 - (j & (C - 1)))
    p[:, 3] = r[:, 3]
    p[:, 4] = ((W - 1) * (np.arange(N) & 1)).reshape(N, 1, 1); r[:, 4] = W - 1 - p[:, 4]
    o = np.argsort(rng.random((N, max(W, 16 * L))), axis=1)[:, :16 * L] & (W - 1)
    p[:, 5] = o.reshape(N, 16, L); r[:, 5] = W - 1 - p[:, 5, ::-1]
    p[:, 6] = C * ((i + 1) % L) + ((j + rng.integers(0, C, (N, 1, 1))) & (C - 1)); r[:, 6] = C * ((i + L - 1) % L) + ((j + rng.integers(0, C, (N, 1, 1))) & (C - 1))
    p[:, 7, :, :L - 1] = ((W - 1) * ((i + j) & 1))[:, :, :L - 1]; r[:, 7, :, :L - 1] = (W - 1) * (j & 1)
    t = rng.choice(np.array([0, 500, 1200, 2000, 4079]), (N, 8)); t[:, 5] = 2048
    z[:, 5] = 255 * rng.integers(0, 2, (N, 1, L)); z[:, 5, :, L - 1] = 0
    x[:, 5, :, 0] = 0; x[:, 5, :, W - 1] = 0; x[:, 5, :8, W - 1] = 255; x[:, 5, 8, W - 1] = 9
    r[:, 5, :8, L - 1] = W - 1; r[:, 5, 15, L - 1] = 0; p[:, 5, :7, L - 1] = W - 1; p[:, 5, 15, L - 1] = 0
    return pack(x, p, r, z, t)
def check_inputs(d):
    bad = []
    for k, lo, hi in (("xt", 0, 255), ("pl", 0, W - 1), ("pr", 0, W - 1), ("z0", 0, 255), ("th", 0, 4079)):
        a = np.asarray(d[k]).astype(np.float64)
        if not (np.min(a) >= lo and np.max(a) <= hi): bad.append("range of " + k)
        if np.any(a != np.floor(a)): bad.append("whole numbers in " + k)
    a = np.asarray(d["th"]).reshape(-1, 16)
    if np.any(a != a[:, :1]): bad.append("the 16 rows of a group in th are alike")
    return bad
def turn(q, s):
    return np.take_along_axis(q, (np.arange(16).reshape(1, 1, 16, 1) + s[:, :, None, :]) & 15, 2)
def items(x, n):
    return np.take_along_axis(x, n.reshape(N, 8, 1, 16 * L), 3).reshape(N, 8, 16, 16, L)
def reference(xt, pl, pr, z0, th):
    x = xt.astype(np.float32).astype(np.int64).reshape(N, 8, 16, W); z = z0.astype(np.float32).astype(np.int64).reshape(N, 8, 16, L)
    p = pl.astype(np.int64).reshape(N, 8, 16, L); r = pr.astype(np.int64).reshape(N, 8, 16, L)
    t = th.astype(np.int64).reshape(N, 8, 16)[:, :, 0]; a = np.zeros((N, 8), np.int64)
    for step in range(ST):
        d = np.add.reduce(np.abs(items(x, r) - z[:, :, :, None, :]), axis=2)
        k = np.argmin(d, axis=2)
        v = items(x, p); y = np.take_along_axis(v, k[:, :, None, None, :], 3)[:, :, :, 0, :]
        f = np.add.reduce(np.abs(v - y[:, :, :, None, :]), axis=2)
        p = turn(p, k); f = turn(f, k); r = turn(r, k + 1); d = turn(d, k + 1)
        lim = (t + (a & 31))[:, :, None, None]; left = f[:, :, 1:8] > lim; right = d[:, :, 1:8] > lim
        p1, p9, r1, r9 = p[:, :, 1:8], p[:, :, 9:16], r[:, :, 1:8], r[:, :, 9:16]
        new = ((p1 * r1 >> 5) + p1 + a[:, :, None, None]) & (W - 1)
        p = np.concatenate([p[:, :, :1], np.where(left, p9, p1), p[:, :, 8:9], np.where(left, new, p9)], axis=2)
        r = np.concatenate([r[:, :, :1], np.where(right, r9, r1), r[:, :, 8:9], np.where(right, r1, r9)], axis=2)
        u = np.add.reduce(y, axis=2)
        np.put_along_axis(x, (C * np.arange(L) + (u & (C - 1)))[:, :, None, :], (y + z) >> 1, 3)
        z = np.abs(y - z)
        if step < ST - 1:
            a = np.add.reduce(left.astype(np.int64), axis=(2, 3))
            p = np.roll(p, H, axis=0); r = np.roll(r, H, axis=0); z = np.roll(z, H, axis=0)
    return {"yx": x.reshape(N, 128, W).astype(np.float32).astype(BF), "yp": p.reshape(N, 128, L).astype(np.float32),
            "yr": r.reshape(N, 128, L).astype(np.float32), "yz": z.reshape(N, 128, L).astype(np.float32).astype(BF)}

@@ -1,0 +1,747 @@
+import numpy as np
+from concourse.bass import DstId, RemoteDMATransfer
+from concourse.mybir import AluOpType as ALU, ActivationFunctionType as AF
+
+ST = 6
+CFG = {
+    "H": 2,
+    "NA": (6, 6),
+    "XF": (0, 0),
+    "XFL": (0, 0),
+    "MIDSEP": 0,
+    "MP": 0,
+    "CPA": 0,
+    "g": 1.56, "sc": 3.8, "cy": 0.001, "pe": 0.0005, "wake": 0.07, "fix": 0.005, "afix": 0.06, "far": 2.3, "issue": 0.5,
+    "bw": 80e3, "row": 0.5, "rounds": 8, "BM": 1, "FIN": (0, 1, 1, 0, 0),
+    "seed": 0, "jit": 1.5, "win": 2.0, "search": 1500,
+    "models": ({}, {"far": 3.5, "issue": 0.8, "wake": 0.12, "bw": 100e3}, {"fix": 0.03, "afix": 0.1, "g": 1.2, "sc": 2.5},
+               {"g": 1.95, "sc": 5.0, "cy": 0.0011}),
+}
+
+SCRATCH = {
+    "X": ("sbuf", [128, 4096], "bfloat16"), "G": ("sbuf", [128, 4096], "bfloat16"),
+    "DD": ("sbuf", [128, 4096], "bfloat16"), "AB": ("sbuf", [128, 4096], "bfloat16"), "AF": ("sbuf", [128, 2048], "bfloat16"),
+    "zl": ("sbuf", [128, ST * 384], "bfloat16"), "zs": ("sbuf", [128, ST * 384], "bfloat16"),
+    "ql": ("sbuf", [128, ST * 256], "uint16"), "qs": ("sbuf", [128, ST * 256], "uint16"),
+    "B": ("sbuf", [128, ST * 288], "float32"), "pin": ("sbuf", [128, ST * 256], "int32"),
+    "PX": ("sbuf", [128, ST * 256], "int32"), "PY": ("sbuf", [128, ST * 256], "int32"),
+    "rawp": ("sbuf", [128, 256], "int32"), "rawq": ("sbuf", [128, 256], "int32"), "thi": ("sbuf", [128, 8], "int32"),
+    "wa": ("sbuf", [128, 512], "float32"), "wb": ("sbuf", [128, 512], "float32"),
+    "wc": ("sbuf", [128, 512], "float32"), "wd": ("sbuf", [128, 512], "float32"),
+    "qf": ("sbuf", [128, 256], "float32"), "pf": ("sbuf", [128, 256], "float32"),
+    "h16": ("sbuf", [128, 512], "float16"), "var": ("sbuf", [128, 4096], "float32"), "fin": ("sbuf", [128, 512], "float32"),
+    "ci": ("sbuf", [128, 256], "int32"), "cj": ("sbuf", [128, 128], "int32"), "col": ("sbuf", [128, 64], "float32"),
+    "idx": ("sbuf", [128, 272], "bfloat16"), "I": ("sbuf", [128, 128], "bfloat16"), "NI": ("sbuf", [128, 128], "bfloat16"),
+    "W1": ("sbuf", [128, 144], "bfloat16"), "W32": ("sbuf", [128, 144], "bfloat16"), "BO": ("sbuf", [128, 128], "bfloat16"),
+    "C": ("sbuf", [128, 256], "bfloat16"), "ROT": ("sbuf", [128, 1024], "float16"), "lst": ("sbuf", [128, 160], "uint16"),
+    "base": ("sbuf", [128, 64], "float32"),
+    "tr": ("sbuf", [128, 512], "float32"), "ki": ("sbuf", [128, 32], "int32"), "U": ("sbuf", [128, 128], "int32"),
+    "m": ("sbuf", [128, 128], "int32"), "t2": ("sbuf", [128, 128], "int32"), "pa16": ("sbuf", [128, 128], "uint16"),
+    "k2": ("sbuf", [128, 256], "float32"), "y16": ("sbuf", [128, 16], "uint16"), "y": ("sbuf", [128, 256], "bfloat16"),
+    "S": ("sbuf", [128, 256], "bfloat16"), "u7": ("sbuf", [128, 128], "bfloat16"), "mdq": ("sbuf", [128, 128], "float32"),
+    "Qa": ("sbuf", [128, 128], "float32"), "pr1": ("sbuf", [128, 128], "int32"), "pr2": ("sbuf", [128, 128], "int32"),
+    "pr3": ("sbuf", [128, 128], "float32"), "pr4": ("sbuf", [128, 128], "int32"), "Lc": ("sbuf", [128, 128], "bfloat16"),
+    "junk": ("sbuf", [128, 128], "bfloat16"), "ui": ("sbuf", [128, 32], "int32"), "uf": ("sbuf", [128, 48], "float32"),
+    "u16": ("sbuf", [128, 32], "uint16"), "avg": ("sbuf", [128, 256], "int32"), "lim": ("sbuf", [128, 32], "float32"),
+    "li": ("sbuf", [128, 16], "int32"),
+    "S0": ("psum", [128, 512], "float32"), "S1": ("psum", [128, 512], "float32"), "S2": ("psum", [128, 512], "float32"),
+    "KA": ("psum", [128, 512], "float32"), "KB": ("psum", [128, 512], "float32"), "P5": ("psum", [128, 512], "float32"),
+    "P6": ("psum", [128, 512], "float32"), "P7": ("psum", [128, 512], "float32"),
+}
+PSUM = ("S0", "S1", "S2", "KA", "KB", "P5", "P6", "P7")
+KINDS = ("az", "aq", "am", "ad", "ap")
+SEMAPHORES = (["pe", "dve", "act", "pool", "sent", "stored", "lx", "lq", "lp", "lz0", "lz1", "lt"]
+              + ["%s%d_%d" % (k, s, h) for k in KINDS for s in range(1, ST) for h in range(2)])
+
+
+PLANS = {}
+
+
+def V(name, a, b, step=1):
+    return (name, a, b, step)
+
+
+def W(name, a, n):
+    return (name, a, a + n, 1)
+
+
+def IND(win, off):
+    return ("*", win, off)
+
+
+def size(v):
+    if v[0] == "*":
+        return 16 * size(v[2])
+    return (v[2] - v[1] + v[3] - 1) // v[3]
+
+
+def two_bytes(v):
+    return SCRATCH[v[0]][2] in ("bfloat16", "float16", "uint16")
+
+
+def build(g, T, nxt_addr, mask, neng):
+    ops = []
+    c = CFG
+    H = c["H"]
+    BL, LH = 16 // H, 256 // H
+    R8 = 8 * BL
+
+    def ap(v):
+        if v[0] == "*":
+            return ap(v[1]).indirect(ap(v[2]))
+        if v[3] == 1:
+            return T[v[0]][:, v[1]:v[2]]
+        return T[v[0]][:, v[1]:v[2]:v[3]]
+
+    def op(q, emit, reads, writes, cost, sem=None, cnt=0):
+        rd, wr = [], []
+        for v in reads:
+            if isinstance(v, tuple):
+                rd += [v[1], v[2]] if v[0] == "*" else [v]
+        for v in writes:
+            if v[0] == "*":
+                wr.append(v[1])
+                rd.append(v[2])
+            else:
+                wr.append(v)
+        ops.append([q, emit, rd, wr, sem, cnt, cost])
+
+    def sc(x):
+        return ap(x) if isinstance(x, tuple) else x
+
+    def vcost(o, a, k):
+        if o[0] == "*":
+            return 0.05 + size(o) * c["sc"] * c["cy"]
+        if a[0] == "*":
+            return 0.05 + size(a) * c["g"] * c["cy"]
+        return c["fix"] + max(64, size(a) * k) * c["cy"]
+
+    def half(o, a):
+        return 0.5 if o[0] != "*" and a[0] != "*" and two_bytes(o) and two_bytes(a) else 1
+
+    def tt(o, a, b, alu):
+        k = 1 if a[0] in PSUM or b[0] in PSUM else 2
+        op("dve", lambda: g.vector.tensor_tensor(ap(o), ap(a), ap(b), alu), [a, b], [o], vcost(o, a, k))
+
+    def ts(o, a, s1, o1, s2=None, o2=None):
+        t = vcost(o, a, half(o, a))
+        if o2 is None:
+            op("dve", lambda: g.vector.tensor_scalar(ap(o), ap(a), sc(s1), None, o1), [a, s1], [o], t)
+        else:
+            op("dve", lambda: g.vector.tensor_scalar(ap(o), ap(a), sc(s1), sc(s2), o1, o2), [a, s1, s2], [o], t)
+
+    def cp(o, a):
+        op("dve", lambda: g.vector.tensor_copy(ap(o), ap(a)), [a], [o], vcost(o, a, half(o, a)))
+
+    def tr32(o, a):
+        op("dve", lambda: g.vector.transpose(ap(o), ap(a)), [a], [o], vcost(o, a, 1))
+
+    def ms(o, k):
+        op("dve", lambda: g.vector.memset(ap(o), k), [], [o], vcost(o, o, half(o, o)))
+
+    def act(o, a, f, bias=0.0, scale=1.0, acc=None):
+        t = 0.065 + size(a) * c["g"] * c["cy"] if a[0] == "*" else c["afix"] + max(64, size(a)) * c["cy"]
+        if acc is None:
+            op("act", lambda: g.scalar.activation(ap(o), ap(a), f, bias=sc(bias), scale=scale), [a, bias], [o], t)
+        else:
+            op("act", lambda: g.scalar.activation(ap(o), ap(a), f, bias=sc(bias), scale=scale, accum_out=ap(acc)),
+               [a, bias], [o, acc], t)
+
+    def mm(o, l, r, start, stop):
+        op("pe", lambda: g.tensor.matmul(ap(o), ap(l), ap(r), start, stop), [l, r], [o], max(64, size(r)) * c["pe"])
+
+    def iota(o, pat, base, cm, flt=False):
+        t = 0.13 + 2 * size(o) * c["cy"]
+        if flt:
+            op("pool", lambda: g.iota(ap(o), pat, base, cm, allow_small_or_imprecise_dtypes=True), [], [o], t)
+        else:
+            op("pool", lambda: g.iota(ap(o), pat, base, cm), [], [o], t)
+
+    def load(q, o, src, sem, t):
+        op(q, lambda: (g.sync if q == "sp" else g.scalar).dma_start(ap(o), src).then_inc(T.sem[sem], 16), [], [o], t, sem, 16)
+
+    nstore = [0]
+
+    def store(dst, a, t):
+        nstore[0] += 1
+        op("sp", lambda: g.sync.dma_start(dst, ap(a)).then_inc(T.sem.stored, 16), [a], [], t, "", 0)
+
+    nsent = [0]
+
+    def send(dst, srcs, sem):
+        nsent[0] += 1
+        if len(srcs) == 1:
+            op("pool", lambda: g.remote_dma(ap(dst), ap(srcs[0]), T.sem[sem], T.sem.sent, nxt_addr[1], nxt_addr[0], mask),
+               srcs, [], c["issue"], "", 0)
+        else:
+            op("pool", lambda: g.remote_dma_fused([RemoteDMATransfer(
+                dst_ids=[DstId(rid=nxt_addr[0], pnc=nxt_addr[1])], dma_engine_mask=mask, remote_sem=T.sem[sem],
+                srcs=[ap(a) for a in srcs], dsts=[ap(dst)], alu_op=1)], local_sem=T.sem.sent), srcs, [], c["issue"], "", 0)
+        op("far", None, [], [dst], c["far"] + c["row"] + 128 * size(dst) * (2 if two_bytes(dst) else 4) * len(srcs) / c["bw"], sem, neng)
+
+    def c1(j):
+        return V("col", j, j + 1)
+
+    I, NI, BO = V("I", 0, 128), V("NI", 0, 128), V("BO", 0, 128)
+    XW = V("X", 0, 4096)
+    L_BC, L_DUP, L_CP, L_CQ, L_EDUP, L_ECP = (W("lst", 0, R8 // 16), V("lst", 8, 40), V("lst", 40, 56), V("lst", 56, 72),
+                                              V("lst", 72, 104), V("lst", 104, 120))
+    NCNT, NLIM, PLIM, NTH = V("lim", 0, 1), V("lim", 8, 9), V("lim", 16, 17), V("lim", 24, 25)
+    ZW = LH + R8
+    MP = H == 1 or c["MP"]
+    L_PDUP = V("lst", 120, 152) if H == 2 and MP else L_EDUP
+
+    load("sp", V("rawq", 0, 256), T.pr[:], "lq", 2.6)
+    load("sp", V("rawp", 0, 256), T.pl[:], "lp", 3.1)
+    load("sp", XW, T.xt[:], "lx", 7.5)
+    for h in range(H):
+        load("act", W("zl", ZW * h, LH), T.z0[:, LH * h:LH * h + LH], "lz%d" % h, 3.5)
+    load("act", V("thi", 0, 1), T.th[:], "lt", 3.5)
+    iota(V("cj", 0, 8), [[1, 8]], 0, 1)
+    iota(V("ci", 0, 32), [[16, 16], [0, 2]], 0, 0)
+    iota(V("ci", 32, 48), [[1, 16]], 0, 0)
+    iota(V("ci", 48, 64), [[0, H], [H, BL]], 0, 0)
+    iota(V("ci", 96, 112), [[256, H], [0, BL]], 0, 0)
+    iota(V("ci", 112, 128), [[8, 2], [256, H], [H, BL // 2]] if MP else [[256, H], [H, BL]], 0, 0)
+    iota(V("idx", 0, 144), [[1, 144]], 0, 0, True)
+    for h in range(H):
+        iota(W("zl", ZW * h + LH, R8), [[-2, 8], [0, BL]], 1, 0, True)
+    iota(V("idx", 144, 272), [[1, 8], [0, 16]], 0, 0, True)
+    iota(V("ci", 64, 96), [[128, H], [1, BL], [0, 2]], 0, 0)
+    iota(V("ci", 160, 176), [[8 * LH, H], [16, BL]], 0, 0)
+    if L_PDUP != L_EDUP:
+        iota(V("ci", 128, 160), [[64, 2], [1, 8], [0, 2]], 0, 0)
+    ts(V("cj", 8, 9), V("cj", 0, 1), 15, ALU.bitwise_and)
+    ts(V("cj", 16, 17), V("cj", 0, 1), 16, ALU.bitwise_and)
+    ts(V("cj", 56, 57), V("cj", 0, 1), BL - 1, ALU.bitwise_and)
+    cp(c1(0), V("cj", 0, 1))
+    cp(c1(1), V("cj", 8, 9))
+    cp(c1(2), V("cj", 16, 17))
+    cp(c1(9), V("cj", 56, 57))
+    ts(L_DUP, V("ci", 0, 32), c1(1), ALU.add)
+    ts(c1(3), c1(9), 32.0, ALU.mult, c1(2), ALU.add)
+    ts(c1(10), c1(1), c1(9), ALU.subtract, 1.0 / BL, ALU.mult)
+    tt(c1(4), c1(0), c1(1), ALU.subtract)
+    ts(V("cj", 64, 80), V("ci", 48, 64), c1(10), ALU.add, 1.0, ALU.add)
+    ts(V("cj", 80, 96), V("cj", 64, 80), 15, ALU.bitwise_and)
+    tt(V("base", 32, 48), V("cj", 80, 96), V("ci", 96, 112), ALU.add)
+    ts(L_CQ, V("base", 32, 48), c1(3), ALU.add)
+    ts(L_CP, V("ci", 112, 128), c1(3), ALU.add, c1(10), ALU.add)
+    ts(V("W1", 0, 144), V("idx", 0, 144), -16.0, ALU.add, c1(4), ALU.is_equal)
+    ts(I, V("idx", 0, 128), c1(0), ALU.is_equal)
+    ts(NI, V("idx", 0, 128), c1(0), ALU.is_equal, -1.0, ALU.mult)
+    ms(W("C", 0, R8), -2.0)
+    ms(W("C", R8, R8), -18.0)
+    ts(V("W32", 0, 144), V("W1", 0, 144), -32.0, ALU.mult)
+    ts(c1(5), c1(4), 1.0 / 16, ALU.mult)
+    ts(c1(6), c1(1), 16.0, ALU.mult)
+    ts(c1(11), c1(1), float(BL), ALU.mult)
+    tt(c1(7), c1(1), c1(2), ALU.add)
+    cp(V("wa", 0, 512), IND(V("rawq", 0, 256), L_DUP))
+    tr32(V("wb", 0, 512), V("wa", 0, 512))
+    cp(V("qf", 0, 256), IND(V("wb", 0, 512), L_CQ))
+    cp(V("ql", 0, 256), V("qf", 0, 256))
+    cp(V("wc", 0, 512), IND(V("rawp", 0, 256), L_DUP))
+    tr32(V("wd", 0, 512), V("wc", 0, 512))
+    cp(V("pin", 0, 256), IND(V("wd", 0, 512), L_CP))
+    for h in range(H):
+        tt(W("tr", R8 * h, R8), W("qf", 2 * R8 * h + R8, R8), W("qf", 2 * R8 * h, R8), ALU.subtract)
+        ts(W("B", 18 * BL * h + 10 * BL, R8), W("tr", R8 * h, R8), 0.5, ALU.mult)
+        tt(W("B", 18 * BL * h + BL, R8), W("qf", 2 * R8 * h, R8), W("B", 18 * BL * h + 10 * BL, R8), ALU.add)
+    ts(L_BC, W("ci", 32, R8 // 16), 0.0, ALU.mult, c1(9), ALU.add)
+    ts(BO, V("idx", 144, 272), c1(5), ALU.is_equal)
+    ts(V("base", 0, 16), V("ci", 32, 48), 256.0, ALU.mult, c1(6), ALU.add)
+    ts(NTH, V("thi", 0, 1), -1.0, ALU.mult, -0.9375, ALU.add)
+    ms(NCNT, -2048.0)
+    ts(NLIM, V("thi", 0, 1), -1.0, ALU.mult, -0.9375, ALU.add)
+    ts(V("cj", 48, 56), V("cj", 0, 8), 7, ALU.bitwise_and)
+    ts(V("cj", 24, 25), V("cj", 0, 1), 120, ALU.bitwise_and)
+    ts(L_EDUP, V("ci", 64, 96), c1(11), ALU.add)
+    if L_PDUP != L_EDUP:
+        ts(c1(12), c1(10), 64.0, ALU.mult, c1(11), ALU.add)
+        ts(L_PDUP, V("ci", 128, 160), c1(12), ALU.add)
+    cp(c1(8), V("cj", 24, 25))
+    ts(L_ECP, V("ci", 32, 48), 32.0, ALU.mult, c1(7), ALU.add)
+    ts(V("col", 16, 24), V("cj", 48, 56), c1(8), ALU.add)
+    ts(V("base", 16, 32), V("ci", 160, 176), c1(1), ALU.add)
+    for s in range(8):
+        ts(V("ROT", 128 * s, 128 * s + 128), V("idx", 0, 128), c1(16 + s), ALU.is_equal)
+
+    banks = ["S0", "S1", "S2"]
+    nb = [0]
+    RC = 512 // LH
+    CH = 64 // BL
+
+    def groups(rows, n):
+        return [rows[j:j + n] for j in range(0, len(rows), n)]
+
+    def at(names, r):
+        return names[1] + BL * ((r & 8) + ((r + names[2]) & 7))
+
+    def plain(rows, names, g0, out, sub):
+        calls = groups(rows, RC)
+        for r in calls:
+            n = len(r) - (1 if names[2] and r[-1] % 8 == 7 and len(r) > 1 else 0)
+            act(W("G", g0 + LH * (r[0] % 8), LH * n), IND(XW, W(names[0], at(names, r[0]), BL * n)), AF.Identity)
+            if n < len(r):
+                act(W("G", g0 + LH * 7, LH), IND(XW, W(names[0], at(names, r[-1]), BL)), AF.Identity)
+        for r in calls:
+            b = banks[nb[0] % 3]
+            nb[0] += 1
+            mm(W(b, 0, LH * len(r)), I, W("G", g0 + LH * (r[0] % 8), LH * len(r)), True, False)
+            for j in range(len(r)):
+                mm(W(b, LH * j, LH), NI, sub, False, j == len(r) - 1)
+            act(W(out[0], out[1] + LH * r[0], LH * len(r)), W(b, 0, LH * len(r)), AF.Abs)
+
+    def fused(rows, names, d0, out, sub, tail):
+        for r in rows:
+            tt(W("DD", d0 + LH * r, LH), IND(XW, W(names[0], at(names, r), BL)), sub, ALU.subtract)
+        runs = []
+        for r in rows:
+            if runs and runs[-1][-1] + 1 == r and len(runs[-1]) < RC and not (tail and r >= rows[-1] - RC // 2 + 1 and r % (RC // 2) == 0
+                                                                               and rows.index(r) >= len(rows) - RC):
+                runs[-1].append(r)
+            else:
+                runs.append([r])
+        for r in runs:
+            act(W(out[0], out[1] + LH * r[0], LH * len(r)), W("DD", d0 + LH * r[0], LH * len(r)), AF.Abs)
+
+    def reduce(bank, c0, w, src, s0, n, first, last):
+        for a in range(16):
+            mm(W(bank, c0, BL * n), V(w, 16 - a, 144 - a), V(src[0], src[1] + LH * s0 + a, src[1] + LH * (s0 + n), 16),
+               first and a == 0, last and a == 15)
+
+    def left_tail(s, h):
+        n = 128 if MP else R8
+        p0 = 256 * s + 2 * n * h
+        LC, E1, E2 = W("Lc", n * h, n), W("P7", 256 + n * h, n), W("P7", 384 + n * h, n)
+        ts(LC, W(fbank(h)[0], 0, n), NLIM, ALU.add, 0.0, ALU.is_lt)
+        if s < ST - 1:
+            tt(W("PY", p0, n), LC, E1, ALU.mult)
+            tt(W("PY", p0 + n, n), LC, E2, ALU.mult)
+            send(W("pin", p0 + 256, 2 * n), [W("PX", p0, 2 * n), W("PY", p0, 2 * n)], "ap%d_%d" % (s + 1, h))
+        else:
+            tt(E1, LC, E1, ALU.mult)
+            tt(E2, LC, E2, ALU.mult)
+            if MP:
+                tt(W("pf", 0, 256), W("PX", p0, 256), W("P7", 256, 256), ALU.add)
+            else:
+                tt(W("pf", 2 * n * h, n), W("PX", p0, n), E1, ALU.add)
+                tt(W("pf", 2 * n * h + n, n), W("PX", p0 + n, n), E2, ALU.add)
+
+    def fbank(h):
+        return ("KB", 0) if H == 1 else ("P5", R8 * h) if MP else ("KB" if h else "KA", 0)
+
+    def pcol(s, h, hi):
+        return 256 * s + (128 * hi + R8 * h if MP else 2 * R8 * h + R8 * hi)
+
+    def remake(s, hs):
+        h, n = hs[0], R8 * len(hs)
+        MD, PA, E1, E2 = [W("P7", 128 * j + R8 * h, n) for j in range(4)]
+        P1, P2, P3, P4, QA = [W(k, R8 * h, n) for k in ("pr1", "pr2", "pr3", "pr4", "Qa")]
+        tt(P1, QA, PA, ALU.mult)
+        ts(P2, P1, 5, ALU.logical_shift_right)
+        tt(P3, P2, PA, ALU.add)
+        ts(P4, P3, NCNT, ALU.add, 2048.0, ALU.add)
+        for k in ([hs] if MP else [[j] for j in hs]):
+            h, n = k[0], R8 * len(k)
+            MD, PA, E1, E2 = [W("P7", 128 * j + R8 * h, n) for j in range(4)]
+            PI, REM = W("PX", pcol(s, h, 0), n), W("PX", pcol(s, h, 1), n)
+            tt(PI, W("pin", pcol(s, h, 1), n), MD, ALU.subtract)
+            ts(REM, W("pr4", R8 * h, n), 4095, ALU.bitwise_and)
+            tt(E1, PA, PI, ALU.subtract)
+            tt(E2, PI, REM, ALU.subtract)
+
+    def limits():
+        cb = "P6" if H == 1 else "P5"
+        mm(W(cb, 0 if H == 1 else 128, 64), BO, V("Lc", 0, 64), True, False)
+        mm(W(cb, 0 if H == 1 else 128, 64), BO, V("Lc", 64, 128), False, True)
+        act(V("junk", 0, 64), W(cb, 0 if H == 1 else 128, 64), AF.Identity, scale=-1.0, acc=NCNT)
+        ts(V("li", 0, 1), NCNT, 2048.0, ALU.add)
+        ts(V("li", 8, 9), V("li", 0, 1), 31, ALU.bitwise_and)
+        ts(NLIM, V("li", 8, 9), -1.0, ALU.mult, NTH, ALU.add)
+
+    def sums_d(s, h):
+        last = s == ST - 1
+        z0, q0, b0, a0 = 384 * s + ZW * h, 256 * s + 2 * R8 * h, 288 * s + 18 * BL * h, 16 * LH * h
+        Z, NT = W("zl", z0, LH), W("zl", z0 + LH, R8)
+        na = c["NA"][h]
+        if s:
+            act(W("B", b0 + R8, BL), W("B", b0, BL), AF.Identity)
+            act(W("B", b0 + 17 * BL, BL), W("B", b0 + 9 * BL, BL), AF.Identity)
+        if not last and (s == 0 or c["MIDSEP"]):
+            send(W("B", b0 + 288, R8), [W("B", b0 + BL, R8)], "am%d_%d" % (s + 1, h))
+        if H == 1:
+            act(W("P5", 0, R8), W("B", b0 + BL, R8), AF.Identity)
+        U7 = W("u7", R8 * h, R8)
+        act(U7, NT, AF.Relu, bias=-176.0, scale=-16.0)
+        QL = ("ql", q0, 1 if s else 0)
+        plain(list(range(8, 8 + na)), QL, 8 * LH * h, ("AB", a0), Z)
+        AB = ("AB", a0)
+        if H == 1:
+            fused(list(range(8 + na, 16)) + [4, 5, 6, 7, 0, 1, 2, 3], QL, a0, AB, Z, True)
+            mm(V("KA", 64, 256), I, V("C", 64, 256), True, False)
+            reduce("KA", 128, "W32", AB, 8, 4, False, False)
+            reduce("KA", 192, "W32", AB, 12, 4, False, False)
+            mm(V("KA", 64, 128), I, W("zl", z0 + LH + 64, 64), False, False)
+            mm(V("KA", 128, 256), I, NT, False, False)
+            mm(V("KA", 128, 256), I, U7, False, False)
+            reduce("KA", 64, "W32", AB, 4, 4, False, True)
+            mm(V("KB", 0, 64), I, V("C", 0, 64), True, False)
+            mm(V("KB", 0, 64), I, W("zl", z0 + LH, 64), False, False)
+            reduce("KB", 0, "W32", AB, 0, 4, False, True)
+        else:
+            fused(list(range(8 + na, 16)) + list(range(8)), QL, a0, AB, Z, False)
+            k = "KB" if h else "KA"
+            mm(V(k, 0, 128), I, V("C", 0, 128), True, False)
+            reduce(k, 64, "W32", AB, 8, 8, False, False)
+            mm(V(k, 0, 64), I, NT, False, False)
+            mm(V(k, 64, 128), I, NT, False, False)
+            mm(V(k, 64, 128), I, U7, False, False)
+            reduce(k, 0, "W32", AB, 0, 8, False, True)
+
+    def turn(s, h):
+        last = s == ST - 1
+        z0, q0, b0, p0 = 384 * s + ZW * h, 256 * s + 2 * R8 * h, 288 * s + 18 * BL * h, 256 * s + 2 * R8 * h
+        Z, NT, ZN, NTN = W("zl", z0, LH), W("zl", z0 + LH, R8), W("zs", z0, LH), W("zs", z0 + LH, R8)
+        M, U, T2 = W("m", R8 * h, R8), W("U", R8 * h, R8), W("t2", R8 * h, R8)
+        MD, PA, MM, SA = [W("P7", 128 * j + R8 * h, R8) for j in range(4)]
+        PLO, PHI = W("pin", pcol(s, h, 0), R8), W("pin", pcol(s, h, 1), R8)
+        KI = W("ki", 16 * h, BL)
+        s0, t0 = 2 * R8 * h, 256 * h
+        if last and h == 0:
+            act(PLIM, NLIM, AF.Identity, scale=-1.0)
+        sg = (PLIM, 1.0 / 32) if last else (NLIM, -1.0 / 32)
+        if not MP:
+            tt(MD, PHI, PLO, ALU.subtract)
+        elif h == 0:
+            tt(W("P7", 0, 128), W("pin", 256 * s + 128, 128), W("pin", 256 * s, 128), ALU.subtract)
+        if H == 1:
+            cp(V("tr", 0, 64), V("KA", 64, 128))
+            tt(V("tr", 64, 128), V("KA", 128, 192), V("tr", 0, 64), ALU.max)
+            tt(V("tr", 128, 192), V("KA", 192, 256), V("tr", 64, 128), ALU.max)
+            act(V("S", 64, 256), V("KA", 64, 256), AF.Sign, bias=sg[0], scale=sg[1])
+            tt(V("tr", 192, 256), V("KB", 0, 64), V("tr", 128, 192), ALU.max)
+            act(V("S", 0, 64), V("KB", 0, 64), AF.Sign, bias=sg[0], scale=sg[1])
+            tt(V("tr", 0, 32), V("tr", 192, 224), V("tr", 224, 256), ALU.max)
+            tt(KI, V("tr", 0, 16), V("tr", 16, 32), ALU.max)
+            kz = "KA"
+        else:
+            kz = "KB" if h else "KA"
+            if c["CPA"]:
+                act(W("tr", t0, 64), V(kz, 64, 128), AF.Identity)
+            else:
+                cp(W("tr", t0, 64), V(kz, 64, 128))
+            tt(W("tr", t0 + 64, 64), V(kz, 0, 64), W("tr", t0, 64), ALU.max)
+            act(W("S", s0, 128), V(kz, 0, 128), AF.Sign, bias=sg[0], scale=sg[1])
+            tt(W("tr", t0 + 128, 32), W("tr", t0 + 64, 32), W("tr", t0 + 96, 32), ALU.max)
+            tt(W("tr", t0 + 160, 16), W("tr", t0 + 128, 16), W("tr", t0 + 144, 16), ALU.max)
+            tt(KI, W("tr", t0 + 160, 8), W("tr", t0 + 168, 8), ALU.max)
+            act(W(kz, 384, R8), W("B", b0 + BL, R8), AF.Identity)
+        MID, DS = (W("P5", 0, R8), W("P5", 256, R8)) if H == 1 else (W(kz, 384, R8), W(kz, 128, R8))
+        mm(DS, I, W("S", s0 + R8, R8), True, False)
+        mm(DS, NI, W("S", s0, R8), False, True)
+        tt(U, IND(KI, L_BC), NT, ALU.subtract)
+        ts(M, U, 4, ALU.arith_shift_right, 1, ALU.bitwise_and)
+        ts(T2, U, 14, ALU.bitwise_and)
+        tt(MD, M, MD, ALU.mult)
+        ts(NTN, T2, -1.0, ALU.mult, 1.0, ALU.add)
+        tt(PA, PLO, MD, ALU.add)
+        ts(MM, M, 2.0, ALU.mult, -1.0, ALU.add)
+        cp(W("pa16", R8 * h, R8), PA)
+        DH, MDQ, QA = W("B", b0 + 10 * BL, R8), W("mdq", R8 * h, R8), W("Qa", R8 * h, R8)
+        tt(MDQ, DH, MM, ALU.mult)
+        tt(SA, M, DS, ALU.mult)
+        tt(SA, W("S", s0, R8), SA, ALU.add)
+        tt(SA, NTN, SA, ALU.max)
+        tt(DH, MDQ, SA, ALU.mult)
+        QF = 2 * R8 * h
+        if not last:
+            tt(W("qf", QF, R8), MID, DH, ALU.subtract)
+            tt(W("qf", QF + R8, R8), MID, DH, ALU.add)
+            cp(W("qs", q0, 2 * R8), W("qf", QF, 2 * R8))
+            send(W("ql", q0 + 256, 2 * R8), [W("qs", q0, 2 * R8)], "aq%d_%d" % (s + 1, h))
+        else:
+            tt(W("qf", QF, R8), MID, DH, ALU.add)
+            tt(W("qf", QF + R8, R8), MID, DH, ALU.subtract)
+        tt(QA, MDQ, MID, ALU.add)
+        k0 = 2 * R8 * h
+        tt(W("k2", k0, R8), NTN, PA, ALU.mult)
+        tt(W("k2", k0 + R8, R8 // 2), W("k2", k0, R8 // 2), W("k2", k0 + R8 // 2, R8 // 2), ALU.max)
+        tt(W("k2", k0, R8 // 4), W("k2", k0 + R8, R8 // 4), W("k2", k0 + R8 + R8 // 4, R8 // 4), ALU.max)
+        tt(W("k2", k0 + R8, BL), W("k2", k0, BL), W("k2", k0 + BL, BL), ALU.max)
+        cp(W("y16", BL * h, BL), W("k2", k0 + R8, BL))
+        Y = W("y", LH * h, LH)
+        cp(Y, IND(XW, W("y16", BL * h, BL)))
+        mm(W(kz, 256, LH), I, Y, True, False)
+        mm(W(kz, 256, LH), NI, Z, False, True)
+        act(ZN, W(kz, 256, LH), AF.Abs)
+        if not last:
+            send(W("zl", z0 + 384, ZW), [W("zs", z0, ZW)], "az%d_%d" % (s + 1, h))
+            if s == 0 or c["MIDSEP"]:
+                send(W("B", b0 + 288 + 9 * BL, R8), [W("B", b0 + 10 * BL, R8)], "ad%d_%d" % (s + 1, h))
+            elif not c["BM"]:
+                send(W("B", b0 + 288, 17 * BL), [W("B", b0 + BL, 17 * BL)], "ad%d_%d" % (s + 1, h))
+            elif h == H - 1:
+                send(W("B", 288 * s + 288, 288 - BL), [W("B", 288 * s + BL, 288 - BL)], "ad%d_%d" % (s + 1, h))
+        else:
+            store(T.yz[:, LH * h:LH * h + LH], ZN, 2.5)
+        mm(W("P6", 256 + LH * h, LH), I, Y, True, False)
+        mm(W("P6", 256 + LH * h, LH), I, Z, False, True)
+        if h == H - 1:
+            for a in range(16):
+                mm(W("P6", 128, 16), V("W1", 16 - a, 144 - a), V("y", a, 256, 16), a == 0, a == 15)
+            cp(W("ui", 0, 16), W("P6", 128, 16))
+            ts(W("avg", 0, 256), W("P6", 256, 256), 0.5, ALU.mult, -0.25, ALU.add)
+            ts(V("ui", 16, 32), V("ui", 0, 16), 15, ALU.bitwise_and)
+            tt(V("uf", 0, 16), V("ui", 16, 32), V("base", 0, 16), ALU.add)
+            cp(V("u16", 0, 16), V("uf", 0, 16))
+            remake(s, list(range(H)))
+        if last:
+            ts(W("uf", 16 + BL * h, BL), W("t2", R8 * h, BL), LH / 2.0, ALU.mult)
+
+    def sums_f(s, h):
+        xf = c["XFL" if s == ST - 1 else "XF"][h]
+        Y, AFB, PL = W("y", LH * h, LH), ("AF", 8 * LH * h), ("pa16", R8 * h, 0)
+        plain(list(range(8 - xf)), PL, 2048 + 8 * LH * h, AFB, Y)
+        if xf:
+            fused(list(range(8 - xf, 8)), PL, 16 * LH * h, AFB, Y, False)
+        for r in groups(list(range(8)), CH):
+            reduce(fbank(h)[0], fbank(h)[1] + BL * r[0], "W1", AFB, r[0], len(r), True, True)
+
+    for s in range(ST):
+        for h in range(H):
+            sums_d(s, h)
+        for h in range(H):
+            turn(s, h)
+            sums_f(s, h)
+        cp(IND(XW, V("u16", 0, 16)), V("avg", 0, 256))
+        if s == ST - 1:
+            store(T.yx[:], XW, 6.5)
+            break
+        for h in range(1 if MP else H):
+            left_tail(s, h)
+        limits()
+
+    def finish(src, lst, w1, w2, o, four, h, dup_v, evac_v):
+        d = IND(V(src, 0, 256), W("lst", lst[1] + 2 * BL * h, 2 * BL))
+        if dup_v:
+            cp(W(w1, 2 * LH * h, 2 * LH), d)
+        else:
+            act(W(w1, 2 * LH * h, 2 * LH), d, AF.Identity)
+        tr32(W(w2, 2 * LH * h, 2 * LH), W(w1, 2 * LH * h, 2 * LH))
+        ts(W("h16", o + LH * h, LH), IND(W(w2, 2 * LH * h, 2 * LH), W("lst", L_ECP[1], BL)), -2048.0, ALU.add)
+        for j, b in enumerate(four):
+            for s in range(RC * j, RC * j + RC):
+                mm(W(b, LH * (s % RC), LH), W("ROT", 128 * s, 128), W("h16", o + LH * h, LH), True, True)
+            if evac_v[j]:
+                cp(W("var", 8 * o + 8 * LH * h + 512 * j, 512), V(b, 0, 512))
+            else:
+                act(W("var", 8 * o + 8 * LH * h + 512 * j, 512), V(b, 0, 512), AF.Identity)
+
+    tt(V("uf", 32, 48), V("uf", 16, 32), V("base", 16, 32), ALU.add)
+    cp(V("u16", 16, 32), V("uf", 32, 48))
+    fin = c["FIN"]
+    for h in range(H):
+        finish("qf", L_EDUP, "wa", "wb", 0, ["S0", "S1", "S2", "P6"][2 * h:2 * h + 4 // H], h, fin[0], [0] * 4)
+    act(V("fin", 0, 256), IND(V("var", 0, 2048), V("u16", 16, 32)), AF.Identity, bias=2048.0)
+    store(T.yr[:], V("fin", 0, 256), 2.7)
+    for h in range(1 if MP else H):
+        left_tail(ST - 1, h)
+    for h in range(H):
+        finish("pf", L_PDUP, "wc", "wd", 256, ["KA", "P5", "KB", "S0"][2 * h:2 * h + 4 // H], h, fin[1 + h], [1, 0, 1, 0] if h == H - 1 else fin[3:5])
+    for h in range(H):
+        o, v = W("fin", 256 + LH * h, LH), IND(W("var", 2048, 8 * LH * (h + 1)), W("u16", 16 + BL * h, BL))
+        if h == H - 1:
+            ts(o, v, 2048.0, ALU.add)
+        else:
+            act(o, v, AF.Identity, bias=2048.0)
+    store(T.yp[:], V("fin", 256, 512), 2.7)
+    return ops, nstore[0], nsent[0]
+
+
+def conflicts(ops):
+    hist, out = {}, []
+    for n, o in enumerate(ops):
+        q, deps = o[0], set()
+        if q == "far":
+            deps.add(n - 1)
+        else:
+            for acc, is_w in [(v, False) for v in o[2]] + [(v, True) for v in o[3]]:
+                for (k, a, b, w) in hist.get(acc[0], []):
+                    if acc[0] in PSUM and (ops[k][0] != q or q == "pe"):
+                        deps.add(k)
+                    elif (w or is_w) and a < acc[2] and acc[1] < b and ops[k][4] != "":
+                        deps.add(k)
+        out.append(deps)
+        for v in o[3]:
+            keep = [e for e in hist.get(v[0], []) if not (v[3] == 1 and v[1] <= e[1] and e[2] <= v[2])]
+            hist[v[0]] = keep
+        for v in o[2]:
+            hist.setdefault(v[0], []).append((n, v[1], v[2], False))
+        for v in o[3]:
+            hist.setdefault(v[0], []).append((n, v[1], v[2], True))
+    return out
+
+
+def figures(g, T):
+    out, keep = [], dict(CFG)
+    for m in keep["models"]:
+        CFG.update(m)
+        out.append(([o[6] for o in build(g, T, (0, 0), 0, 0)[0]], CFG["far"], CFG["wake"] - keep["wake"]))
+        CFG.update(keep)
+    return out
+
+
+def plan(ops, deps, others):
+    c = CFG
+    n = len(ops)
+    kids = [[] for _ in ops]
+    for j in range(n):
+        for k in deps[j]:
+            kids[k].append(j)
+
+    def gap(k, j):
+        if ops[k][0] == "pe":
+            return 0.0 if ops[j][0] == "pe" else c["wake"] + 0.1
+        return 0.0 if ops[j][0] == "far" else c["wake"]
+    dur = [o[6] for o in ops]
+    hold = [0.05 if o[4] is not None and o[0] in ("sp", "act") else o[6] - c["far"] if o[0] == "far" else o[6] for o in ops]
+    pre = [[(k, gap(k, j)) for k in deps[j]] for j in range(n)]
+    post = [[(k, gap(j, k)) for k in kids[j]] for j in range(n)]
+
+    def place(seq, back):
+        busy, start = {}, [0.0] * n
+        for j in seq:
+            if back:
+                t = max([start[k] + hold[k] + d for k, d in post[j]] + [0.0]) + dur[j] - hold[j]
+            else:
+                t = max([start[k] + dur[k] + d for k, d in pre[j]] + [0.0])
+            if hold[j]:
+                l = busy.setdefault(ops[j][0], [])
+                i = len(l)
+                while i > 0 and l[i - 1][1] > t + 1e-9:
+                    i -= 1
+                while i < len(l) and l[i][0] < t + hold[j] - 1e-9:
+                    t = max(t, l[i][1])
+                    i += 1
+                l.insert(i, (t, t + hold[j]))
+            start[j] = t
+        return start
+    prio = [0.0] * n
+    for j in range(n - 1, -1, -1):
+        prio[j] = dur[j] + max([prio[k] + d for k, d in post[j]] + [0.0])
+    start = place(sorted(range(n), key=lambda j: (-prio[j], j)), False)
+    best = (max(start[j] + dur[j] for j in range(n)), start)
+    for _ in range(c["rounds"]):
+        late = place(sorted(range(n), key=lambda j: (-start[j] - dur[j], -j)), True)
+        start = place(sorted(range(n), key=lambda j: (-late[j] - hold[j], j)), False)
+        span = max(start[j] + dur[j] for j in range(n))
+        if span < best[0]:
+            best = (span, start)
+
+    def spans(start):
+        seq = sorted(range(n), key=lambda j: (start[j], j))
+        out = []
+        for d, far, wake in others:
+            free, end = {}, [0.0] * n
+            for j in seq:
+                q = ops[j][0]
+                t = free.get(q, 0.0)
+                for k, x in pre[j]:
+                    x = end[k] + (x + wake if x else 0.0)
+                    if x > t:
+                        t = x
+                end[j] = t + d[j]
+                free[q] = t + (d[j] - far if q == "far" else d[j] if hold[j] == dur[j] else hold[j])
+            out.append(max(end))
+        return out
+    base = spans(best[1])
+    best = (float(len(base)), best[1])
+    x = np.arange(n, dtype=np.int64) * 7919 + c["seed"]
+    for it in range(c["search"]):
+        x = (x * 1103515245 + 12345) % 2147483648
+        mid = (int(x[0]) % 1000) * best[1][-1] / 1000
+        amp = c["jit"] * (0.2 + (int(x[1]) % 100) / 100)
+        key = [s + (amp * float(r) if abs(s - mid) < c["win"] else 0.5 * amp) for s, r in zip(best[1], (x >> 8) / 8388608.0)]
+        for j in range(n):
+            for k, _ in pre[j]:
+                if key[k] >= key[j]:
+                    key[j] = key[k] + 1e-6
+        start = place(sorted(range(n), key=lambda j: (key[j], j)), False)
+        now = spans(start)
+        score = sum(a / b for a, b in zip(now, base))
+        if score <= best[0]:
+            best = (score, start)
+    c["span"] = [round(v, 1) for v in base + spans(best[1])]
+    loads = [j for j in range(n) if ops[j][4] and ops[j][0] != "far"]
+    return loads + sorted(set(range(n)) - set(loads), key=lambda j: (best[1][j], j))
+
+
+def emit(g, T, ops, deps, order, nstore, nsent, neng):
+    queues = {"pe": g.tensor, "dve": g.vector, "act": g.scalar, "pool": g, "sp": g.sync}
+    known = {q: {} for q in queues}
+    pos = {q: 0 for q in queues}
+    rank = {j: i for i, j in enumerate(order)}
+    clock, waits, sig, needed = {}, {}, {}, set()
+    for n in order:
+        q, sem = ops[n][0], ops[n][4]
+        if sem:
+            sig[n] = (sem, 1)
+        elif sem is None:
+            pos[q] += 1
+            sig[n] = (q, pos[q])
+        else:
+            sig[n] = None
+        mine, ck = [], {}
+        if q != "far":
+            kn = known[q]
+            for k in sorted(deps[n], key=lambda k: -rank[k]):
+                if q == "pe" and ops[k][0] == "pe":
+                    continue
+                s, p = sig[k]
+                if kn.get(s, 0) >= p:
+                    continue
+                mine.append(k)
+                needed.add(k)
+                for s2, p2 in clock[k].items():
+                    if kn.get(s2, 0) < p2:
+                        kn[s2] = p2
+            ck = dict(kn)
+        if sig[n] is not None:
+            ck[sig[n][0]] = max(ck.get(sig[n][0], 0), sig[n][1])
+        clock[n], waits[n] = ck, mine
+    count = {q: 0 for q in queues}
+    value = {}
+    for n in order:
+        o = ops[n]
+        if o[4] is None and n in needed:
+            count[o[0]] += 1
+            value[n] = count[o[0]]
+        elif o[4]:
+            value[n] = o[5]
+    for n in order:
+        o = ops[n]
+        if o[0] == "far":
+            continue
+        for k in waits[n]:
+            queues[o[0]].wait_ge(T.sem[sig[k][0]], value[k])
+        ins = o[1]()
+        if o[4] is None and n in needed:
+            ins.then_inc(T.sem[o[0]], 1)
+    g.sync.wait_ge(T.sem.stored, 16 * nstore)
+    g.wait_ge(T.sem.sent, neng * nsent)
+
+
+def rank_program(g, core, T, topo):
+    rank = T.rank_of(core)
+    if rank is None:
+        return
+    nxt = T.cores[(rank + 1) % len(T.cores)]
+    neng = len(topo.engines(core, nxt))
+    ops, nstore, nsent = build(g, T, topo.addr(nxt), topo.mask(core, nxt), neng)
+    key = repr(sorted((k, v) for k, v in CFG.items() if k != "span"))
+    if key not in PLANS:
+        deps = conflicts(ops)
+        PLANS[key] = (deps, plan(ops, deps, figures(g, T)))
+    emit(g, T, ops, PLANS[key][0], PLANS[key][1], nstore, nsent, neng)

@@ -1,21 +1,21 @@
 import numpy as np
 from concourse.bass import DstId, RemoteDMATransfer
-from concourse.mybir import AluOpType as ALU, ActivationFunctionType as AF
+from concourse.mybir import AluOpType as ALU, ActivationFunctionType as AF, AxisListType
 
 ST = 6
 CFG = {
     "H": 2,
-    "NA": (6, 6),
-    "XF": (0, 0),
-    "XFL": (0, 0),
+    "NA": (7, 4),
+    "XF": (0, 3),
+    "XFL": (0, 2),
     "MIDSEP": 0,
     "MP": 0,
     "CPA": 0,
-    "g": 1.56, "sc": 3.8, "cy": 0.001, "pe": 0.0005, "wake": 0.07, "fix": 0.005, "afix": 0.06, "far": 2.3, "issue": 0.5,
-    "bw": 80e3, "row": 0.5, "rounds": 8, "BM": 1, "FIN": (0, 1, 1, 0, 0),
-    "seed": 0, "jit": 1.5, "win": 2.0, "search": 1500,
-    "models": ({}, {"far": 3.5, "issue": 0.8, "wake": 0.12, "bw": 100e3}, {"fix": 0.03, "afix": 0.1, "g": 1.2, "sc": 2.5},
-               {"g": 1.95, "sc": 5.0, "cy": 0.0011}),
+    "g": 1.56, "sc": 3.8, "cy": 0.001, "pe": 0.0005, "wake": 0.14, "fix": 0.005, "afix": 0.1, "far": 2.8, "issue": 0.5,
+    "bw": 90e3, "row": 0.5, "rounds": 3, "BM": 1, "FIN": (0, 1, 1, 0, 0),
+    "seed": 0, "jit": 1.0, "win": 2.0, "search": 1200, "XPE": 0, "XV": 0, "SOFT": 0, "SV": 1, "GC": 4, "AC": 4,
+    "models": ({"far": 2.3}, {"wake": 0.19, "cy": 0.00083, "afix": 0.065, "far": 2.3},
+               {"wake": 0.2, "cy": 0.0012, "g": 1.8, "far": 3.0}, {"wake": 0.1, "afix": 0.18, "far": 2.3}),
 }
 
 SCRATCH = {
@@ -34,7 +34,7 @@ SCRATCH = {
     "idx": ("sbuf", [128, 272], "bfloat16"), "I": ("sbuf", [128, 128], "bfloat16"), "NI": ("sbuf", [128, 128], "bfloat16"),
     "W1": ("sbuf", [128, 144], "bfloat16"), "W32": ("sbuf", [128, 144], "bfloat16"), "BO": ("sbuf", [128, 128], "bfloat16"),
     "C": ("sbuf", [128, 256], "bfloat16"), "ROT": ("sbuf", [128, 1024], "float16"), "lst": ("sbuf", [128, 160], "uint16"),
-    "base": ("sbuf", [128, 64], "float32"),
+    "base": ("sbuf", [128, 64], "float32"), "ZR": ("sbuf", [128, 128], "bfloat16"),
     "tr": ("sbuf", [128, 512], "float32"), "ki": ("sbuf", [128, 32], "int32"), "U": ("sbuf", [128, 128], "int32"),
     "m": ("sbuf", [128, 128], "int32"), "t2": ("sbuf", [128, 128], "int32"), "pa16": ("sbuf", [128, 128], "uint16"),
     "k2": ("sbuf", [128, 256], "float32"), "y16": ("sbuf", [128, 16], "uint16"), "y": ("sbuf", [128, 256], "bfloat16"),
@@ -44,11 +44,11 @@ SCRATCH = {
     "junk": ("sbuf", [128, 128], "bfloat16"), "ui": ("sbuf", [128, 32], "int32"), "uf": ("sbuf", [128, 48], "float32"),
     "u16": ("sbuf", [128, 32], "uint16"), "avg": ("sbuf", [128, 256], "int32"), "lim": ("sbuf", [128, 32], "float32"),
     "li": ("sbuf", [128, 16], "int32"),
-    "S0": ("psum", [128, 512], "float32"), "S1": ("psum", [128, 512], "float32"), "S2": ("psum", [128, 512], "float32"),
-    "KA": ("psum", [128, 512], "float32"), "KB": ("psum", [128, 512], "float32"), "P5": ("psum", [128, 512], "float32"),
+    "S0": ("psum", [128, 1024], "float32"), "S1": ("psum", [128, 1024], "float32"),
+    "KA": ("psum", [128, 512], "float32"), "KB": ("psum", [128, 512], "float32"),
     "P6": ("psum", [128, 512], "float32"), "P7": ("psum", [128, 512], "float32"),
 }
-PSUM = ("S0", "S1", "S2", "KA", "KB", "P5", "P6", "P7")
+PSUM = ("S0", "S1", "KA", "KB", "P6", "P7")
 KINDS = ("az", "aq", "am", "ad", "ap")
 SEMAPHORES = (["pe", "dve", "act", "pool", "sent", "stored", "lx", "lq", "lp", "lz0", "lz1", "lt"]
               + ["%s%d_%d" % (k, s, h) for k in KINDS for s in range(1, ST) for h in range(2)])
@@ -230,6 +230,9 @@ def build(g, T, nxt_addr, mask, neng):
     ts(V("W1", 0, 144), V("idx", 0, 144), -16.0, ALU.add, c1(4), ALU.is_equal)
     ts(I, V("idx", 0, 128), c1(0), ALU.is_equal)
     ts(NI, V("idx", 0, 128), c1(0), ALU.is_equal, -1.0, ALU.mult)
+    if c["XPE"]:
+        ms(V("ZR", 0, 128), 0.0)
+    ms(W("C", 128, 64), 1.0)
     ms(W("C", 0, R8), -2.0)
     ms(W("C", R8, R8), -18.0)
     ts(V("W32", 0, 144), V("W1", 0, 144), -32.0, ALU.mult)
@@ -241,13 +244,13 @@ def build(g, T, nxt_addr, mask, neng):
     tr32(V("wb", 0, 512), V("wa", 0, 512))
     cp(V("qf", 0, 256), IND(V("wb", 0, 512), L_CQ))
     cp(V("ql", 0, 256), V("qf", 0, 256))
-    cp(V("wc", 0, 512), IND(V("rawp", 0, 256), L_DUP))
-    tr32(V("wd", 0, 512), V("wc", 0, 512))
-    cp(V("pin", 0, 256), IND(V("wd", 0, 512), L_CP))
     for h in range(H):
         tt(W("tr", R8 * h, R8), W("qf", 2 * R8 * h + R8, R8), W("qf", 2 * R8 * h, R8), ALU.subtract)
         ts(W("B", 18 * BL * h + 10 * BL, R8), W("tr", R8 * h, R8), 0.5, ALU.mult)
         tt(W("B", 18 * BL * h + BL, R8), W("qf", 2 * R8 * h, R8), W("B", 18 * BL * h + 10 * BL, R8), ALU.add)
+    cp(V("wc", 0, 512), IND(V("rawp", 0, 256), L_DUP))
+    tr32(V("wd", 0, 512), V("wc", 0, 512))
+    cp(V("pin", 0, 256), IND(V("wd", 0, 512), L_CP))
     ts(L_BC, W("ci", 32, R8 // 16), 0.0, ALU.mult, c1(9), ALU.add)
     ts(BO, V("idx", 144, 272), c1(5), ALU.is_equal)
     ts(V("base", 0, 16), V("ci", 32, 48), 256.0, ALU.mult, c1(6), ALU.add)
@@ -267,7 +270,7 @@ def build(g, T, nxt_addr, mask, neng):
     for s in range(8):
         ts(V("ROT", 128 * s, 128 * s + 128), V("idx", 0, 128), c1(16 + s), ALU.is_equal)
 
-    banks = ["S0", "S1", "S2"]
+    banks = ["S0", "S1"]
     nb = [0]
     RC = 512 // LH
     CH = 64 // BL
@@ -279,27 +282,26 @@ def build(g, T, nxt_addr, mask, neng):
         return names[1] + BL * ((r & 8) + ((r + names[2]) & 7))
 
     def plain(rows, names, g0, out, sub):
-        calls = groups(rows, RC)
-        for r in calls:
+        for r in groups(rows, c["GC"]):
             n = len(r) - (1 if names[2] and r[-1] % 8 == 7 and len(r) > 1 else 0)
             act(W("G", g0 + LH * (r[0] % 8), LH * n), IND(XW, W(names[0], at(names, r[0]), BL * n)), AF.Identity)
             if n < len(r):
                 act(W("G", g0 + LH * 7, LH), IND(XW, W(names[0], at(names, r[-1]), BL)), AF.Identity)
-        for r in calls:
-            b = banks[nb[0] % 3]
+        for r2 in groups(rows, 2 * RC):
+            b = banks[nb[0] % 2]
             nb[0] += 1
-            mm(W(b, 0, LH * len(r)), I, W("G", g0 + LH * (r[0] % 8), LH * len(r)), True, False)
-            for j in range(len(r)):
-                mm(W(b, LH * j, LH), NI, sub, False, j == len(r) - 1)
-            act(W(out[0], out[1] + LH * r[0], LH * len(r)), W(b, 0, LH * len(r)), AF.Abs)
+            for i, r in enumerate(groups(r2, RC)):
+                mm(W(b, 512 * i, LH * len(r)), I, W("G", g0 + LH * (r[0] % 8), LH * len(r)), True, False)
+                for j in range(len(r)):
+                    mm(W(b, 512 * i + LH * j, LH), NI, sub, False, j == len(r) - 1)
+            act(W(out[0], out[1] + LH * r2[0], LH * len(r2)), W(b, 0, LH * len(r2)), AF.Abs)
 
     def fused(rows, names, d0, out, sub, tail):
         for r in rows:
             tt(W("DD", d0 + LH * r, LH), IND(XW, W(names[0], at(names, r), BL)), sub, ALU.subtract)
         runs = []
         for r in rows:
-            if runs and runs[-1][-1] + 1 == r and len(runs[-1]) < RC and not (tail and r >= rows[-1] - RC // 2 + 1 and r % (RC // 2) == 0
-                                                                               and rows.index(r) >= len(rows) - RC):
+            if runs and runs[-1][-1] + 1 == r and len(runs[-1]) < c["AC"]:
                 runs[-1].append(r)
             else:
                 runs.append([r])
@@ -310,6 +312,8 @@ def build(g, T, nxt_addr, mask, neng):
         for a in range(16):
             mm(W(bank, c0, BL * n), V(w, 16 - a, 144 - a), V(src[0], src[1] + LH * s0 + a, src[1] + LH * (s0 + n), 16),
                first and a == 0, last and a == 15)
+            if a < c["XPE"]:
+                mm(W(bank, c0, BL * n), V("ZR", 0, 128), V(src[0], src[1] + LH * s0 + a, src[1] + LH * (s0 + n), 16), False, False)
 
     def left_tail(s, h):
         n = 128 if MP else R8
@@ -353,10 +357,11 @@ def build(g, T, nxt_addr, mask, neng):
             tt(E2, PI, REM, ALU.subtract)
 
     def limits():
-        cb = "P6" if H == 1 else "P5"
-        mm(W(cb, 0 if H == 1 else 128, 64), BO, V("Lc", 0, 64), True, False)
-        mm(W(cb, 0 if H == 1 else 128, 64), BO, V("Lc", 64, 128), False, True)
-        act(V("junk", 0, 64), W(cb, 0 if H == 1 else 128, 64), AF.Identity, scale=-1.0, acc=NCNT)
+        cnt = W("P6", 0, 64)
+        mm(cnt, BO, V("Lc", 0, 64), True, False)
+        mm(cnt, BO, V("Lc", 64, 128), False, True)
+        op("dve", lambda: g.vector.tensor_reduce(ap(NCNT), ap(cnt), AxisListType.X, ALU.add, negate=True), [cnt], [NCNT],
+           vcost(NCNT, cnt, 1))
         ts(V("li", 0, 1), NCNT, 2048.0, ALU.add)
         ts(V("li", 8, 9), V("li", 0, 1), 31, ALU.bitwise_and)
         ts(NLIM, V("li", 8, 9), -1.0, ALU.mult, NTH, ALU.add)
@@ -367,14 +372,12 @@ def build(g, T, nxt_addr, mask, neng):
         Z, NT = W("zl", z0, LH), W("zl", z0 + LH, R8)
         na = c["NA"][h]
         if s:
-            act(W("B", b0 + R8, BL), W("B", b0, BL), AF.Identity)
-            act(W("B", b0 + 17 * BL, BL), W("B", b0 + 9 * BL, BL), AF.Identity)
-        if not last and (s == 0 or c["MIDSEP"]):
+            cp(W("B", b0 + R8, BL), W("B", b0, BL))
+            cp(W("B", b0 + 17 * BL, BL), W("B", b0 + 9 * BL, BL))
+        elif not last:
             send(W("B", b0 + 288, R8), [W("B", b0 + BL, R8)], "am%d_%d" % (s + 1, h))
-        if H == 1:
-            act(W("P5", 0, R8), W("B", b0 + BL, R8), AF.Identity)
         U7 = W("u7", R8 * h, R8)
-        act(U7, NT, AF.Relu, bias=-176.0, scale=-16.0)
+        ts(U7, NT, -13.0, ALU.is_equal, 32.0, ALU.mult)
         QL = ("ql", q0, 1 if s else 0)
         plain(list(range(8, 8 + na)), QL, 8 * LH * h, ("AB", a0), Z)
         AB = ("AB", a0)
@@ -409,8 +412,8 @@ def build(g, T, nxt_addr, mask, neng):
         PLO, PHI = W("pin", pcol(s, h, 0), R8), W("pin", pcol(s, h, 1), R8)
         KI = W("ki", 16 * h, BL)
         s0, t0 = 2 * R8 * h, 256 * h
-        if last and h == 0:
-            act(PLIM, NLIM, AF.Identity, scale=-1.0)
+        if h == 0 and (last or c["SV"]):
+            ts(PLIM, NLIM, 32.0 if c["SV"] else -1.0, ALU.mult)
         sg = (PLIM, 1.0 / 32) if last else (NLIM, -1.0 / 32)
         if not MP:
             tt(MD, PHI, PLO, ALU.subtract)
@@ -433,14 +436,20 @@ def build(g, T, nxt_addr, mask, neng):
             else:
                 cp(W("tr", t0, 64), V(kz, 64, 128))
             tt(W("tr", t0 + 64, 64), V(kz, 0, 64), W("tr", t0, 64), ALU.max)
-            act(W("S", s0, 128), V(kz, 0, 128), AF.Sign, bias=sg[0], scale=sg[1])
+            if c["SV"]:
+                ts(W("S", s0, 128), V(kz, 0, 128), PLIM, ALU.is_gt if last else ALU.is_lt, 2.0, ALU.mult)
+            else:
+                act(W("S", s0, 128), V(kz, 0, 128), AF.Sign, bias=sg[0], scale=sg[1])
             tt(W("tr", t0 + 128, 32), W("tr", t0 + 64, 32), W("tr", t0 + 96, 32), ALU.max)
             tt(W("tr", t0 + 160, 16), W("tr", t0 + 128, 16), W("tr", t0 + 144, 16), ALU.max)
             tt(KI, W("tr", t0 + 160, 8), W("tr", t0 + 168, 8), ALU.max)
-            act(W(kz, 384, R8), W("B", b0 + BL, R8), AF.Identity)
-        MID, DS = (W("P5", 0, R8), W("P5", 256, R8)) if H == 1 else (W(kz, 384, R8), W(kz, 128, R8))
+            cp(W(kz, 384, R8), W("B", b0 + BL, R8))
+        MID, DS, SL = W(kz, 384, R8), W(kz, 128, R8), W(kz, 192, R8)
         mm(DS, I, W("S", s0 + R8, R8), True, False)
         mm(DS, NI, W("S", s0, R8), False, True)
+        if c["SV"]:
+            mm(SL, I, W("S", s0, R8), True, False)
+            mm(SL, NI, W("C", 128, R8), False, True)
         tt(U, IND(KI, L_BC), NT, ALU.subtract)
         ts(M, U, 4, ALU.arith_shift_right, 1, ALU.bitwise_and)
         ts(T2, U, 14, ALU.bitwise_and)
@@ -449,10 +458,16 @@ def build(g, T, nxt_addr, mask, neng):
         tt(PA, PLO, MD, ALU.add)
         ts(MM, M, 2.0, ALU.mult, -1.0, ALU.add)
         cp(W("pa16", R8 * h, R8), PA)
+        for j in range(c["XV"]):
+            ts(W("ZR", 8 * j, 8), W("zl", z0, 8), 1.0, ALU.mult)
         DH, MDQ, QA = W("B", b0 + 10 * BL, R8), W("mdq", R8 * h, R8), W("Qa", R8 * h, R8)
         tt(MDQ, DH, MM, ALU.mult)
-        tt(SA, M, DS, ALU.mult)
-        tt(SA, W("S", s0, R8), SA, ALU.add)
+        if c["SV"]:
+            tt(W("pr3", R8 * h, R8), M, DS, ALU.mult)
+            tt(SA, W("pr3", R8 * h, R8), SL, ALU.add)
+        else:
+            tt(SA, M, DS, ALU.mult)
+            tt(SA, W("S", s0, R8), SA, ALU.add)
         tt(SA, NTN, SA, ALU.max)
         tt(DH, MDQ, SA, ALU.mult)
         QF = 2 * R8 * h
@@ -478,10 +493,8 @@ def build(g, T, nxt_addr, mask, neng):
         act(ZN, W(kz, 256, LH), AF.Abs)
         if not last:
             send(W("zl", z0 + 384, ZW), [W("zs", z0, ZW)], "az%d_%d" % (s + 1, h))
-            if s == 0 or c["MIDSEP"]:
+            if s == 0:
                 send(W("B", b0 + 288 + 9 * BL, R8), [W("B", b0 + 10 * BL, R8)], "ad%d_%d" % (s + 1, h))
-            elif not c["BM"]:
-                send(W("B", b0 + 288, 17 * BL), [W("B", b0 + BL, 17 * BL)], "ad%d_%d" % (s + 1, h))
             elif h == H - 1:
                 send(W("B", 288 * s + 288, 288 - BL), [W("B", 288 * s + BL, 288 - BL)], "ad%d_%d" % (s + 1, h))
         else:
@@ -531,25 +544,27 @@ def build(g, T, nxt_addr, mask, neng):
             act(W(w1, 2 * LH * h, 2 * LH), d, AF.Identity)
         tr32(W(w2, 2 * LH * h, 2 * LH), W(w1, 2 * LH * h, 2 * LH))
         ts(W("h16", o + LH * h, LH), IND(W(w2, 2 * LH * h, 2 * LH), W("lst", L_ECP[1], BL)), -2048.0, ALU.add)
-        for j, b in enumerate(four):
-            for s in range(RC * j, RC * j + RC):
-                mm(W(b, LH * (s % RC), LH), W("ROT", 128 * s, 128), W("h16", o + LH * h, LH), True, True)
-            if evac_v[j]:
-                cp(W("var", 8 * o + 8 * LH * h + 512 * j, 512), V(b, 0, 512))
+        s = 0
+        for (b, n), on_v in zip(four, evac_v):
+            for j in range(n // LH):
+                mm(W(b, LH * j, LH), W("ROT", 128 * (s + j), 128), W("h16", o + LH * h, LH), True, True)
+            if on_v:
+                cp(W("var", 8 * o + 8 * LH * h + LH * s, n), W(b, 0, n))
             else:
-                act(W("var", 8 * o + 8 * LH * h + 512 * j, 512), V(b, 0, 512), AF.Identity)
+                act(W("var", 8 * o + 8 * LH * h + LH * s, n), W(b, 0, n), AF.Identity)
+            s += n // LH
 
     tt(V("uf", 32, 48), V("uf", 16, 32), V("base", 16, 32), ALU.add)
     cp(V("u16", 16, 32), V("uf", 32, 48))
     fin = c["FIN"]
     for h in range(H):
-        finish("qf", L_EDUP, "wa", "wb", 0, ["S0", "S1", "S2", "P6"][2 * h:2 * h + 4 // H], h, fin[0], [0] * 4)
+        finish("qf", L_EDUP, "wa", "wb", 0, [(banks[h], 1024)], h, fin[0], [0])
     act(V("fin", 0, 256), IND(V("var", 0, 2048), V("u16", 16, 32)), AF.Identity, bias=2048.0)
     store(T.yr[:], V("fin", 0, 256), 2.7)
     for h in range(1 if MP else H):
         left_tail(ST - 1, h)
     for h in range(H):
-        finish("pf", L_PDUP, "wc", "wd", 256, ["KA", "P5", "KB", "S0"][2 * h:2 * h + 4 // H], h, fin[1 + h], [1, 0, 1, 0] if h == H - 1 else fin[3:5])
+        finish("pf", L_PDUP, "wc", "wd", 256, [("KB", 512), ("P6", 512)] if h else [("S0", 1024)], h, fin[1 + h], [1, 0] if h else fin[3:4])
     for h in range(H):
         o, v = W("fin", 256 + LH * h, LH), IND(W("var", 2048, 8 * LH * (h + 1)), W("u16", 16 + BL * h, BL))
         if h == H - 1:
@@ -584,6 +599,12 @@ def conflicts(ops):
     return out
 
 
+def reads_from(ops, k, j):
+    if ops[k][0] != ops[j][0] or ops[k][4] is not None:
+        return True
+    return any(a[0] == b[0] and a[1] < b[2] and b[1] < a[2] for a in ops[k][3] for b in ops[j][2])
+
+
 def figures(g, T):
     out, keep = [], dict(CFG)
     for m in keep["models"]:
@@ -602,6 +623,8 @@ def plan(ops, deps, others):
             kids[k].append(j)
 
     def gap(k, j):
+        if c["SOFT"] and not reads_from(ops, k, j):
+            return 0.0
         if ops[k][0] == "pe":
             return 0.0 if ops[j][0] == "pe" else c["wake"] + 0.1
         return 0.0 if ops[j][0] == "far" else c["wake"]
@@ -697,7 +720,7 @@ def emit(g, T, ops, deps, order, nstore, nsent, neng):
         if q != "far":
             kn = known[q]
             for k in sorted(deps[n], key=lambda k: -rank[k]):
-                if q == "pe" and ops[k][0] == "pe":
+                if q == "pe" and ops[k][0] == "pe" or CFG["SOFT"] and not reads_from(ops, k, n):
                     continue
                 s, p = sig[k]
                 if kn.get(s, 0) >= p:

@@ -4,57 +4,58 @@ from concourse.mybir import AluOpType as ALU, ActivationFunctionType as AF, Axis
 
 ST = 6
 CFG = {
-    "H": 2,
-    "NA": (7, 4),
-    "XF": (0, 3),
-    "XFL": (0, 2),
-    "MIDSEP": 0,
-    "MP": 0,
-    "CPA": 0,
-    "g": 1.56, "sc": 3.8, "cy": 0.001, "pe": 0.0005, "wake": 0.14, "fix": 0.005, "afix": 0.1, "far": 2.8, "issue": 0.5,
-    "bw": 90e3, "row": 0.5, "rounds": 3, "BM": 1, "FIN": (0, 1, 1, 0, 0),
-    "seed": 0, "jit": 1.0, "win": 2.0, "search": 1200, "XPE": 0, "XV": 0, "SOFT": 0, "SV": 1, "GC": 4, "AC": 4,
-    "models": ({"far": 2.3}, {"wake": 0.19, "cy": 0.00083, "afix": 0.065, "far": 2.3},
-               {"wake": 0.2, "cy": 0.0012, "g": 1.8, "far": 3.0}, {"wake": 0.1, "afix": 0.18, "far": 2.3}),
+    "D": ("rrrrrrrrsssssssa", "ssaaaaaasssssssa"), "F": ("ssssssss", "ssssssss"),
+    "D0": ("rrrrrrrrsssssssa", "ssaaaaaasssssssa"), "FL": ("ssssssss", "ssssssss"),
+    "FIRST": (0, 1),
+    "CPS": (2, 2),
+    "GC": 4, "AC": 4, "RC": 4,
+    "MIX": 1, "X2": 1, "SC": 2, "lead": {}, "YT": (0, 0), "ZV": (1, 1), "PV": 0, "CUT": (0, 1), "ZW": (1, 1), "ZS": 0, "SGN": (0, 0),
+    "short": 0.16, "bonus": 0.0, "RU": 0, "MK": (0, 0), "reach": 2.0, "FIN": 1, "END": "r0 f1 p0 r1 p1", "EV": (0, 5, 1, 1),
+    "order": ("-f1a1 d0g0 d0g1 d0a0 d0a1 d0b0 d1g1 d1g2 d1g0 d1a1 d1b2 d1b0 d1a2 d1a0 d1b1 f0g0 f0g1 t0z f0a0 f0a1 f1g0 f1g1 t1z f1a0",
+              "d0v0 d0v1 d0v2 d0v3 d0v4 d0v5 d0v6 d0v7 d0c0 d0v15 d0c1 d1v15 d1v2 d1v3 d1v4 t0ki d1v5 t0U d1v6 t0M d1v7",
+              "d0s0 d0s1 d0k d1s1 d1s2 d1s0 d1k", "t0pors t0pozs t1pors t1pozs", "t0uh t0uh' t0MS256' t0uu t1ys", "t0avg t1yu",
+              "t1uh t1uh' t1avg xX t1uu xX'", "t1MS264 t1K1384 f1s0 t1MS264' f1s1", "t1P1192' f1P1320"), "heat": 0.0, "swaps": 13000, "blame": 300, "back": 3, "step": 0.5, "mean": 0.5,
+    "g": 1.56, "sc": 3.8, "cy": 0.0009, "pe": 0.00047, "wake": 0.17, "fix": 0.005, "afix": 0.08, "far": 3.5, "issue": 0.5,
+    "bw": 90e3, "row": 0.5, "rounds": 4, "seed": 4, "jit": 1.0, "win": 2.0, "search": 0,
+    "models": ({"cy": 0.00083, "pe": 0.00042, "afix": 0.065, "far": 2.0, "wake": 0.15},
+               {"wake": 0.2, "cy": 0.0012, "pe": 0.0006, "g": 1.8, "far": 4.5},
+               {"wake": 0.15, "cy": 0.00083, "pe": 0.00042, "g": 1.56, "afix": 0.065, "far": 3.0, "issue": 1.2, "row": 1.0},
+               {"wake": 0.2, "cy": 0.00083, "pe": 0.00042, "g": 1.2, "afix": 0.065, "far": 4.5}),
 }
 
 SCRATCH = {
-    "X": ("sbuf", [128, 4096], "bfloat16"), "G": ("sbuf", [128, 4096], "bfloat16"),
-    "DD": ("sbuf", [128, 4096], "bfloat16"), "AB": ("sbuf", [128, 4096], "bfloat16"), "AF": ("sbuf", [128, 2048], "bfloat16"),
-    "zl": ("sbuf", [128, ST * 384], "bfloat16"), "zs": ("sbuf", [128, ST * 384], "bfloat16"),
-    "ql": ("sbuf", [128, ST * 256], "uint16"), "qs": ("sbuf", [128, ST * 256], "uint16"),
-    "B": ("sbuf", [128, ST * 288], "float32"), "pin": ("sbuf", [128, ST * 256], "int32"),
-    "PX": ("sbuf", [128, ST * 256], "int32"), "PY": ("sbuf", [128, ST * 256], "int32"),
+    "X": ("sbuf", [128, 4096], "bfloat16"), "X2": ("sbuf", [128, 4096], "bfloat16"),
+    "G": ("sbuf", [128, 6144], "bfloat16"), "DD": ("sbuf", [128, 6144], "bfloat16"), "AB": ("sbuf", [128, 6144], "bfloat16"),
+    "zl": ("sbuf", [128, ST * 1024], "bfloat16"), "zs": ("sbuf", [128, ST * 1024], "bfloat16"),
+    "rl": ("sbuf", [128, ST * 512], "float16"), "rs": ("sbuf", [128, ST * 512], "float16"),
+    "var": ("sbuf", [128, 4096], "float32"), "tf": ("sbuf", [128, 24], "float32"), "tu": ("sbuf", [128, 16], "uint16"),
+    "yd": ("sbuf", [128, 256], "bfloat16"), "nt": ("sbuf", [128, 64], "bfloat16"), "rc": ("sbuf", [128, 128], "float16"),
+    "pn": ("sbuf", [128, ST * 256], "float16"), "ps": ("sbuf", [128, ST * 256], "float16"),
+    "ru": ("sbuf", [128, ST * 256], "uint16"), "rv": ("sbuf", [128, ST * 256], "uint16"),
     "rawp": ("sbuf", [128, 256], "int32"), "rawq": ("sbuf", [128, 256], "int32"), "thi": ("sbuf", [128, 8], "int32"),
-    "wa": ("sbuf", [128, 512], "float32"), "wb": ("sbuf", [128, 512], "float32"),
-    "wc": ("sbuf", [128, 512], "float32"), "wd": ("sbuf", [128, 512], "float32"),
-    "qf": ("sbuf", [128, 256], "float32"), "pf": ("sbuf", [128, 256], "float32"),
-    "h16": ("sbuf", [128, 512], "float16"), "var": ("sbuf", [128, 4096], "float32"), "fin": ("sbuf", [128, 512], "float32"),
-    "ci": ("sbuf", [128, 256], "int32"), "cj": ("sbuf", [128, 128], "int32"), "col": ("sbuf", [128, 64], "float32"),
-    "idx": ("sbuf", [128, 272], "bfloat16"), "I": ("sbuf", [128, 128], "bfloat16"), "NI": ("sbuf", [128, 128], "bfloat16"),
-    "W1": ("sbuf", [128, 144], "bfloat16"), "W32": ("sbuf", [128, 144], "bfloat16"), "BO": ("sbuf", [128, 128], "bfloat16"),
-    "C": ("sbuf", [128, 256], "bfloat16"), "ROT": ("sbuf", [128, 1024], "float16"), "lst": ("sbuf", [128, 160], "uint16"),
-    "base": ("sbuf", [128, 64], "float32"), "ZR": ("sbuf", [128, 128], "bfloat16"),
-    "tr": ("sbuf", [128, 512], "float32"), "ki": ("sbuf", [128, 32], "int32"), "U": ("sbuf", [128, 128], "int32"),
-    "m": ("sbuf", [128, 128], "int32"), "t2": ("sbuf", [128, 128], "int32"), "pa16": ("sbuf", [128, 128], "uint16"),
-    "k2": ("sbuf", [128, 256], "float32"), "y16": ("sbuf", [128, 16], "uint16"), "y": ("sbuf", [128, 256], "bfloat16"),
-    "S": ("sbuf", [128, 256], "bfloat16"), "u7": ("sbuf", [128, 128], "bfloat16"), "mdq": ("sbuf", [128, 128], "float32"),
-    "Qa": ("sbuf", [128, 128], "float32"), "pr1": ("sbuf", [128, 128], "int32"), "pr2": ("sbuf", [128, 128], "int32"),
-    "pr3": ("sbuf", [128, 128], "float32"), "pr4": ("sbuf", [128, 128], "int32"), "Lc": ("sbuf", [128, 128], "bfloat16"),
-    "junk": ("sbuf", [128, 128], "bfloat16"), "ui": ("sbuf", [128, 32], "int32"), "uf": ("sbuf", [128, 48], "float32"),
-    "u16": ("sbuf", [128, 32], "uint16"), "avg": ("sbuf", [128, 256], "int32"), "lim": ("sbuf", [128, 32], "float32"),
-    "li": ("sbuf", [128, 16], "int32"),
-    "S0": ("psum", [128, 1024], "float32"), "S1": ("psum", [128, 1024], "float32"),
-    "KA": ("psum", [128, 512], "float32"), "KB": ("psum", [128, 512], "float32"),
-    "P6": ("psum", [128, 512], "float32"), "P7": ("psum", [128, 512], "float32"),
+    "h1": ("sbuf", [128, 512], "float16"), "h2": ("sbuf", [128, 512], "float16"), "fin": ("sbuf", [128, 512], "float32"),
+    "rm": ("sbuf", [128, 3072], "float16"), "bit": ("sbuf", [128, 768], "int32"),
+    "ci": ("sbuf", [128, 32], "int32"), "cj": ("sbuf", [128, 64], "int32"), "col": ("sbuf", [128, 64], "float32"),
+    "idx": ("sbuf", [128, 272], "bfloat16"), "WB": ("sbuf", [128, 32 * 128], "bfloat16"), "WH": ("sbuf", [128, 16 * 128], "float16"),
+    "WF": ("sbuf", [128, 128], "float32"), "WR": ("sbuf", [128, 432], "bfloat16"),
+    "C": ("sbuf", [128, 448], "bfloat16"), "lst": ("sbuf", [128, 8], "uint16"), "base": ("sbuf", [128, 16], "float16"),
+    "tr": ("sbuf", [128, 512], "float32"), "ki": ("sbuf", [128, 16], "int32"), "U": ("sbuf", [128, 128], "int32"),
+    "M": ("sbuf", [128, 128], "int32"), "T2": ("sbuf", [128, 128], "int32"), "sg": ("sbuf", [128, 128], "bfloat16"),
+    "ab": ("sbuf", [128, 256], "bfloat16"), "dq": ("sbuf", [128, 128], "float32"), "dh": ("sbuf", [128, 128], "float32"),
+    "qa": ("sbuf", [128, 128], "float16"), "pa": ("sbuf", [128, 128], "float16"), "pu": ("sbuf", [128, 128], "uint16"),
+    "ys": ("sbuf", [128, 128], "float16"), "yu": ("sbuf", [128, 16], "uint16"), "y": ("sbuf", [128, 256], "bfloat16"),
+    "p1": ("sbuf", [128, 128], "float32"), "p2": ("sbuf", [128, 128], "int32"), "rem": ("sbuf", [128, 128], "int32"),
+    "lc": ("sbuf", [128, 128], "bfloat16"), "f": ("sbuf", [128, 256], "float32"), "avg": ("sbuf", [128, 256], "int32"),
+    "uh": ("sbuf", [128, 32], "float16"), "uu": ("sbuf", [128, 16], "uint16"), "at": ("sbuf", [128, 64], "float16"),
+    "lim": ("sbuf", [128, 16], "float32"), "hh": ("sbuf", [128, 8], "bfloat16"), "w": ("sbuf", [128, 128], "bfloat16"),
+    "S": ("psum", [128, 1536], "float32"), "K0": ("psum", [128, 512], "float32"), "K1": ("psum", [128, 512], "float32"),
+    "P0": ("psum", [128, 512], "float32"), "P1": ("psum", [128, 512], "float32"), "MS": ("psum", [128, 512], "float32"),
 }
-PSUM = ("S0", "S1", "KA", "KB", "P6", "P7")
-KINDS = ("az", "aq", "am", "ad", "ap")
-SEMAPHORES = (["pe", "dve", "act", "pool", "sent", "stored", "lx", "lq", "lp", "lz0", "lz1", "lt"]
-              + ["%s%d_%d" % (k, s, h) for k in KINDS for s in range(1, ST) for h in range(2)])
-
-
+PSUM = ("S", "K0", "K1", "P0", "P1", "MS")
+SEMAPHORES = (["pe", "dve", "act", "pool", "sent", "stored", "lx", "lq", "lp", "lz0", "lz1", "lt", "l2"]
+              + ["%s%d_%d" % (k, s, h) for k in ("az", "ar", "ap", "au") for s in range(1, ST) for h in range(2)])
 PLANS = {}
+HA, HU = 132096.0, 16448.0
 
 
 def V(name, a, b, step=1):
@@ -75,16 +76,28 @@ def size(v):
     return (v[2] - v[1] + v[3] - 1) // v[3]
 
 
+def kind(v):
+    return SCRATCH[v[0]][2]
+
+
 def two_bytes(v):
-    return SCRATCH[v[0]][2] in ("bfloat16", "float16", "uint16")
+    return kind(v) in ("bfloat16", "float16", "uint16")
+
+
+def banks_of(views):
+    return sorted({(v[0], k) for v in views if v[0] in PSUM for k in range(v[1] // 512, (v[2] - 1) // 512 + 1)})
 
 
 def build(g, T, nxt_addr, mask, neng):
-    ops = []
+    ops, head, times = [], [], {}
     c = CFG
-    H = c["H"]
-    BL, LH = 16 // H, 256 // H
-    R8 = 8 * BL
+    at = [-1, "", 0]
+
+    def enter(s, name):
+        at[:] = [s, name, 0]
+
+    def call(name):
+        ops[-1][7] = (at[0], at[1] + name, at[2])
 
     def ap(v):
         if v[0] == "*":
@@ -93,18 +106,20 @@ def build(g, T, nxt_addr, mask, neng):
             return T[v[0]][:, v[1]:v[2]]
         return T[v[0]][:, v[1]:v[2]:v[3]]
 
-    def op(q, emit, reads, writes, cost, sem=None, cnt=0):
-        rd, wr = [], []
+    def op(q, emit, reads, writes, cost, sem=None, cnt=0, adds=(), to=None):
+        acc = []
         for v in reads:
             if isinstance(v, tuple):
-                rd += [v[1], v[2]] if v[0] == "*" else [v]
+                acc += [(v[1], "r"), (v[2], "r")] if v[0] == "*" else [(v, "r")]
         for v in writes:
-            if v[0] == "*":
-                wr.append(v[1])
-                rd.append(v[2])
-            else:
-                wr.append(v)
-        ops.append([q, emit, rd, wr, sem, cnt, cost])
+            acc += [(v[1], "w"), (v[2], "r")] if v[0] == "*" else [(v, "w")]
+        acc += [(v, "a") for v in adds]
+        what = ([v for v, m in acc if m == "w"] + [acc[0][0]])[0]
+        name = at[1] + (q[:2] if q in ("pool", "far", "sp") else "") + what[0] + (str(what[1]) if what[0] in PSUM else "")
+        times[at[0], name] = times.get((at[0], name), 0) + 1
+        name += "'" * (times[at[0], name] - 1)
+        (ops if to is None else to).append([q, emit, acc, sem, cnt, cost, banks_of([v for v, _ in acc]), (at[0], name, at[2])])
+        at[2] += 1
 
     def sc(x):
         return ap(x) if isinstance(x, tuple) else x
@@ -123,32 +138,43 @@ def build(g, T, nxt_addr, mask, neng):
         k = 1 if a[0] in PSUM or b[0] in PSUM else 2
         op("dve", lambda: g.vector.tensor_tensor(ap(o), ap(a), ap(b), alu), [a, b], [o], vcost(o, a, k))
 
-    def ts(o, a, s1, o1, s2=None, o2=None):
+    def ts(o, a, s1, o1, s2=None, o2=None, to=None):
         t = vcost(o, a, half(o, a))
         if o2 is None:
-            op("dve", lambda: g.vector.tensor_scalar(ap(o), ap(a), sc(s1), None, o1), [a, s1], [o], t)
+            op("dve", lambda: g.vector.tensor_scalar(ap(o), ap(a), sc(s1), None, o1), [a, s1], [o], t, to=to)
         else:
-            op("dve", lambda: g.vector.tensor_scalar(ap(o), ap(a), sc(s1), sc(s2), o1, o2), [a, s1, s2], [o], t)
+            op("dve", lambda: g.vector.tensor_scalar(ap(o), ap(a), sc(s1), sc(s2), o1, o2), [a, s1, s2], [o], t, to=to)
 
     def cp(o, a):
         op("dve", lambda: g.vector.tensor_copy(ap(o), ap(a)), [a], [o], vcost(o, a, half(o, a)))
 
     def tr32(o, a):
-        op("dve", lambda: g.vector.transpose(ap(o), ap(a)), [a], [o], vcost(o, a, 1))
+        op("dve", lambda: g.vector.transpose(ap(o), ap(a)), [a], [o], vcost(o, a, half(o, a)))
+
+    def red(o, a, alu):
+        op("dve", lambda: g.vector.tensor_reduce(ap(o), ap(a), AxisListType.X, alu), [a], [o], vcost(o, a, 1))
 
     def ms(o, k):
         op("dve", lambda: g.vector.memset(ap(o), k), [], [o], vcost(o, o, half(o, o)))
 
-    def act(o, a, f, bias=0.0, scale=1.0, acc=None):
+    def act(o, a, f, bias=0.0):
         t = 0.065 + size(a) * c["g"] * c["cy"] if a[0] == "*" else c["afix"] + max(64, size(a)) * c["cy"]
-        if acc is None:
-            op("act", lambda: g.scalar.activation(ap(o), ap(a), f, bias=sc(bias), scale=scale), [a, bias], [o], t)
-        else:
-            op("act", lambda: g.scalar.activation(ap(o), ap(a), f, bias=sc(bias), scale=scale, accum_out=ap(acc)),
-               [a, bias], [o, acc], t)
+        op("act", lambda: g.scalar.activation(ap(o), ap(a), f, bias=sc(bias)), [a, bias], [o], t)
 
-    def mm(o, l, r, start, stop):
-        op("pe", lambda: g.tensor.matmul(ap(o), ap(l), ap(r), start, stop), [l, r], [o], max(64, size(r)) * c["pe"])
+    def mms(*groups, start=True, stop=True):
+        def emit():
+            for items in groups:
+                for i, (o, l, r) in enumerate(items):
+                    ins = g.tensor.matmul(ap(o), ap(l), ap(r), start and i == 0, stop and i == len(items) - 1)
+            return ins
+        every = [x for items in groups for x in items]
+        mark = [("#%s%d" % banks_of([every[0][0]])[0], 0, 1, 1)]
+        t = sum(max(64, size(r)) * (4 if kind(r) == "float32" else 1) for _, _, r in every) * c["pe"]
+        ins = [v for _, l, r in every for v in (l, r)]
+        if start and stop:
+            op("pe", emit, ins + mark, [items[0][0] for items in groups], t)
+        else:
+            op("pe", emit, ins, [o for o, _, _ in every] + mark, t)
 
     def iota(o, pat, base, cm, flt=False):
         t = 0.13 + 2 * size(o) * c["cy"]
@@ -157,461 +183,534 @@ def build(g, T, nxt_addr, mask, neng):
         else:
             op("pool", lambda: g.iota(ap(o), pat, base, cm), [], [o], t)
 
-    def load(q, o, src, sem, t):
-        op(q, lambda: (g.sync if q == "sp" else g.scalar).dma_start(ap(o), src).then_inc(T.sem[sem], 16), [], [o], t, sem, 16)
+    def load(q, o, src, sem, t, reads=()):
+        op(q, lambda: (g.sync if q == "sp" else g.scalar).dma_start(ap(o), sc(src)).then_inc(T.sem[sem], 16),
+           list(reads), [o], t, sem, 16)
 
-    nstore = [0]
+    nstore, nsent = [0], [0]
 
     def store(dst, a, t):
         nstore[0] += 1
         op("sp", lambda: g.sync.dma_start(dst, ap(a)).then_inc(T.sem.stored, 16), [a], [], t, "", 0)
 
-    nsent = [0]
-
-    def send(dst, srcs, sem):
+    def send(dst, src, sem):
         nsent[0] += 1
-        if len(srcs) == 1:
-            op("pool", lambda: g.remote_dma(ap(dst), ap(srcs[0]), T.sem[sem], T.sem.sent, nxt_addr[1], nxt_addr[0], mask),
-               srcs, [], c["issue"], "", 0)
+        n, k = size(src), size(dst) // size(src)
+        if k == 1:
+            op("pool", lambda: g.remote_dma(ap(dst), ap(src), T.sem[sem], T.sem.sent, nxt_addr[1], nxt_addr[0], mask),
+               [src], [], c["issue"], "", 0)
         else:
             op("pool", lambda: g.remote_dma_fused([RemoteDMATransfer(
-                dst_ids=[DstId(rid=nxt_addr[0], pnc=nxt_addr[1])], dma_engine_mask=mask, remote_sem=T.sem[sem],
-                srcs=[ap(a) for a in srcs], dsts=[ap(dst)], alu_op=1)], local_sem=T.sem.sent), srcs, [], c["issue"], "", 0)
-        op("far", None, [], [dst], c["far"] + c["row"] + 128 * size(dst) * (2 if two_bytes(dst) else 4) * len(srcs) / c["bw"], sem, neng)
+                dst_ids=[DstId(rid=nxt_addr[0], pnc=nxt_addr[1])] * k, dma_engine_mask=mask, remote_sem=T.sem[sem], src=ap(src),
+                dsts=[ap(W(dst[0], dst[1] + n * j, n)) for j in range(k)])], local_sem=T.sem.sent), [src], [], c["issue"], "", 0)
+        op("far", None, [], [dst], c["far"] + k * c["row"] + 256 * size(dst) / c["bw"], sem, neng * k)
 
     def c1(j):
         return V("col", j, j + 1)
 
-    I, NI, BO = V("I", 0, 128), V("NI", 0, 128), V("BO", 0, 128)
+    IDX = V("idx", 0, 128)
+    made = {}
+
+    def wt(k, like, shift=0.0, to=0):
+        buf = "WF" if kind(like) == "float32" else "WH" if kind(like) == "float16" and not c["MIX"] else "WB"
+        key = (buf, k, shift, to)
+        if key not in made:
+            made[key] = W(buf, 128 * len([x for x in made if x[0] == buf]), 128)
+            keep = list(at)
+            at[:] = [-1, "w", len(made)]
+            if shift:
+                ts(made[key], IDX, shift, ALU.add, c1(to), ALU.is_equal, to=head)
+            else:
+                ts(made[key], IDX, c1(to), ALU.is_equal, float(k), ALU.mult, to=head)
+            at[:] = keep
+        return made[key]
+
+    def lin(o, *terms):
+        return [(o, wt(k, v), v) for k, v in terms]
+
     XW = V("X", 0, 4096)
-    L_BC, L_DUP, L_CP, L_CQ, L_EDUP, L_ECP = (W("lst", 0, R8 // 16), V("lst", 8, 40), V("lst", 40, 56), V("lst", 56, 72),
-                                              V("lst", 72, 104), V("lst", 104, 120))
-    NCNT, NLIM, PLIM, NTH = V("lim", 0, 1), V("lim", 8, 9), V("lim", 16, 17), V("lim", 24, 25)
-    ZW = LH + R8
-    MP = H == 1 or c["MP"]
-    L_PDUP = V("lst", 120, 152) if H == 2 and MP else L_EDUP
+    BC = W("lst", 0, 4)
+    A, THR, HH, AT = V("lim", 0, 1), V("lim", 8, 9), V("hh", 0, 1), V("at", 0, 64)
+    CF, NTH = c1(8), V("lim", 12, 13)
+    HALF, C2K = W("C", 128, 64), W("C", 192, 256)
 
     load("sp", V("rawq", 0, 256), T.pr[:], "lq", 2.6)
-    load("sp", V("rawp", 0, 256), T.pl[:], "lp", 3.1)
-    load("sp", XW, T.xt[:], "lx", 7.5)
-    for h in range(H):
-        load("act", W("zl", ZW * h, LH), T.z0[:, LH * h:LH * h + LH], "lz%d" % h, 3.5)
+    load("sp", XW, T.xt[:], "lx", 7.0)
+    load("sp", V("rawp", 0, 256), T.pl[:], "lp", 7.5)
+    for h in range(2):
+        load("act", W("zl", 512 * h, 128), T.z0[:, 128 * h:128 * h + 128], "lz%d" % h, 3.5)
     load("act", V("thi", 0, 1), T.th[:], "lt", 3.5)
-    iota(V("cj", 0, 8), [[1, 8]], 0, 1)
-    iota(V("ci", 0, 32), [[16, 16], [0, 2]], 0, 0)
-    iota(V("ci", 32, 48), [[1, 16]], 0, 0)
-    iota(V("ci", 48, 64), [[0, H], [H, BL]], 0, 0)
-    iota(V("ci", 96, 112), [[256, H], [0, BL]], 0, 0)
-    iota(V("ci", 112, 128), [[8, 2], [256, H], [H, BL // 2]] if MP else [[256, H], [H, BL]], 0, 0)
+    iota(V("cj", 0, 1), [[1, 1]], 0, 1)
     iota(V("idx", 0, 144), [[1, 144]], 0, 0, True)
-    for h in range(H):
-        iota(W("zl", ZW * h + LH, R8), [[-2, 8], [0, BL]], 1, 0, True)
     iota(V("idx", 144, 272), [[1, 8], [0, 16]], 0, 0, True)
-    iota(V("ci", 64, 96), [[128, H], [1, BL], [0, 2]], 0, 0)
-    iota(V("ci", 160, 176), [[8 * LH, H], [16, BL]], 0, 0)
-    if L_PDUP != L_EDUP:
-        iota(V("ci", 128, 160), [[64, 2], [1, 8], [0, 2]], 0, 0)
+    iota(V("ci", 0, 16), [[256, 16]], int(HU), 0)
+    iota(W("nt", 0, 64), [[-2, 8], [0, 8]], 1, 0, True)
+    cp(c1(0), V("cj", 0, 1))
     ts(V("cj", 8, 9), V("cj", 0, 1), 15, ALU.bitwise_and)
     ts(V("cj", 16, 17), V("cj", 0, 1), 16, ALU.bitwise_and)
-    ts(V("cj", 56, 57), V("cj", 0, 1), BL - 1, ALU.bitwise_and)
-    cp(c1(0), V("cj", 0, 1))
-    cp(c1(1), V("cj", 8, 9))
-    cp(c1(2), V("cj", 16, 17))
-    cp(c1(9), V("cj", 56, 57))
-    ts(L_DUP, V("ci", 0, 32), c1(1), ALU.add)
-    ts(c1(3), c1(9), 32.0, ALU.mult, c1(2), ALU.add)
-    ts(c1(10), c1(1), c1(9), ALU.subtract, 1.0 / BL, ALU.mult)
-    tt(c1(4), c1(0), c1(1), ALU.subtract)
-    ts(V("cj", 64, 80), V("ci", 48, 64), c1(10), ALU.add, 1.0, ALU.add)
-    ts(V("cj", 80, 96), V("cj", 64, 80), 15, ALU.bitwise_and)
-    tt(V("base", 32, 48), V("cj", 80, 96), V("ci", 96, 112), ALU.add)
-    ts(L_CQ, V("base", 32, 48), c1(3), ALU.add)
-    ts(L_CP, V("ci", 112, 128), c1(3), ALU.add, c1(10), ALU.add)
-    ts(V("W1", 0, 144), V("idx", 0, 144), -16.0, ALU.add, c1(4), ALU.is_equal)
-    ts(I, V("idx", 0, 128), c1(0), ALU.is_equal)
-    ts(NI, V("idx", 0, 128), c1(0), ALU.is_equal, -1.0, ALU.mult)
-    if c["XPE"]:
-        ms(V("ZR", 0, 128), 0.0)
-    ms(W("C", 128, 64), 1.0)
-    ms(W("C", 0, R8), -2.0)
-    ms(W("C", R8, R8), -18.0)
-    ts(V("W32", 0, 144), V("W1", 0, 144), -32.0, ALU.mult)
+    ts(V("cj", 24, 25), V("cj", 0, 1), 7, ALU.bitwise_and)
+    ts(c1(1), V("cj", 16, 17), 1024.0, ALU.mult, c1(0), ALU.add)
+    ts(c1(2), V("cj", 16, 17), -1024.0, ALU.mult, c1(0), ALU.add)
+    ts(c1(2), c1(2), 16384.0, ALU.add)
+    ts(c1(4), V("cj", 8, 9), -1.0, ALU.mult, c1(0), ALU.add)
     ts(c1(5), c1(4), 1.0 / 16, ALU.mult)
-    ts(c1(6), c1(1), 16.0, ALU.mult)
-    ts(c1(11), c1(1), float(BL), ALU.mult)
-    tt(c1(7), c1(1), c1(2), ALU.add)
-    cp(V("wa", 0, 512), IND(V("rawq", 0, 256), L_DUP))
-    tr32(V("wb", 0, 512), V("wa", 0, 512))
-    cp(V("qf", 0, 256), IND(V("wb", 0, 512), L_CQ))
-    cp(V("ql", 0, 256), V("qf", 0, 256))
-    for h in range(H):
-        tt(W("tr", R8 * h, R8), W("qf", 2 * R8 * h + R8, R8), W("qf", 2 * R8 * h, R8), ALU.subtract)
-        ts(W("B", 18 * BL * h + 10 * BL, R8), W("tr", R8 * h, R8), 0.5, ALU.mult)
-        tt(W("B", 18 * BL * h + BL, R8), W("qf", 2 * R8 * h, R8), W("B", 18 * BL * h + 10 * BL, R8), ALU.add)
-    cp(V("wc", 0, 512), IND(V("rawp", 0, 256), L_DUP))
-    tr32(V("wd", 0, 512), V("wc", 0, 512))
-    cp(V("pin", 0, 256), IND(V("wd", 0, 512), L_CP))
-    ts(L_BC, W("ci", 32, R8 // 16), 0.0, ALU.mult, c1(9), ALU.add)
-    ts(BO, V("idx", 144, 272), c1(5), ALU.is_equal)
-    ts(V("base", 0, 16), V("ci", 32, 48), 256.0, ALU.mult, c1(6), ALU.add)
-    ts(NTH, V("thi", 0, 1), -1.0, ALU.mult, -0.9375, ALU.add)
-    ms(NCNT, -2048.0)
-    ts(NLIM, V("thi", 0, 1), -1.0, ALU.mult, -0.9375, ALU.add)
-    ts(V("cj", 48, 56), V("cj", 0, 8), 7, ALU.bitwise_and)
-    ts(V("cj", 24, 25), V("cj", 0, 1), 120, ALU.bitwise_and)
-    ts(L_EDUP, V("ci", 64, 96), c1(11), ALU.add)
-    if L_PDUP != L_EDUP:
-        ts(c1(12), c1(10), 64.0, ALU.mult, c1(11), ALU.add)
-        ts(L_PDUP, V("ci", 128, 160), c1(12), ALU.add)
-    cp(c1(8), V("cj", 24, 25))
-    ts(L_ECP, V("ci", 32, 48), 32.0, ALU.mult, c1(7), ALU.add)
-    ts(V("col", 16, 24), V("cj", 48, 56), c1(8), ALU.add)
-    ts(V("base", 16, 32), V("ci", 160, 176), c1(1), ALU.add)
-    for s in range(8):
-        ts(V("ROT", 128 * s, 128 * s + 128), V("idx", 0, 128), c1(16 + s), ALU.is_equal)
+    ts(c1(6), V("cj", 8, 9), 16.0, ALU.mult)
+    cp(c1(7), V("cj", 24, 25))
+    ts(BC, W("idx", 0, 4), 0.0, ALU.mult, c1(7), ALU.add)
+    ts(V("base", 0, 16), V("ci", 0, 16), c1(6), ALU.add)
+    ts(W("WR", 0, 144), V("idx", 0, 144), -16.0, ALU.add, c1(4), ALU.is_equal)
+    ts(W("WR", 144, 144), W("WR", 0, 144), -32.0, ALU.mult)
+    ts(W("WR", 288, 144), W("WR", 0, 144), 32.0, ALU.mult)
+    BO = W("WB", 31 * 128, 128)
+    ts(BO, V("idx", 144, 272), c1(5), ALU.is_equal, 32.0, ALU.mult)
+    ms(W("C", 0, 64), -2.0)
+    ms(W("C", 64, 64), -18.0)
+    ms(HALF, 0.5)
+    ms(C2K, 2048.0)
+    ts(AT, HALF, -65536.0, ALU.mult)
+    ts(CF, V("thi", 0, 1), 32.0, ALU.mult, HA + 30, ALU.add)
+    ts(THR, V("thi", 0, 1), 32.0, ALU.mult, 30.0, ALU.add)
+    ts(NTH, V("thi", 0, 1), -32.0, ALU.mult, -30.0, ALU.add)
+    for h in range(2):
+        cp(W("rl", 256 * h + 128, 64), W("nt", 0, 64))
+        ts(W("rl", 256 * h + 192, 64), W("nt", 0, 64), 1.0, ALU.is_equal)
+        for j in range(1, c["ZW"][h]):
+            cp(W("zl", 512 * h + 128 * j, 128), W("zl", 512 * h, 128))
+    if c["FIN"]:
+        iota(V("cj", 32, 40), [[1, 8]], 0, 1)
+        cp(c1(11), V("cj", 8, 9))
+        ts(W("tf", 16, 8), W("idx", 0, 8), 16.0, ALU.mult)
+        ts(V("cj", 40, 48), V("cj", 32, 40), 7, ALU.bitwise_and)
+        ts(c1(12), c1(7), -1.0, ALU.mult, c1(0), ALU.add)
+        ts(V("col", 16, 24), V("cj", 40, 48), c1(12), ALU.add)
+    ops.append("head")
 
-    banks = ["S0", "S1"]
+    def sel(src, dst, like):
+        return wt(1, like, 16.0 * (src - dst), 1 + src)
+
     nb = [0]
-    RC = 512 // LH
-    CH = 64 // BL
 
-    def groups(rows, n):
-        return [rows[j:j + n] for j in range(0, len(rows), n)]
+    def stage():
+        nb[0] += 1
+        return 512 * (nb[0] % 3)
 
-    def at(names, r):
-        return names[1] + BL * ((r & 8) + ((r + names[2]) & 7))
+    def names_in(raw, o, dst, wide):
+        a, b, st = W("h1", o, 256), W("h2", o, 256), stage()
+        ts(a, V(raw, 0, 256), -2048.0, ALU.add)
+        tr32(b, a)
+        it = lin(W("S", st, 256), (1, C2K))
+        for h in range(2):
+            for k in range(8):
+                for g1 in range(2):
+                    it.append((V("S", st + 128 * h + k, st + 128 * h + 128, 8), sel(k & 1, g1, b),
+                               W("h2", o + 128 * h + 32 * (k >> 1) + 16 * g1, 16)))
+        mms(it)
+        for h in range(2):
+            ts(W(dst, wide * h, 128), W("S", st + 128 * h, 128), -2048.0, ALU.add)
 
-    def plain(rows, names, g0, out, sub):
-        for r in groups(rows, c["GC"]):
-            n = len(r) - (1 if names[2] and r[-1] % 8 == 7 and len(r) > 1 else 0)
-            act(W("G", g0 + LH * (r[0] % 8), LH * n), IND(XW, W(names[0], at(names, r[0]), BL * n)), AF.Identity)
-            if n < len(r):
-                act(W("G", g0 + LH * 7, LH), IND(XW, W(names[0], at(names, r[-1]), BL)), AF.Identity)
-        for r2 in groups(rows, 2 * RC):
-            b = banks[nb[0] % 2]
-            nb[0] += 1
-            for i, r in enumerate(groups(r2, RC)):
-                mm(W(b, 512 * i, LH * len(r)), I, W("G", g0 + LH * (r[0] % 8), LH * len(r)), True, False)
-                for j in range(len(r)):
-                    mm(W(b, 512 * i + LH * j, LH), NI, sub, False, j == len(r) - 1)
-            act(W(out[0], out[1] + LH * r2[0], LH * len(r2)), W(b, 0, LH * len(r2)), AF.Abs)
+    names_in("rawq", 0, "rl", 256)
+    names_in("rawp", 256, "pn", 128)
 
-    def fused(rows, names, d0, out, sub, tail):
+    def runs(rows, n, col):
+        out = []
         for r in rows:
-            tt(W("DD", d0 + LH * r, LH), IND(XW, W(names[0], at(names, r), BL)), sub, ALU.subtract)
-        runs = []
-        for r in rows:
-            if runs and runs[-1][-1] + 1 == r and len(runs[-1]) < c["AC"]:
-                runs[-1].append(r)
+            if out and out[-1][-1] + 1 == r and len(out[-1]) < n and col(out[-1][-1]) + 8 == col(r):
+                out[-1].append(r)
             else:
-                runs.append([r])
-        for r in runs:
-            act(W(out[0], out[1] + LH * r[0], LH * len(r)), W("DD", d0 + LH * r[0], LH * len(r)), AF.Abs)
+                out.append([r])
+        return out
 
-    def reduce(bank, c0, w, src, s0, n, first, last):
-        for a in range(16):
-            mm(W(bank, c0, BL * n), V(w, 16 - a, 144 - a), V(src[0], src[1] + LH * s0 + a, src[1] + LH * (s0 + n), 16),
-               first and a == 0, last and a == 15)
-            if a < c["XPE"]:
-                mm(W(bank, c0, BL * n), V("ZR", 0, 128), V(src[0], src[1] + LH * s0 + a, src[1] + LH * (s0 + n), 16), False, False)
+    def fetch(plan, names, col, d0, sub, wide=1):
+        srows = [r for r, k in enumerate(plan) if k == "s"]
+        for i, r in enumerate(runs(srows, c["GC"], col)):
+            act(W("G", d0 + 128 * r[0], 128 * len(r)), IND(XW, W(names, col(r[0]), 8 * len(r))), AF.Identity)
+            call("g%d" % i)
+        for i, r in enumerate(runs(srows, 4, lambda r: 8 * r)):
+            st, n = stage(), 128 * len(r)
+            it = lin(W("S", st, n), (1, W("G", d0 + 128 * r[0], n)))
+            for j in range(len(r)):
+                it += lin(W("S", st + 128 * j, 128), (-1, sub))
+            mms(it)
+            call("s%d" % i)
+            act(W("AB", d0 + 128 * r[0], n), W("S", st, n), AF.Abs)
+            call("a%d" % i)
+        def fused(rows, name):
+            for k in runs(rows, wide, col):
+                n = len(k)
+                tt(W("DD", d0 + 128 * k[0], 128 * n), IND(XW, W(names, col(k[0]), 8 * n)), W(sub[0], sub[1], 128 * n), ALU.subtract)
+                call("v%d" % k[0])
+        for i, r in enumerate(runs([r for r, k in enumerate(plan) if k == "a"], c["AC"], lambda r: 8 * r)):
+            fused(r, "u%d" % i)
+            act(W("AB", d0 + 128 * r[0], 128 * len(r)), W("DD", d0 + 128 * r[0], 128 * len(r)), AF.Abs)
+            call("b%d" % i)
+        for i, r in enumerate(runs([r for r, k in enumerate(plan) if k == "r"], c["RC"], lambda r: 8 * r)):
+            fused(r, "v%d" % i)
+            ts(W("AB", d0 + 128 * r[0], 128 * len(r)), W("DD", d0 + 128 * r[0], 128 * len(r)), 0.0, ALU.max, 2.0, ALU.mult)
+            call("c%d" % i)
 
-    def left_tail(s, h):
-        n = 128 if MP else R8
-        p0 = 256 * s + 2 * n * h
-        LC, E1, E2 = W("Lc", n * h, n), W("P7", 256 + n * h, n), W("P7", 384 + n * h, n)
-        ts(LC, W(fbank(h)[0], 0, n), NLIM, ALU.add, 0.0, ALU.is_lt)
-        if s < ST - 1:
-            tt(W("PY", p0, n), LC, E1, ALU.mult)
-            tt(W("PY", p0 + n, n), LC, E2, ALU.mult)
-            send(W("pin", p0 + 256, 2 * n), [W("PX", p0, 2 * n), W("PY", p0, 2 * n)], "ap%d_%d" % (s + 1, h))
+    def sums(o, w, buf, a0, n):
+        return [(o, W("WR", w + 16 - a, 128), V(buf, a0 + a, a0 + n, 16)) for a in range(16)]
+
+    def reduce(plan, bank, k0, d0, first):
+        cut = []
+        for r in runs([r for r, k in enumerate(plan) if k == "r"], 8, lambda r: 8 * r):
+            cut += sums(W(bank, k0 + 8 * r[0], 8 * len(r)), 288, "DD", d0 + 128 * r[0], 128 * len(r))
+        rest = sums(W(bank, k0, 64), 144, "AB", d0, 1024)
+        if first and cut:
+            mms(first + cut, stop=False)
+            mms(rest, start=False)
         else:
-            tt(E1, LC, E1, ALU.mult)
-            tt(E2, LC, E2, ALU.mult)
-            if MP:
-                tt(W("pf", 0, 256), W("PX", p0, 256), W("P7", 256, 256), ALU.add)
-            else:
-                tt(W("pf", 2 * n * h, n), W("PX", p0, n), E1, ALU.add)
-                tt(W("pf", 2 * n * h + n, n), W("PX", p0 + n, n), E2, ALU.add)
+            mms(first + rest + cut)
 
-    def fbank(h):
-        return ("KB", 0) if H == 1 else ("P5", R8 * h) if MP else ("KB" if h else "KA", 0)
-
-    def pcol(s, h, hi):
-        return 256 * s + (128 * hi + R8 * h if MP else 2 * R8 * h + R8 * hi)
-
-    def remake(s, hs):
-        h, n = hs[0], R8 * len(hs)
-        MD, PA, E1, E2 = [W("P7", 128 * j + R8 * h, n) for j in range(4)]
-        P1, P2, P3, P4, QA = [W(k, R8 * h, n) for k in ("pr1", "pr2", "pr3", "pr4", "Qa")]
-        tt(P1, QA, PA, ALU.mult)
-        ts(P2, P1, 5, ALU.logical_shift_right)
-        tt(P3, P2, PA, ALU.add)
-        ts(P4, P3, NCNT, ALU.add, 2048.0, ALU.add)
-        for k in ([hs] if MP else [[j] for j in hs]):
-            h, n = k[0], R8 * len(k)
-            MD, PA, E1, E2 = [W("P7", 128 * j + R8 * h, n) for j in range(4)]
-            PI, REM = W("PX", pcol(s, h, 0), n), W("PX", pcol(s, h, 1), n)
-            tt(PI, W("pin", pcol(s, h, 1), n), MD, ALU.subtract)
-            ts(REM, W("pr4", R8 * h, n), 4095, ALU.bitwise_and)
-            tt(E1, PA, PI, ALU.subtract)
-            tt(E2, PI, REM, ALU.subtract)
-
-    def limits():
-        cnt = W("P6", 0, 64)
-        mm(cnt, BO, V("Lc", 0, 64), True, False)
-        mm(cnt, BO, V("Lc", 64, 128), False, True)
-        op("dve", lambda: g.vector.tensor_reduce(ap(NCNT), ap(cnt), AxisListType.X, ALU.add, negate=True), [cnt], [NCNT],
-           vcost(NCNT, cnt, 1))
-        ts(V("li", 0, 1), NCNT, 2048.0, ALU.add)
-        ts(V("li", 8, 9), V("li", 0, 1), 31, ALU.bitwise_and)
-        ts(NLIM, V("li", 8, 9), -1.0, ALU.mult, NTH, ALU.add)
+    def t64(name, h):
+        return W(name, 64 * h, 64)
 
     def sums_d(s, h):
-        last = s == ST - 1
-        z0, q0, b0, a0 = 384 * s + ZW * h, 256 * s + 2 * R8 * h, 288 * s + 18 * BL * h, 16 * LH * h
-        Z, NT = W("zl", z0, LH), W("zl", z0 + LH, R8)
-        na = c["NA"][h]
+        K, P = "K%d" % h, "P%d" % h
+        q0, n0 = 512 * s + 256 * h, 256 * s + 128 * h
+        Z, NT = W("zl", 4 * n0, 128), W("rl", q0 + 128, 64)
+        if s == 0 or not c["RU"]:
+            ts(W("ru", n0, 128), W("rl", q0, 128), 2048.0, ALU.add)
+        r1, r0, r9, r8 = W("rl", q0 + 8, 56), W("rl", q0, 8), W("rl", q0 + 72, 56), W("rl", q0 + 64, 8)
+        k = -1 if s == 0 else 1
+        mms(lin(W(K, 128, 56), (1, r9), (-1, r1)), lin(W(K, 184, 8), (k, r8), (-k, r0)),
+            lin(W(K, 192, 64), (0.5, W("rl", q0 + 8, 64))) + lin(W(K, 192, 56), (0.5, r9)) + lin(W(K, 248, 8), (0.5, r0)))
+        mms(lin(W(P, 128, 64), (1, W("pn", n0 + 64, 64)), (-1, W("pn", n0, 64))))
+        plan = c["D" if s else "D0"][h]
         if s:
-            cp(W("B", b0 + R8, BL), W("B", b0, BL))
-            cp(W("B", b0 + 17 * BL, BL), W("B", b0 + 9 * BL, BL))
-        elif not last:
-            send(W("B", b0 + 288, R8), [W("B", b0 + BL, R8)], "am%d_%d" % (s + 1, h))
-        U7 = W("u7", R8 * h, R8)
-        ts(U7, NT, -13.0, ALU.is_equal, 32.0, ALU.mult)
-        QL = ("ql", q0, 1 if s else 0)
-        plain(list(range(8, 8 + na)), QL, 8 * LH * h, ("AB", a0), Z)
-        AB = ("AB", a0)
-        if H == 1:
-            fused(list(range(8 + na, 16)) + [4, 5, 6, 7, 0, 1, 2, 3], QL, a0, AB, Z, True)
-            mm(V("KA", 64, 256), I, V("C", 64, 256), True, False)
-            reduce("KA", 128, "W32", AB, 8, 4, False, False)
-            reduce("KA", 192, "W32", AB, 12, 4, False, False)
-            mm(V("KA", 64, 128), I, W("zl", z0 + LH + 64, 64), False, False)
-            mm(V("KA", 128, 256), I, NT, False, False)
-            mm(V("KA", 128, 256), I, U7, False, False)
-            reduce("KA", 64, "W32", AB, 4, 4, False, True)
-            mm(V("KB", 0, 64), I, V("C", 0, 64), True, False)
-            mm(V("KB", 0, 64), I, W("zl", z0 + LH, 64), False, False)
-            reduce("KB", 0, "W32", AB, 0, 4, False, True)
+            fetch(plan, "ru", lambda r: n0 + 8 * ((r & 8) + ((r + 1) & 7)), 2048 * h, Z, c["ZW"][h])
         else:
-            fused(list(range(8 + na, 16)) + list(range(8)), QL, a0, AB, Z, False)
-            k = "KB" if h else "KA"
-            mm(V(k, 0, 128), I, V("C", 0, 128), True, False)
-            reduce(k, 64, "W32", AB, 8, 8, False, False)
-            mm(V(k, 0, 64), I, NT, False, False)
-            mm(V(k, 64, 128), I, NT, False, False)
-            mm(V(k, 64, 128), I, U7, False, False)
-            reduce(k, 0, "W32", AB, 0, 8, False, True)
+            fetch(plan, "ru", lambda r: n0 + 8 * ((r + 1) & 15), 2048 * h, Z, c["ZW"][h])
+        marks = (lin(W(K, 0, 64), (1, W("C", 0, 64)), (1, NT)),
+                 lin(W(K, 64, 64), (1, W("C", 64, 64)), (1, NT)) + lin(W(K, 64, 56), (32, W("rl", q0 + 200, 56)))
+                 + lin(W(K, 120, 8), (32, W("rl", q0 + 192, 8))))
+        halves = (c["FIRST"][h], 1 - c["FIRST"][h])
+        if c["CPS"][h] < 2:
+            for k in halves:
+                reduce(plan[8 * k:8 * k + 8], K, 64 * k, 2048 * h + 1024 * k, marks[k])
+            return
+        its = [sums(W(K, 64 * k, 64), 144, "AB", 2048 * h + 1024 * k, 1024) for k in halves]
+        for r in runs([r for r, k in enumerate(plan) if k == "r"], 16, lambda r: 8 * r):
+            its.insert(c["CUT"][h], sums(W(K, 8 * r[0], 8 * len(r)), 288, "DD", 2048 * h + 128 * r[0], 128 * len(r)))
+        k = c["MK"][h]
+        its[k] = marks[0][1:] + marks[1][1:] + its[k]
+        its[0] = lin(W(K, 0, 128), (1, W("C", 0, 128))) + its[0]
+        for i, it in enumerate(its):
+            mms(it, start=i == 0, stop=i == len(its) - 1)
+            call("k")
 
     def turn(s, h):
         last = s == ST - 1
-        z0, q0, b0, p0 = 384 * s + ZW * h, 256 * s + 2 * R8 * h, 288 * s + 18 * BL * h, 256 * s + 2 * R8 * h
-        Z, NT, ZN, NTN = W("zl", z0, LH), W("zl", z0 + LH, R8), W("zs", z0, LH), W("zs", z0 + LH, R8)
-        M, U, T2 = W("m", R8 * h, R8), W("U", R8 * h, R8), W("t2", R8 * h, R8)
-        MD, PA, MM, SA = [W("P7", 128 * j + R8 * h, R8) for j in range(4)]
-        PLO, PHI = W("pin", pcol(s, h, 0), R8), W("pin", pcol(s, h, 1), R8)
-        KI = W("ki", 16 * h, BL)
-        s0, t0 = 2 * R8 * h, 256 * h
-        if h == 0 and (last or c["SV"]):
-            ts(PLIM, NLIM, 32.0 if c["SV"] else -1.0, ALU.mult)
-        sg = (PLIM, 1.0 / 32) if last else (NLIM, -1.0 / 32)
-        if not MP:
-            tt(MD, PHI, PLO, ALU.subtract)
-        elif h == 0:
-            tt(W("P7", 0, 128), W("pin", 256 * s + 128, 128), W("pin", 256 * s, 128), ALU.subtract)
-        if H == 1:
-            cp(V("tr", 0, 64), V("KA", 64, 128))
-            tt(V("tr", 64, 128), V("KA", 128, 192), V("tr", 0, 64), ALU.max)
-            tt(V("tr", 128, 192), V("KA", 192, 256), V("tr", 64, 128), ALU.max)
-            act(V("S", 64, 256), V("KA", 64, 256), AF.Sign, bias=sg[0], scale=sg[1])
-            tt(V("tr", 192, 256), V("KB", 0, 64), V("tr", 128, 192), ALU.max)
-            act(V("S", 0, 64), V("KB", 0, 64), AF.Sign, bias=sg[0], scale=sg[1])
-            tt(V("tr", 0, 32), V("tr", 192, 224), V("tr", 224, 256), ALU.max)
-            tt(KI, V("tr", 0, 16), V("tr", 16, 32), ALU.max)
-            kz = "KA"
+        K, P = "K%d" % h, "P%d" % h
+        q0, n0, t0 = 512 * s + 256 * h, 256 * s + 128 * h, 256 * h
+        Z, NT = W("zl", 4 * n0, 128), W("rl", q0 + 128, 64)
+        zw = c["ZW"][h] if c["ZS"] and not last else 1
+        ZN, NTN, ZH = W("zs", 4 * n0, 128 * zw), W("rs", q0 + 128, 64), W("rs", q0 + 192, 64)
+        U, M, T2, SG, DQ, DH, QA, PA, PU, YS = [t64(k, h) for k in ("U", "M", "T2", "sg", "dq", "dh", "qa", "pa", "pu", "ys")]
+        DR, MID, XS, ZB = [W(K, 128 + 64 * j, 64) for j in range(4)]
+        PAP, PBP, E, WW, E1 = [W(P, 64 * j, 64) for j in range(5)]
+        PLO, PHI, KI = W("pn", n0, 64), W("pn", n0 + 64, 64), W("ki", 8 * h, 8)
+        k = 64 * c["FIRST"][h]
+        if c["CPS"][h] == 2:
+            for b in range(8):
+                red(W("ki", 8 * h + b, 1), V(K, b, 128, 8), ALU.max)
+                call("ki")
         else:
-            kz = "KB" if h else "KA"
-            if c["CPA"]:
-                act(W("tr", t0, 64), V(kz, 64, 128), AF.Identity)
+            if c["CPS"][h]:
+                act(W("tr", t0, 64), W(K, k, 64), AF.Identity)
             else:
-                cp(W("tr", t0, 64), V(kz, 64, 128))
-            tt(W("tr", t0 + 64, 64), V(kz, 0, 64), W("tr", t0, 64), ALU.max)
-            if c["SV"]:
-                ts(W("S", s0, 128), V(kz, 0, 128), PLIM, ALU.is_gt if last else ALU.is_lt, 2.0, ALU.mult)
-            else:
-                act(W("S", s0, 128), V(kz, 0, 128), AF.Sign, bias=sg[0], scale=sg[1])
+                cp(W("tr", t0, 64), W(K, k, 64))
+            tt(W("tr", t0 + 64, 64), W(K, 64 - k, 64), W("tr", t0, 64), ALU.max)
             tt(W("tr", t0 + 128, 32), W("tr", t0 + 64, 32), W("tr", t0 + 96, 32), ALU.max)
             tt(W("tr", t0 + 160, 16), W("tr", t0 + 128, 16), W("tr", t0 + 144, 16), ALU.max)
             tt(KI, W("tr", t0 + 160, 8), W("tr", t0 + 168, 8), ALU.max)
-            cp(W(kz, 384, R8), W("B", b0 + BL, R8))
-        MID, DS, SL = W(kz, 384, R8), W(kz, 128, R8), W(kz, 192, R8)
-        mm(DS, I, W("S", s0 + R8, R8), True, False)
-        mm(DS, NI, W("S", s0, R8), False, True)
-        if c["SV"]:
-            mm(SL, I, W("S", s0, R8), True, False)
-            mm(SL, NI, W("C", 128, R8), False, True)
-        tt(U, IND(KI, L_BC), NT, ALU.subtract)
+        tt(U, IND(KI, BC), NT, ALU.subtract)
         ts(M, U, 4, ALU.arith_shift_right, 1, ALU.bitwise_and)
         ts(T2, U, 14, ALU.bitwise_and)
-        tt(MD, M, MD, ALU.mult)
+        tt(E, E, M, ALU.mult)
+        tt(PA, E, PLO, ALU.add)
+        ts(PU, PA, 2048.0, ALU.add)
+        ts(ZH, T2, 0.0, ALU.is_equal)
+        tt(YS, ZH, PA, ALU.mult)
+        YSUM, Y = W("MS", 336 + 8 * h, 8), W("y", 128 * h, 128)
+        if c["YT"][h]:
+            for n in (32, 16):
+                tt(W("ys", 64 * h, n), W("ys", 64 * h, n), W("ys", 64 * h + n, n), ALU.add)
+            if c["YT"][h] == 1:
+                YSUM = W("ys", 64 * h, 8)
+                tt(YSUM, YSUM, W("ys", 64 * h + 8, 8), ALU.add)
+        if c["YT"][h] != 1:
+            mms(lin(YSUM, *[(1, W("ys", 64 * h + 8 * r, 8)) for r in range(2 if c["YT"][h] else 8)]))
+        ts(W("yu", 8 * h, 8), YSUM, 2048.0, ALU.add)
+        if c["ZV"][h]:
+            tt(W("yd", 128 * h, 128), IND(XW, W("yu", 8 * h, 8)), Z, ALU.subtract)
+        cp(Y, IND(XW, W("yu", 8 * h, 8)))
+        if c["ZV"][h]:
+            act(ZN, W("yd", 128 * h, 128), AF.Abs)
+        elif zw > 1:
+            mms(*[lin(W("MS", 128 * j, 128), (1, Y), (-1, Z)) for j in range(zw)])
+            act(ZN, W("MS", 0, 128 * zw), AF.Abs)
+        else:
+            mms(lin(W(P, 384, 128), (1, Y), (-1, Z)))
+            act(ZN, W(P, 384, 128), AF.Abs)
+        call("z")
         ts(NTN, T2, -1.0, ALU.mult, 1.0, ALU.add)
-        tt(PA, PLO, MD, ALU.add)
-        ts(MM, M, 2.0, ALU.mult, -1.0, ALU.add)
-        cp(W("pa16", R8 * h, R8), PA)
-        for j in range(c["XV"]):
-            ts(W("ZR", 8 * j, 8), W("zl", z0, 8), 1.0, ALU.mult)
-        DH, MDQ, QA = W("B", b0 + 10 * BL, R8), W("mdq", R8 * h, R8), W("Qa", R8 * h, R8)
-        tt(MDQ, DH, MM, ALU.mult)
-        if c["SV"]:
-            tt(W("pr3", R8 * h, R8), M, DS, ALU.mult)
-            tt(SA, W("pr3", R8 * h, R8), SL, ALU.add)
-        else:
-            tt(SA, M, DS, ALU.mult)
-            tt(SA, W("S", s0, R8), SA, ALU.add)
-        tt(SA, NTN, SA, ALU.max)
-        tt(DH, MDQ, SA, ALU.mult)
-        QF = 2 * R8 * h
         if not last:
-            tt(W("qf", QF, R8), MID, DH, ALU.subtract)
-            tt(W("qf", QF + R8, R8), MID, DH, ALU.add)
-            cp(W("qs", q0, 2 * R8), W("qf", QF, 2 * R8))
-            send(W("ql", q0 + 256, 2 * R8), [W("qs", q0, 2 * R8)], "aq%d_%d" % (s + 1, h))
+            send(W("zl", 4 * n0 + 1024, 128 * c["ZW"][h]), ZN, "az%d_%d" % (s + 1, h))
         else:
-            tt(W("qf", QF, R8), MID, DH, ALU.add)
-            tt(W("qf", QF + R8, R8), MID, DH, ALU.subtract)
-        tt(QA, MDQ, MID, ALU.add)
-        k0 = 2 * R8 * h
-        tt(W("k2", k0, R8), NTN, PA, ALU.mult)
-        tt(W("k2", k0 + R8, R8 // 2), W("k2", k0, R8 // 2), W("k2", k0 + R8 // 2, R8 // 2), ALU.max)
-        tt(W("k2", k0, R8 // 4), W("k2", k0 + R8, R8 // 4), W("k2", k0 + R8 + R8 // 4, R8 // 4), ALU.max)
-        tt(W("k2", k0 + R8, BL), W("k2", k0, BL), W("k2", k0 + BL, BL), ALU.max)
-        cp(W("y16", BL * h, BL), W("k2", k0 + R8, BL))
-        Y = W("y", LH * h, LH)
-        cp(Y, IND(XW, W("y16", BL * h, BL)))
-        mm(W(kz, 256, LH), I, Y, True, False)
-        mm(W(kz, 256, LH), NI, Z, False, True)
-        act(ZN, W(kz, 256, LH), AF.Abs)
+            store(T.yz[:, 128 * h:128 * h + 128], ZN, 2.5)
+        if h or c["SC"] == 2:
+            u0, n = (8 * h, 8) if c["SC"] == 2 else (0, 16)
+            US = W("MS", 256 + u0, n)
+            mms(sums(US, 0, "y", 16 * u0, 16 * n))
+            ts(W("uh", u0, n), US, HU - 7.5, ALU.add)
+            ts(W("uh", 16 + u0, n), US, -2048.0, ALU.add)
+            mms(lin(US, (1, W("base", u0, n)), (-1, W("uh", u0, n)), (1, W("uh", 16 + u0, n))))
+            ts(W("uu", u0, n), US, 2048.0 - 256 * u0, ALU.add)
+        mms(lin(W(K, 384, 128), (1, Y), (1, Z)))
+        ts(W("avg", 128 * h, 128), W(K, 384, 128), 0.5, ALU.mult, -0.25, ALU.add)
+        SA, SB, k = W("ab", 128 * h, 64), W("ab", 128 * h + 64, 64), -1 if last else 1
+        e = 1 if c["SGN"][h] else 2
+        if c["SGN"][h]:
+            act(W("ab", 128 * h, 128), W(K, 0, 128), AF.Sign, THR)
+        else:
+            ts(W("ab", 128 * h, 128), W(K, 0, 128), NTH, ALU.is_ge, -0.5, ALU.add)
+        mms(lin(ZB, (e, SA), (-e, SB)))
+        ts(SG, M, -0.5, ALU.add)
+        tt(t64("w", h), ZB, M, ALU.mult)
+        tt(DQ, DR, SG, ALU.mult)
+        mms(lin(XS, (-k * e, SA), (k, t64("w", h))))
+        tt(XS, XS, NTN, ALU.max)
+        tt(QA, MID, DQ, ALU.add)
+        tt(DH, XS, DQ, ALU.mult)
+        tt(W("rs", q0, 64), MID, DH, ALU.add if last else ALU.subtract)
+        tt(W("rs", q0 + 64, 64), MID, DH, ALU.subtract if last else ALU.add)
         if not last:
-            send(W("zl", z0 + 384, ZW), [W("zs", z0, ZW)], "az%d_%d" % (s + 1, h))
-            if s == 0:
-                send(W("B", b0 + 288 + 9 * BL, R8), [W("B", b0 + 10 * BL, R8)], "ad%d_%d" % (s + 1, h))
-            elif h == H - 1:
-                send(W("B", 288 * s + 288, 288 - BL), [W("B", 288 * s + BL, 288 - BL)], "ad%d_%d" % (s + 1, h))
+            if c["RU"]:
+                ts(W("rv", n0, 128), W("rs", q0, 128), 2048.0, ALU.add)
+                send(W("ru", n0 + 256, 128), W("rv", n0, 128), "au%d_%d" % (s + 1, h))
+            send(W("rl", q0 + 512, 256), W("rs", q0, 256), "ar%d_%d" % (s + 1, h))
+        mms(lin(PAP, (1, PA)), lin(PBP, (1, PLO), (1, PHI), (-1, PA)))
+        if c["PV"] & 1:
+            tt(E1, PBP, PA, ALU.subtract)
         else:
-            store(T.yz[:, LH * h:LH * h + LH], ZN, 2.5)
-        mm(W("P6", 256 + LH * h, LH), I, Y, True, False)
-        mm(W("P6", 256 + LH * h, LH), I, Z, False, True)
-        if h == H - 1:
-            for a in range(16):
-                mm(W("P6", 128, 16), V("W1", 16 - a, 144 - a), V("y", a, 256, 16), a == 0, a == 15)
-            cp(W("ui", 0, 16), W("P6", 128, 16))
-            ts(W("avg", 0, 256), W("P6", 256, 256), 0.5, ALU.mult, -0.25, ALU.add)
-            ts(V("ui", 16, 32), V("ui", 0, 16), 15, ALU.bitwise_and)
-            tt(V("uf", 0, 16), V("ui", 16, 32), V("base", 0, 16), ALU.add)
-            cp(V("u16", 0, 16), V("uf", 0, 16))
-            remake(s, list(range(H)))
-        if last:
-            ts(W("uf", 16 + BL * h, BL), W("t2", R8 * h, BL), LH / 2.0, ALU.mult)
+            mms(lin(E1, (1, PLO), (1, PHI), (-2, PA)))
+        if not c["PV"] & 2:
+            mms(lin(E, (1, PLO), (1, PHI), (-1, PA), (1, W("C", 192, 64))))
+        mms(lin(WW, (2080, PA), (2048, QA), (2, AT)))
+        tt(t64("p1", h), PAP, QA, ALU.mult)
+        tt(t64("p2", h), WW, t64("p1", h), ALU.add)
+        ts(t64("rem", h), t64("p2", h), 5, ALU.arith_shift_right, 4095, ALU.bitwise_and)
+        if c["PV"] & 2:
+            ts(t64("rc", h), t64("rem", h), -2048.0, ALU.add)
+            tt(WW, t64("rc", h), PBP, ALU.subtract)
+        else:
+            tt(WW, t64("rem", h), E, ALU.subtract)
 
     def sums_f(s, h):
-        xf = c["XFL" if s == ST - 1 else "XF"][h]
-        Y, AFB, PL = W("y", LH * h, LH), ("AF", 8 * LH * h), ("pa16", R8 * h, 0)
-        plain(list(range(8 - xf)), PL, 2048 + 8 * LH * h, AFB, Y)
-        if xf:
-            fused(list(range(8 - xf, 8)), PL, 16 * LH * h, AFB, Y, False)
-        for r in groups(list(range(8)), CH):
-            reduce(fbank(h)[0], fbank(h)[1] + BL * r[0], "W1", AFB, r[0], len(r), True, True)
+        plan = c["F" if s < ST - 1 else "FL"][h]
+        fetch(plan, "pu", lambda r: 64 * h + 8 * r, 4096 + 1024 * h, W("y", 128 * h, 128))
+        reduce(plan, "P%d" % h, 320, 4096 + 1024 * h, [])
+
+    def left(s, h):
+        P, n0 = "P%d" % h, 256 * s + 128 * h
+        PAP, PBP, E, WW, E1, FK = [W(P, 64 * j, 64) for j in range(6)]
+        LC, F1, F2 = t64("lc", h), W("f", 128 * h, 64), W("f", 128 * h + 64, 64)
+        if c["SGN"] == (1, 1):
+            ts(LC, FK, THR, ALU.add, 0.0, ALU.is_lt)
+        else:
+            ts(LC, FK, NTH, ALU.is_lt)
+        tt(F1, E1, LC, ALU.mult)
+        tt(F2, WW, LC, ALU.mult)
+        tt(W("ps", n0, 64), PAP, F1, ALU.add)
+        tt(W("ps", n0 + 64, 64), PBP, F2, ALU.add)
+        if s < ST - 1:
+            send(W("pn", n0 + 256, 128), W("ps", n0, 128), "ap%d_%d" % (s + 1, h))
+
+    def limits():
+        CNT = W("MS", 272, 64)
+        mms([(CNT, BO, t64("lc", 0)), (CNT, BO, t64("lc", 1))])
+        red(A, CNT, ALU.add)
+        ts(HH, A, HA - 496, ALU.add)
+        if 1 in c["SGN"]:
+            ts(THR, A, HH, ALU.subtract, CF, ALU.add)
+        if 0 in c["SGN"]:
+            ts(NTH, HH, A, ALU.subtract, CF, ALU.subtract)
+        ts(AT, HALF, A, ALU.mult, -32768.0, ALU.add)
+
+    def names_out(x, bank, h, o):
+        for i in range(3):
+            n, m0, y, b0 = 8 << i, 1536 * (o // 256) + 768 * h + 256 * i, 128 * (i & 1), 384 * h + 128 * i
+            for k in (0, 64):
+                tt(W("rm", m0 + k, 64), W(bank, 128 - y + k, 64) if i else W(x[0], x[1] + k, 64), W("bit", b0, 64), ALU.mult)
+            if i:
+                for k in (0, 64):
+                    tt(W("rm", m0 + 128 + k, 64), W(bank, 128 - y + k, 64), W("bit", b0 + 64, 64), ALU.mult)
+                it = lin(W(bank, y, 128), (1, W("rm", m0 + 128, 128)))
+            else:
+                it = lin(W(bank, y, 128), (1, x), (-1, W("rm", m0, 128)))
+            for k in (0, 64):
+                it += lin(W(bank, y + k + n, 64 - n), (1, W("rm", m0 + k, 64 - n)))
+                it += lin(W(bank, y + k, n), (1, W("rm", m0 + k + 64 - n, n)))
+            mms(it)
+        a, st = W("h1", o + 128 * h, 128), stage()
+        cp(a, W(bank, 0, 128))
+        it = lin(W("S", st, 128), (1, W("C", 192, 128)))
+        for k in range(8):
+            for g1 in range(2):
+                it.append((W("S", st + 32 * (k >> 1) + 16 * g1, 16), sel(g1, k & 1, a), V("h1", a[1] + k, a[2], 8)))
+        mms(it)
+        tr32(W("fin", o + 128 * h, 128), W("S", st, 128))
+
+    def names_turned(x, bank, h, o):
+        a, b, v0 = W("h1", o + 128 * h, 128), W("h2", o + 128 * h, 128), 8 * o + 1024 * h
+        it = lin(W(bank, 0, 128), (1, W("C", 192, 128)))
+        for k in range(8):
+            for g1 in range(2):
+                it.append((W(bank, 32 * (k >> 1) + 16 * g1, 16), sel(g1, k & 1, x), V(x[0], x[1] + k, x[2], 8)))
+        mms(it)
+        ts(a, W(bank, 0, 128), -2048.0, ALU.add)
+        tr32(b, a)
+        for k in (0, 4):
+            st = stage()
+            mms(*[[(W("S", st + 128 * j, 128), wt(1, b, 0.0, 16 + k + j), b)] for j in range(4)])
+            if c["EV"][2 * (o // 256) + h] > k:
+                cp(W("var", v0 + 128 * k, 512), W("S", st, 512))
+            else:
+                act(W("var", v0 + 128 * k, 512), W("S", st, 512), AF.Identity)
+        act(W("fin", o + 128 * h, 128), IND(W("var", v0, 1024), W("tu", 8 * h, 8)), AF.Identity, 2048.0)
+
+    def finish(k):
+        h = int(k[1])
+        enter(ST - 1, k)
+        if k[0] == "r":
+            ts(W("tf", 8 * h, 8), W("T2", 64 * h, 8), 64.0, ALU.mult, c1(11), ALU.add)
+            tt(W("tf", 8 * h, 8), W("tf", 8 * h, 8), W("tf", 16, 8), ALU.add)
+            cp(W("tu", 8 * h, 8), W("tf", 8 * h, 8))
+            names_turned(W("rs", 512 * (ST - 1) + 256 * h, 128), "K%d" % h, h, 0)
+            store(T.yr[:, 128 * h:128 * h + 128], W("fin", 128 * h, 128), 2.6)
+        else:
+            left(ST - 1, h)
+            names_turned(W("ps", 256 * (ST - 1) + 128 * h, 128), "P%d" % h, h, 256)
+            store(T.yp[:, 128 * h:128 * h + 128], W("fin", 256 + 128 * h, 128), 2.6)
 
     for s in range(ST):
-        for h in range(H):
+        last = s == ST - 1
+        for h in range(2):
+            enter(s, "d%d" % h)
             sums_d(s, h)
-        for h in range(H):
+        for h in range(2):
+            enter(s, "t%d" % h)
             turn(s, h)
+            for k in c["END"].split()[:c["END"].split().index("f1")] if last and h else ():
+                finish(k)
+            enter(s, "f%d" % h)
             sums_f(s, h)
-        cp(IND(XW, V("u16", 0, 16)), V("avg", 0, 256))
-        if s == ST - 1:
-            store(T.yx[:], XW, 6.5)
+        enter(s, "x")
+        XO = V("X2", 0, 4096) if last and c["X2"] else XW
+        if c["SC"] == 1:
+            cp(IND(XO, W("uu", 0, 16)), W("avg", 0, 256))
+        for h in range(2 if c["SC"] == 2 else 0):
+            cp(IND(W(XO[0], 2048 * h, 2048), W("uu", 8 * h, 8)), W("avg", 128 * h, 128))
+        if s == ST - 2 and c["X2"]:
+            load("sp", V("X2", 0, 4096), XW, "l2", 6.5, [XW])
+        if last:
+            for h in range(2):
+                store(T.yx[:, 2048 * h:2048 * h + 2048], W(XO[0], 2048 * h, 2048), 4.4)
+            enter(s, "e")
             break
-        for h in range(1 if MP else H):
-            left_tail(s, h)
+        for h in range(2):
+            left(s, h)
         limits()
 
-    def finish(src, lst, w1, w2, o, four, h, dup_v, evac_v):
-        d = IND(V(src, 0, 256), W("lst", lst[1] + 2 * BL * h, 2 * BL))
-        if dup_v:
-            cp(W(w1, 2 * LH * h, 2 * LH), d)
-        else:
-            act(W(w1, 2 * LH * h, 2 * LH), d, AF.Identity)
-        tr32(W(w2, 2 * LH * h, 2 * LH), W(w1, 2 * LH * h, 2 * LH))
-        ts(W("h16", o + LH * h, LH), IND(W(w2, 2 * LH * h, 2 * LH), W("lst", L_ECP[1], BL)), -2048.0, ALU.add)
-        s = 0
-        for (b, n), on_v in zip(four, evac_v):
-            for j in range(n // LH):
-                mm(W(b, LH * j, LH), W("ROT", 128 * (s + j), 128), W("h16", o + LH * h, LH), True, True)
-            if on_v:
-                cp(W("var", 8 * o + 8 * LH * h + LH * s, n), W(b, 0, n))
-            else:
-                act(W("var", 8 * o + 8 * LH * h + LH * s, n), W(b, 0, n), AF.Identity)
-            s += n // LH
-
-    tt(V("uf", 32, 48), V("uf", 16, 32), V("base", 16, 32), ALU.add)
-    cp(V("u16", 16, 32), V("uf", 32, 48))
-    fin = c["FIN"]
-    for h in range(H):
-        finish("qf", L_EDUP, "wa", "wb", 0, [(banks[h], 1024)], h, fin[0], [0])
-    act(V("fin", 0, 256), IND(V("var", 0, 2048), V("u16", 16, 32)), AF.Identity, bias=2048.0)
-    store(T.yr[:], V("fin", 0, 256), 2.7)
-    for h in range(1 if MP else H):
-        left_tail(ST - 1, h)
-    for h in range(H):
-        finish("pf", L_PDUP, "wc", "wd", 256, [("KB", 512), ("P6", 512)] if h else [("S0", 1024)], h, fin[1 + h], [1, 0] if h else fin[3:4])
-    for h in range(H):
-        o, v = W("fin", 256 + LH * h, LH), IND(W("var", 2048, 8 * LH * (h + 1)), W("u16", 16 + BL * h, BL))
-        if h == H - 1:
-            ts(o, v, 2048.0, ALU.add)
-        else:
-            act(o, v, AF.Identity, bias=2048.0)
-    store(T.yp[:], V("fin", 256, 512), 2.7)
-    return ops, nstore[0], nsent[0]
+    for k in c["END"].split()[c["END"].split().index("f1") + 1:]:
+        finish(k)
+    for h in range(0 if c["FIN"] else 2):
+        for i in range(3):
+            b0 = 384 * h + 128 * i
+            ts(W("bit", b0, 64), IND(W("T2", 64 * h, 8), BC), i + 1, ALU.arith_shift_right, 1, ALU.bitwise_and)
+            if i:
+                ts(W("bit", b0 + 64, 64), W("bit", b0, 64), 0.0, ALU.is_equal)
+        names_out(W("rs", 512 * (ST - 1) + 256 * h, 128), "K%d" % h, h, 0)
+        store(T.yr[:, 128 * h:128 * h + 128], W("fin", 128 * h, 128), 2.6)
+    for h in range(0 if c["FIN"] else 2):
+        left(ST - 1, h)
+        names_out(W("ps", 256 * (ST - 1) + 128 * h, 128), "P%d" % h, h, 256)
+        store(T.yp[:, 128 * h:128 * h + 128], W("fin", 256 + 128 * h, 128), 2.6)
+    k = ops.index("head")
+    return ops[:k] + head + ops[k + 1:], nstore[0], nsent[0]
 
 
 def conflicts(ops):
     hist, out = {}, []
     for n, o in enumerate(ops):
-        q, deps = o[0], set()
-        if q == "far":
+        deps = set()
+        if o[0] == "far":
             deps.add(n - 1)
         else:
-            for acc, is_w in [(v, False) for v in o[2]] + [(v, True) for v in o[3]]:
-                for (k, a, b, w) in hist.get(acc[0], []):
-                    if acc[0] in PSUM and (ops[k][0] != q or q == "pe"):
+            for v, m in o[2]:
+                for (k, a, b, w) in hist.get(v[0], []):
+                    if a < v[2] and v[1] < b and (w != m or m == "w") and ops[k][3] != "":
                         deps.add(k)
-                    elif (w or is_w) and a < acc[2] and acc[1] < b and ops[k][4] != "":
-                        deps.add(k)
+        deps.discard(n)
         out.append(deps)
-        for v in o[3]:
-            keep = [e for e in hist.get(v[0], []) if not (v[3] == 1 and v[1] <= e[1] and e[2] <= v[2])]
-            hist[v[0]] = keep
-        for v in o[2]:
-            hist.setdefault(v[0], []).append((n, v[1], v[2], False))
-        for v in o[3]:
-            hist.setdefault(v[0], []).append((n, v[1], v[2], True))
+        for v, m in o[2]:
+            if m == "w" and v[3] == 1:
+                hist[v[0]] = [e for e in hist.get(v[0], []) if not (v[1] <= e[1] and e[2] <= v[2])]
+        for v, m in o[2]:
+            hist.setdefault(v[0], []).append((n, v[1], v[2], m))
+    above = []
+    for n, deps in enumerate(out):
+        far = 0
+        for k in deps:
+            far |= above[k]
+        above.append(far | sum(1 << k for k in deps))
+        out[n] = {k for k in deps if not far >> k & 1}
     return out
 
 
-def reads_from(ops, k, j):
-    if ops[k][0] != ops[j][0] or ops[k][4] is not None:
-        return True
-    return any(a[0] == b[0] and a[1] < b[2] and b[1] < a[2] for a in ops[k][3] for b in ops[j][2])
+def with_banks(ops, deps, order):
+    seen, out = {}, [None] * len(ops)
+    for j in order:
+        d = set(deps[j])
+        for b in ops[j][6]:
+            s = seen.setdefault(b, {})
+            d.update(k for q, k in s.items() if q != ops[j][0])
+            s[ops[j][0]] = j
+        out[j] = d
+    return out
 
 
 def figures(g, T):
     out, keep = [], dict(CFG)
     for m in keep["models"]:
         CFG.update(m)
-        out.append(([o[6] for o in build(g, T, (0, 0), 0, 0)[0]], CFG["far"], CFG["wake"] - keep["wake"]))
+        out.append(([o[5] for o in build(g, T, (0, 0), 0, 0)[0]], CFG["far"], CFG["wake"]))
         CFG.update(keep)
     return out
+
+
+def replay(ops, deps, order, d, far, wake):
+    free, seen, start, end, why = {}, {}, [0.0] * len(ops), [0.0] * len(ops), [None] * len(ops)
+    for j in order:
+        q = ops[j][0]
+        t, w = free.get(q, (0.0, None))
+        for k in deps[j]:
+            p = ops[k][0]
+            x = end[k] + ((0.0 if q == "pe" else wake + 0.1) if p == "pe" else 0.0 if q == "far" else wake)
+            if x > t:
+                t, w = x, k
+        for b in ops[j][6]:
+            s = seen.setdefault(b, {})
+            for p, k in s.items():
+                if p != q:
+                    x = end[k] + wake + (0.1 if p == "pe" else 0.0)
+                    if x > t:
+                        t, w = x, k
+            s[q] = j
+        start[j], end[j], why[j] = t, t + d[j], w
+        free[q] = (t + (d[j] - far if q == "far" else 0.05 if q == "sp" or q == "act" and ops[j][3] else d[j]), j)
+    return start, end, why
 
 
 def plan(ops, deps, others):
@@ -623,82 +722,243 @@ def plan(ops, deps, others):
             kids[k].append(j)
 
     def gap(k, j):
-        if c["SOFT"] and not reads_from(ops, k, j):
-            return 0.0
         if ops[k][0] == "pe":
             return 0.0 if ops[j][0] == "pe" else c["wake"] + 0.1
         return 0.0 if ops[j][0] == "far" else c["wake"]
-    dur = [o[6] for o in ops]
-    hold = [0.05 if o[4] is not None and o[0] in ("sp", "act") else o[6] - c["far"] if o[0] == "far" else o[6] for o in ops]
+    dur = [o[5] for o in ops]
+    hold = [0.05 if o[3] is not None and o[0] in ("sp", "act") else o[5] - c["far"] if o[0] == "far" else o[5] for o in ops]
+    lag = [c["wake"] + (0.1 if o[0] == "pe" else 0.0) for o in ops]
     pre = [[(k, gap(k, j)) for k in deps[j]] for j in range(n)]
     post = [[(k, gap(j, k)) for k in kids[j]] for j in range(n)]
+    named = {}
+    for j, o in enumerate(ops):
+        named.setdefault(o[7][:2], []).append(j)
+    for names in c["order"]:
+        seq = [j for s in range(ST + 1) for k in names.split() for j in named.get((s - (k[0] == "-"), k.lstrip("-")), [])]
+        for i, j in zip(seq, seq[1:]):
+            pre[j].append((i, 0.0))
+            post[i].append((j, 0.0))
+    topo, left = [j for j in range(n) if not pre[j]], [len(p) for p in pre]
+    for j in topo:
+        for k, _ in post[j]:
+            left[k] -= 1
+            if not left[k]:
+                topo.append(k)
+    assert len(topo) == n
 
     def place(seq, back):
-        busy, start = {}, [0.0] * n
+        busy, used, start = {}, {}, [0.0] * n
         for j in seq:
             if back:
                 t = max([start[k] + hold[k] + d for k, d in post[j]] + [0.0]) + dur[j] - hold[j]
             else:
                 t = max([start[k] + dur[k] + d for k, d in pre[j]] + [0.0])
-            if hold[j]:
-                l = busy.setdefault(ops[j][0], [])
+            q, h = ops[j][0], hold[j]
+            l = busy.setdefault(q, [])
+            while True:
                 i = len(l)
                 while i > 0 and l[i - 1][1] > t + 1e-9:
                     i -= 1
-                while i < len(l) and l[i][0] < t + hold[j] - 1e-9:
+                while i < len(l) and l[i][0] < t + h - 1e-9:
                     t = max(t, l[i][1])
                     i += 1
-                l.insert(i, (t, t + hold[j]))
+                t0 = t
+                for b in ops[j][6]:
+                    for (x, y, p) in used.get(b, ())[-24:]:
+                        if ops[p][0] != q:
+                            before, after = (lag[p], lag[j]) if back else (lag[j], lag[p])
+                            if x < t + h + before - 1e-9 and t < y + after - 1e-9:
+                                t = y + after
+                if t == t0:
+                    break
+            l.insert(i, (t, t + h))
+            for b in ops[j][6]:
+                used.setdefault(b, []).append((t, t + h, j))
             start[j] = t
         return start
-    prio = [0.0] * n
-    for j in range(n - 1, -1, -1):
-        prio[j] = dur[j] + max([prio[k] + d for k, d in post[j]] + [0.0])
-    start = place(sorted(range(n), key=lambda j: (-prio[j], j)), False)
-    best = (max(start[j] + dur[j] for j in range(n)), start)
-    for _ in range(c["rounds"]):
-        late = place(sorted(range(n), key=lambda j: (-start[j] - dur[j], -j)), True)
-        start = place(sorted(range(n), key=lambda j: (-late[j] - hold[j], j)), False)
-        span = max(start[j] + dur[j] for j in range(n))
-        if span < best[0]:
-            best = (span, start)
 
     def spans(start):
         seq = sorted(range(n), key=lambda j: (start[j], j))
-        out = []
-        for d, far, wake in others:
-            free, end = {}, [0.0] * n
-            for j in seq:
-                q = ops[j][0]
-                t = free.get(q, 0.0)
-                for k, x in pre[j]:
-                    x = end[k] + (x + wake if x else 0.0)
-                    if x > t:
-                        t = x
-                end[j] = t + d[j]
-                free[q] = t + (d[j] - far if q == "far" else d[j] if hold[j] == dur[j] else hold[j])
-            out.append(max(end))
-        return out
-    base = spans(best[1])
-    best = (float(len(base)), best[1])
-    x = np.arange(n, dtype=np.int64) * 7919 + c["seed"]
-    for it in range(c["search"]):
-        x = (x * 1103515245 + 12345) % 2147483648
-        mid = (int(x[0]) % 1000) * best[1][-1] / 1000
-        amp = c["jit"] * (0.2 + (int(x[1]) % 100) / 100)
-        key = [s + (amp * float(r) if abs(s - mid) < c["win"] else 0.5 * amp) for s, r in zip(best[1], (x >> 8) / 8388608.0)]
-        for j in range(n):
+        return [max(replay(ops, deps, seq, d, far, wake)[1]) for d, far, wake in others]
+    prio = [0.0] * n
+    for j in reversed(topo):
+        prio[j] = dur[j] + max([prio[k] + d for k, d in post[j]] + [0.0])
+
+    span = max(prio)
+    for j in range(n):
+        if dur[j] < c["short"] and ops[j][0] in ("dve", "pe"):
+            prio[j] += c["bonus"]
+
+    def settle(key):
+        for j in topo:
             for k, _ in pre[j]:
                 if key[k] >= key[j]:
                     key[j] = key[k] + 1e-6
-        start = place(sorted(range(n), key=lambda j: (key[j], j)), False)
-        now = spans(start)
-        score = sum(a / b for a, b in zip(now, base))
+        return place(sorted(range(n), key=lambda j: (key[j], j)), False)
+    def pull(key):
+        for j in reversed(topo):
+            for k, _ in post[j]:
+                if key[j] > key[k] - dur[j]:
+                    key[j] = key[k] - dur[j]
+        return settle(key)
+    start = pull([-prio[j] for j in range(n)])
+    base = spans(start)
+    best = (float(len(base)), start)
+    lead, keep, x = {}, {}, 777 + c["seed"]
+    for it in range(c["blame"]):
+        seq = sorted(range(n), key=lambda j: (start[j], j))
+        runs = [replay(ops, deps, seq, d, far, wake) for d, far, wake in others]
+        score = sum(max(r[1]) / b for r, b in zip(runs, base))
+        if score < best[0]:
+            best, keep = (score, start), dict(lead)
+        elif it % c["back"] == 0:
+            lead = dict(keep)
+        x = (x * 1103515245 + 12345) % 2147483648
+        t0, end, why = runs[(x >> 8) % len(runs)]
+        j, late = max(range(n), key=lambda j: end[j]), {}
+        while why[j] is not None:
+            if why[j] not in deps[j]:
+                late[ops[j][7][1:]] = (j, why[j])
+            j = why[j]
+        late = list(late.values())
+        for _ in range(1 + (x >> 20) % 3):
+            x = (x * 1103515245 + 12345) % 2147483648
+            j, i = late[(x >> 8) % len(late)]
+            k, d = (ops[j][7][1:], 1) if (x >> 6) % 2 else (ops[i][7][1:], -1)
+            lead[k] = lead.get(k, 0.0) + d * c["step"] * ((x >> 16) % 16 + 1) / 8
+        start = pull([-prio[j] - lead.get(ops[j][7][1:], 0.0) for j in range(n)])
+    start = best[1]
+    for _ in range(c["rounds"]):
+        late = place(sorted(range(n), key=lambda j: (-start[j] - dur[j], -j)), True)
+        start = place(sorted(range(n), key=lambda j: (-late[j] - hold[j], j)), False)
+        score = sum(a / b for a, b in zip(spans(start), base))
+        if score < best[0]:
+            best = (score, start)
+    first, cur = spans(best[1]), best
+    tags = {}
+    tag = np.array([tags.setdefault(o[7][1:], len(tags)) for o in ops])
+    model = [j for j in range(n) if ops[j][7][0] == 2]
+    x = np.arange(n, dtype=np.int64) * 7919 + c["seed"]
+    for it in range(c["search"]):
+        x = (x * 1103515245 + 12345) % 2147483648
+        amp = c["jit"] * (0.2 + (int(x[1]) % 100) / 100)
+        now, r = np.array(cur[1]), (x >> 8) / 8388608.0 - 0.5
+        if it % 3 == 2:
+            key = now + amp * r * (abs(now - now[int(x[0] >> 4) % n]) < c["win"])
+        else:
+            mid, hit = now[model[int(x[0] >> 4) % len(model)]], np.zeros(n)
+            for j in model:
+                hit[tag[j]] = abs(now[j] - mid) < c["win"]
+            key = now + amp * (r * hit)[tag]
+        start = settle(list(key))
+        score = sum(a / b for a, b in zip(spans(start), base))
+        if score <= cur[0] + c["heat"] * (1 - it / c["search"]) * (int(x[2] >> 8) % 100) / 100:
+            cur = (score, start)
         if score <= best[0]:
             best = (score, start)
-    c["span"] = [round(v, 1) for v in base + spans(best[1])]
-    loads = [j for j in range(n) if ops[j][4] and ops[j][0] != "far"]
-    return loads + sorted(set(range(n)) - set(loads), key=lambda j: (best[1][j], j))
+    loads = [j for j in range(n) if ops[j][3] and ops[j][0] != "far" and not deps[j]]
+    order = loads + sorted(set(range(n)) - set(loads), key=lambda j: (best[1][j], j))
+
+    same = {o[7]: j for j, o in enumerate(ops)}
+
+    qs = [o[0] for o in ops]
+    fast = []
+    for d, far, wake in others:
+        lagm = [wake + (0.1 if q == "pe" else 0.0) for q in qs]
+        fast.append((d, [d[j] - far if qs[j] == "far" else hold[j] if hold[j] != dur[j] else d[j] for j in range(n)], lagm,
+                     [[(k, 0.0 if qs[j] == "far" or qs[j] == qs[k] == "pe" else lagm[k]) for k in deps[j]] for j in range(n)]))
+
+    def judge(seq):
+        free, seen, links = {}, {}, []
+        for j in seq:
+            q, other = qs[j], ()
+            if ops[j][6]:
+                other = []
+                for b in ops[j][6]:
+                    s = seen.setdefault(b, {})
+                    other += [k for p, k in s.items() if p != q]
+                    s[q] = j
+            links.append((j, free.get(q), other))
+            free[q] = j
+        runs = []
+        for d, hd, lagm, before in fast:
+            start, end, why = [0.0] * n, [0.0] * n, [None] * n
+            for j, w, other in links:
+                t = 0.0 if w is None else start[w] + hd[w]
+                for k, x in before[j]:
+                    x += end[k]
+                    if x > t:
+                        t, w = x, k
+                for k in other:
+                    x = end[k] + lagm[k]
+                    if x > t:
+                        t, w = x, k
+                start[j], end[j], why[j] = t, t + d[j], w
+            runs.append((start, end, why))
+        return sum((max(r[1]) + c["mean"] * sum(r[1]) / n) / b for r, b in zip(runs, base)), runs
+
+    def moved(seq, i, j, way):
+        seq, done = list(seq), False
+        steps = range(ST) if ops[i][7][0] >= 0 and way & 2 else [0]
+        for s in steps:
+            a, b = i, j
+            if len(steps) > 1:
+                a = same.get((s,) + ops[i][7][1:])
+                b = same.get((s + ops[j][7][0] - ops[i][7][0],) + ops[j][7][1:])
+                if a is None or b is None or ops[a][0] != ops[i][0] or ops[b][0] != ops[j][0]:
+                    continue
+            pa, pb = seq.index(a), seq.index(b)
+            if pa > pb:
+                continue
+            part = seq[pa:pb + 1]
+            if way & 1:
+                take = {b}
+                for k in reversed(part):
+                    if k in take:
+                        take.update(deps[k])
+                if a in take:
+                    continue
+                seq[pa:pb + 1] = [k for k in part if k in take] + [k for k in part if k not in take]
+            else:
+                take = {a}
+                for k in part:
+                    if deps[k] & take:
+                        take.add(k)
+                if b in take:
+                    continue
+                seq[pa:pb + 1] = [k for k in part if k not in take] + [k for k in part if k in take]
+            done = True
+        return seq if done else None
+    cur = (order,) + judge(order)
+    best, x = cur, 12345 + c["seed"]
+    for it in range(c["swaps"]):
+        x = (x * 1103515245 + 12345) % 2147483648
+        start, end, why = cur[2][(x >> 8) % len(others)]
+        j, pairs = max(range(n), key=lambda j: end[j]) if it % 2 else (x >> 6) % n, []
+        while why[j] is not None and (it % 2 or len(pairs) < 6):
+            if why[j] not in deps[j] and why[j] not in loads:
+                pairs.append((why[j], j))
+            j = why[j]
+        if not pairs:
+            continue
+        i, j = pairs[(x >> 12) % len(pairs)]
+        if (x >> 20) % 2 and ops[i][0] == ops[j][0]:
+            if (x >> 24) % 2:
+                ready = max([end[k] for k in deps[j]] + [0.0]) if (x >> 5) % 2 else start[j] - c["reach"]
+                can = [k for k in cur[0] if ops[k][0] == ops[j][0] and ready - 0.3 < start[k] < start[j] and k not in loads]
+                i = can[(x >> 9) % len(can)] if can else i
+            else:
+                can = [k for k in cur[0] if ops[k][0] == ops[j][0] and start[j] <= start[k] < start[j] + 1.5]
+                j = can[(x >> 9) % len(can)]
+        seq = moved(cur[0], i, j, (x >> 24) % 4 | (2 if (x >> 28) % 2 else 0))
+        if seq:
+            new = (seq,) + judge(seq)
+            if new[1] <= cur[1] + c["heat"] * (1 - it / c["swaps"]) * ((x >> 4) % 64) / 64:
+                cur = new
+                if new[1] < best[1]:
+                    best = new
+    c["span"] = [round(v, 1) for v in [span] + base + first + [max(r[1]) for r in best[2]]]
+    return best[0]
 
 
 def emit(g, T, ops, deps, order, nstore, nsent, neng):
@@ -708,7 +968,7 @@ def emit(g, T, ops, deps, order, nstore, nsent, neng):
     rank = {j: i for i, j in enumerate(order)}
     clock, waits, sig, needed = {}, {}, {}, set()
     for n in order:
-        q, sem = ops[n][0], ops[n][4]
+        q, sem = ops[n][0], ops[n][3]
         if sem:
             sig[n] = (sem, 1)
         elif sem is None:
@@ -720,7 +980,7 @@ def emit(g, T, ops, deps, order, nstore, nsent, neng):
         if q != "far":
             kn = known[q]
             for k in sorted(deps[n], key=lambda k: -rank[k]):
-                if q == "pe" and ops[k][0] == "pe" or CFG["SOFT"] and not reads_from(ops, k, n):
+                if q == "pe" and ops[k][0] == "pe":
                     continue
                 s, p = sig[k]
                 if kn.get(s, 0) >= p:
@@ -738,11 +998,11 @@ def emit(g, T, ops, deps, order, nstore, nsent, neng):
     value = {}
     for n in order:
         o = ops[n]
-        if o[4] is None and n in needed:
+        if o[3] is None and n in needed:
             count[o[0]] += 1
             value[n] = count[o[0]]
-        elif o[4]:
-            value[n] = o[5]
+        elif o[3]:
+            value[n] = o[4]
     for n in order:
         o = ops[n]
         if o[0] == "far":
@@ -750,7 +1010,7 @@ def emit(g, T, ops, deps, order, nstore, nsent, neng):
         for k in waits[n]:
             queues[o[0]].wait_ge(T.sem[sig[k][0]], value[k])
         ins = o[1]()
-        if o[4] is None and n in needed:
+        if o[3] is None and n in needed:
             ins.then_inc(T.sem[o[0]], 1)
     g.sync.wait_ge(T.sem.stored, 16 * nstore)
     g.wait_ge(T.sem.sent, neng * nsent)
@@ -763,8 +1023,8 @@ def rank_program(g, core, T, topo):
     nxt = T.cores[(rank + 1) % len(T.cores)]
     neng = len(topo.engines(core, nxt))
     ops, nstore, nsent = build(g, T, topo.addr(nxt), topo.mask(core, nxt), neng)
-    key = repr(sorted((k, v) for k, v in CFG.items() if k != "span"))
-    if key not in PLANS:
+    if not PLANS:
         deps = conflicts(ops)
-        PLANS[key] = (deps, plan(ops, deps, figures(g, T)))
-    emit(g, T, ops, PLANS[key][0], PLANS[key][1], nstore, nsent, neng)
+        order = plan(ops, deps, figures(g, T))
+        PLANS["it"] = (with_banks(ops, deps, order), order)
+    emit(g, T, ops, PLANS["it"][0], PLANS["it"][1], nstore, nsent, neng)

import numpy as np
from concourse.bass import DstId, RemoteDMATransfer
from concourse.mybir import AluOpType as ALU, ActivationFunctionType as AF, AxisListType

ST = 6
CFG = {
    "D": ("rrrrrrrrsssssssa", "ssaaaaaasssssssa"), "F": ("ssssssss", "ssssssss"),
    "D0": ("rrrrrrrrsssssssa", "ssaaaaaasssssssa"), "FL": ("ssssssss", "ssssssss"),
    "FIRST": (0, 1),
    "CPS": (2, 2),
    "GC": 4, "AC": 4, "RC": 4,
    "MIX": 1, "X2": 1, "SC": 2, "lead": {}, "YT": (0, 0), "ZV": (1, 1), "PV": 0, "CUT": (0, 1), "ZW": (1, 1), "ZS": 0, "SGN": (0, 0),
    "short": 0.16, "bonus": 0.0, "RU": 0, "MK": (0, 0), "reach": 2.0, "FIN": 1, "END": "r0 f1 p0 r1 p1", "EV": (0, 5, 1, 1),
    "order": ("-f1a1 d0g0 d0g1 d0a0 d0a1 d0b0 d1g1 d1g2 d1g0 d1a1 d1b2 d1b0 d1a2 d1a0 d1b1 f0g0 f0g1 t0z f0a0 f0a1 f1g0 f1g1 t1z f1a0",
              "d0v0 d0v1 d0v2 d0v3 d0v4 d0v5 d0v6 d0v7 d0c0 d0v15 d0c1 d1v15 d1v2 d1v3 d1v4 t0ki d1v5 t0U d1v6 t0M d1v7",
              "d0s0 d0s1 d0k d1s1 d1s2 d1s0 d1k", "t0pors t0pozs t1pors t1pozs", "t0uh t0uh' t0MS256' t0uu t1ys", "t0avg t1yu",
              "t1uh t1uh' t1avg xX t1uu xX'", "t1MS264 t1K1384 f1s0 t1MS264' f1s1", "t1P1192' f1P1320"), "heat": 0.0, "swaps": 13000, "blame": 300, "back": 3, "step": 0.5, "mean": 0.5,
    "g": 1.56, "sc": 3.8, "cy": 0.0009, "pe": 0.00047, "wake": 0.17, "fix": 0.005, "afix": 0.08, "far": 3.5, "issue": 0.5,
    "bw": 90e3, "row": 0.5, "rounds": 4, "seed": 4, "jit": 1.0, "win": 2.0, "search": 0,
    "models": ({"cy": 0.00083, "pe": 0.00042, "afix": 0.065, "far": 2.0, "wake": 0.15},
               {"wake": 0.2, "cy": 0.0012, "pe": 0.0006, "g": 1.8, "far": 4.5},
               {"wake": 0.15, "cy": 0.00083, "pe": 0.00042, "g": 1.56, "afix": 0.065, "far": 3.0, "issue": 1.2, "row": 1.0},
               {"wake": 0.2, "cy": 0.00083, "pe": 0.00042, "g": 1.2, "afix": 0.065, "far": 4.5}),
}

SCRATCH = {
    "X": ("sbuf", [128, 4096], "bfloat16"), "X2": ("sbuf", [128, 4096], "bfloat16"),
    "G": ("sbuf", [128, 6144], "bfloat16"), "DD": ("sbuf", [128, 6144], "bfloat16"), "AB": ("sbuf", [128, 6144], "bfloat16"),
    "zl": ("sbuf", [128, ST * 1024], "bfloat16"), "zs": ("sbuf", [128, ST * 1024], "bfloat16"),
    "rl": ("sbuf", [128, ST * 512], "float16"), "rs": ("sbuf", [128, ST * 512], "float16"),
    "var": ("sbuf", [128, 4096], "float32"), "tf": ("sbuf", [128, 24], "float32"), "tu": ("sbuf", [128, 16], "uint16"),
    "yd": ("sbuf", [128, 256], "bfloat16"), "nt": ("sbuf", [128, 64], "bfloat16"), "rc": ("sbuf", [128, 128], "float16"),
    "pn": ("sbuf", [128, ST * 256], "float16"), "ps": ("sbuf", [128, ST * 256], "float16"),
    "ru": ("sbuf", [128, ST * 256], "uint16"), "rv": ("sbuf", [128, ST * 256], "uint16"),
    "rawp": ("sbuf", [128, 256], "int32"), "rawq": ("sbuf", [128, 256], "int32"), "thi": ("sbuf", [128, 8], "int32"),
    "h1": ("sbuf", [128, 512], "float16"), "h2": ("sbuf", [128, 512], "float16"), "fin": ("sbuf", [128, 512], "float32"),
    "rm": ("sbuf", [128, 3072], "float16"), "bit": ("sbuf", [128, 768], "int32"),
    "ci": ("sbuf", [128, 32], "int32"), "cj": ("sbuf", [128, 64], "int32"), "col": ("sbuf", [128, 64], "float32"),
    "idx": ("sbuf", [128, 272], "bfloat16"), "WB": ("sbuf", [128, 32 * 128], "bfloat16"), "WH": ("sbuf", [128, 16 * 128], "float16"),
    "WF": ("sbuf", [128, 128], "float32"), "WR": ("sbuf", [128, 432], "bfloat16"),
    "C": ("sbuf", [128, 448], "bfloat16"), "lst": ("sbuf", [128, 8], "uint16"), "base": ("sbuf", [128, 16], "float16"),
    "tr": ("sbuf", [128, 512], "float32"), "ki": ("sbuf", [128, 16], "int32"), "U": ("sbuf", [128, 128], "int32"),
    "M": ("sbuf", [128, 128], "int32"), "T2": ("sbuf", [128, 128], "int32"), "sg": ("sbuf", [128, 128], "bfloat16"),
    "ab": ("sbuf", [128, 256], "bfloat16"), "dq": ("sbuf", [128, 128], "float32"), "dh": ("sbuf", [128, 128], "float32"),
    "qa": ("sbuf", [128, 128], "float16"), "pa": ("sbuf", [128, 128], "float16"), "pu": ("sbuf", [128, 128], "uint16"),
    "ys": ("sbuf", [128, 128], "float16"), "yu": ("sbuf", [128, 16], "uint16"), "y": ("sbuf", [128, 256], "bfloat16"),
    "p1": ("sbuf", [128, 128], "float32"), "p2": ("sbuf", [128, 128], "int32"), "rem": ("sbuf", [128, 128], "int32"),
    "lc": ("sbuf", [128, 128], "bfloat16"), "f": ("sbuf", [128, 256], "float32"), "avg": ("sbuf", [128, 256], "int32"),
    "uh": ("sbuf", [128, 32], "float16"), "uu": ("sbuf", [128, 16], "uint16"), "at": ("sbuf", [128, 64], "float16"),
    "lim": ("sbuf", [128, 16], "float32"), "hh": ("sbuf", [128, 8], "bfloat16"), "w": ("sbuf", [128, 128], "bfloat16"),
    "S": ("psum", [128, 1536], "float32"), "K0": ("psum", [128, 512], "float32"), "K1": ("psum", [128, 512], "float32"),
    "P0": ("psum", [128, 512], "float32"), "P1": ("psum", [128, 512], "float32"), "MS": ("psum", [128, 512], "float32"),
}
PSUM = ("S", "K0", "K1", "P0", "P1", "MS")
SEMAPHORES = (["pe", "dve", "act", "pool", "sent", "stored", "lx", "lq", "lp", "lz0", "lz1", "lt", "l2"]
              + ["%s%d_%d" % (k, s, h) for k in ("az", "ar", "ap", "au") for s in range(1, ST) for h in range(2)])
PLANS = {}
HA, HU = 132096.0, 16448.0


def V(name, a, b, step=1):
    return (name, a, b, step)


def W(name, a, n):
    return (name, a, a + n, 1)


def IND(win, off):
    return ("*", win, off)


def size(v):
    if v[0] == "*":
        return 16 * size(v[2])
    return (v[2] - v[1] + v[3] - 1) // v[3]


def kind(v):
    return SCRATCH[v[0]][2]


def two_bytes(v):
    return kind(v) in ("bfloat16", "float16", "uint16")


def banks_of(views):
    return sorted({(v[0], k) for v in views if v[0] in PSUM for k in range(v[1] // 512, (v[2] - 1) // 512 + 1)})


def build(g, T, nxt_addr, mask, neng):
    ops, head, times = [], [], {}
    c = CFG
    at = [-1, "", 0]

    def enter(s, name):
        at[:] = [s, name, 0]

    def call(name):
        ops[-1][7] = (at[0], at[1] + name, at[2])

    def ap(v):
        if v[0] == "*":
            return ap(v[1]).indirect(ap(v[2]))
        if v[3] == 1:
            return T[v[0]][:, v[1]:v[2]]
        return T[v[0]][:, v[1]:v[2]:v[3]]

    def op(q, emit, reads, writes, cost, sem=None, cnt=0, adds=(), to=None):
        acc = []
        for v in reads:
            if isinstance(v, tuple):
                acc += [(v[1], "r"), (v[2], "r")] if v[0] == "*" else [(v, "r")]
        for v in writes:
            acc += [(v[1], "w"), (v[2], "r")] if v[0] == "*" else [(v, "w")]
        acc += [(v, "a") for v in adds]
        what = ([v for v, m in acc if m == "w"] + [acc[0][0]])[0]
        name = at[1] + (q[:2] if q in ("pool", "far", "sp") else "") + what[0] + (str(what[1]) if what[0] in PSUM else "")
        times[at[0], name] = times.get((at[0], name), 0) + 1
        name += "'" * (times[at[0], name] - 1)
        (ops if to is None else to).append([q, emit, acc, sem, cnt, cost, banks_of([v for v, _ in acc]), (at[0], name, at[2])])
        at[2] += 1

    def sc(x):
        return ap(x) if isinstance(x, tuple) else x

    def vcost(o, a, k):
        if o[0] == "*":
            return 0.05 + size(o) * c["sc"] * c["cy"]
        if a[0] == "*":
            return 0.05 + size(a) * c["g"] * c["cy"]
        return c["fix"] + max(64, size(a) * k) * c["cy"]

    def half(o, a):
        return 0.5 if o[0] != "*" and a[0] != "*" and two_bytes(o) and two_bytes(a) else 1

    def tt(o, a, b, alu):
        k = 1 if a[0] in PSUM or b[0] in PSUM else 2
        op("dve", lambda: g.vector.tensor_tensor(ap(o), ap(a), ap(b), alu), [a, b], [o], vcost(o, a, k))

    def ts(o, a, s1, o1, s2=None, o2=None, to=None):
        t = vcost(o, a, half(o, a))
        if o2 is None:
            op("dve", lambda: g.vector.tensor_scalar(ap(o), ap(a), sc(s1), None, o1), [a, s1], [o], t, to=to)
        else:
            op("dve", lambda: g.vector.tensor_scalar(ap(o), ap(a), sc(s1), sc(s2), o1, o2), [a, s1, s2], [o], t, to=to)

    def cp(o, a):
        op("dve", lambda: g.vector.tensor_copy(ap(o), ap(a)), [a], [o], vcost(o, a, half(o, a)))

    def tr32(o, a):
        op("dve", lambda: g.vector.transpose(ap(o), ap(a)), [a], [o], vcost(o, a, half(o, a)))

    def red(o, a, alu):
        op("dve", lambda: g.vector.tensor_reduce(ap(o), ap(a), AxisListType.X, alu), [a], [o], vcost(o, a, 1))

    def ms(o, k):
        op("dve", lambda: g.vector.memset(ap(o), k), [], [o], vcost(o, o, half(o, o)))

    def act(o, a, f, bias=0.0):
        t = 0.065 + size(a) * c["g"] * c["cy"] if a[0] == "*" else c["afix"] + max(64, size(a)) * c["cy"]
        op("act", lambda: g.scalar.activation(ap(o), ap(a), f, bias=sc(bias)), [a, bias], [o], t)

    def mms(*groups, start=True, stop=True):
        def emit():
            for items in groups:
                for i, (o, l, r) in enumerate(items):
                    ins = g.tensor.matmul(ap(o), ap(l), ap(r), start and i == 0, stop and i == len(items) - 1)
            return ins
        every = [x for items in groups for x in items]
        mark = [("#%s%d" % banks_of([every[0][0]])[0], 0, 1, 1)]
        t = sum(max(64, size(r)) * (4 if kind(r) == "float32" else 1) for _, _, r in every) * c["pe"]
        ins = [v for _, l, r in every for v in (l, r)]
        if start and stop:
            op("pe", emit, ins + mark, [items[0][0] for items in groups], t)
        else:
            op("pe", emit, ins, [o for o, _, _ in every] + mark, t)

    def iota(o, pat, base, cm, flt=False):
        t = 0.13 + 2 * size(o) * c["cy"]
        if flt:
            op("pool", lambda: g.iota(ap(o), pat, base, cm, allow_small_or_imprecise_dtypes=True), [], [o], t)
        else:
            op("pool", lambda: g.iota(ap(o), pat, base, cm), [], [o], t)

    def load(q, o, src, sem, t, reads=()):
        op(q, lambda: (g.sync if q == "sp" else g.scalar).dma_start(ap(o), sc(src)).then_inc(T.sem[sem], 16),
           list(reads), [o], t, sem, 16)

    nstore, nsent = [0], [0]

    def store(dst, a, t):
        nstore[0] += 1
        op("sp", lambda: g.sync.dma_start(dst, ap(a)).then_inc(T.sem.stored, 16), [a], [], t, "", 0)

    def send(dst, src, sem):
        nsent[0] += 1
        n, k = size(src), size(dst) // size(src)
        if k == 1:
            op("pool", lambda: g.remote_dma(ap(dst), ap(src), T.sem[sem], T.sem.sent, nxt_addr[1], nxt_addr[0], mask),
               [src], [], c["issue"], "", 0)
        else:
            op("pool", lambda: g.remote_dma_fused([RemoteDMATransfer(
                dst_ids=[DstId(rid=nxt_addr[0], pnc=nxt_addr[1])] * k, dma_engine_mask=mask, remote_sem=T.sem[sem], src=ap(src),
                dsts=[ap(W(dst[0], dst[1] + n * j, n)) for j in range(k)])], local_sem=T.sem.sent), [src], [], c["issue"], "", 0)
        op("far", None, [], [dst], c["far"] + k * c["row"] + 256 * size(dst) / c["bw"], sem, neng * k)

    def c1(j):
        return V("col", j, j + 1)

    IDX = V("idx", 0, 128)
    made = {}

    def wt(k, like, shift=0.0, to=0):
        buf = "WF" if kind(like) == "float32" else "WH" if kind(like) == "float16" and not c["MIX"] else "WB"
        key = (buf, k, shift, to)
        if key not in made:
            made[key] = W(buf, 128 * len([x for x in made if x[0] == buf]), 128)
            keep = list(at)
            at[:] = [-1, "w", len(made)]
            if shift:
                ts(made[key], IDX, shift, ALU.add, c1(to), ALU.is_equal, to=head)
            else:
                ts(made[key], IDX, c1(to), ALU.is_equal, float(k), ALU.mult, to=head)
            at[:] = keep
        return made[key]

    def lin(o, *terms):
        return [(o, wt(k, v), v) for k, v in terms]

    XW = V("X", 0, 4096)
    BC = W("lst", 0, 4)
    A, THR, HH, AT = V("lim", 0, 1), V("lim", 8, 9), V("hh", 0, 1), V("at", 0, 64)
    CF, NTH = c1(8), V("lim", 12, 13)
    HALF, C2K = W("C", 128, 64), W("C", 192, 256)

    load("sp", V("rawq", 0, 256), T.pr[:], "lq", 2.6)
    load("sp", XW, T.xt[:], "lx", 7.0)
    load("sp", V("rawp", 0, 256), T.pl[:], "lp", 7.5)
    for h in range(2):
        load("act", W("zl", 512 * h, 128), T.z0[:, 128 * h:128 * h + 128], "lz%d" % h, 3.5)
    load("act", V("thi", 0, 1), T.th[:], "lt", 3.5)
    iota(V("cj", 0, 1), [[1, 1]], 0, 1)
    iota(V("idx", 0, 144), [[1, 144]], 0, 0, True)
    iota(V("idx", 144, 272), [[1, 8], [0, 16]], 0, 0, True)
    iota(V("ci", 0, 16), [[256, 16]], int(HU), 0)
    iota(W("nt", 0, 64), [[-2, 8], [0, 8]], 1, 0, True)
    cp(c1(0), V("cj", 0, 1))
    ts(V("cj", 8, 9), V("cj", 0, 1), 15, ALU.bitwise_and)
    ts(V("cj", 16, 17), V("cj", 0, 1), 16, ALU.bitwise_and)
    ts(V("cj", 24, 25), V("cj", 0, 1), 7, ALU.bitwise_and)
    ts(c1(1), V("cj", 16, 17), 1024.0, ALU.mult, c1(0), ALU.add)
    ts(c1(2), V("cj", 16, 17), -1024.0, ALU.mult, c1(0), ALU.add)
    ts(c1(2), c1(2), 16384.0, ALU.add)
    ts(c1(4), V("cj", 8, 9), -1.0, ALU.mult, c1(0), ALU.add)
    ts(c1(5), c1(4), 1.0 / 16, ALU.mult)
    ts(c1(6), V("cj", 8, 9), 16.0, ALU.mult)
    cp(c1(7), V("cj", 24, 25))
    ts(BC, W("idx", 0, 4), 0.0, ALU.mult, c1(7), ALU.add)
    ts(V("base", 0, 16), V("ci", 0, 16), c1(6), ALU.add)
    ts(W("WR", 0, 144), V("idx", 0, 144), -16.0, ALU.add, c1(4), ALU.is_equal)
    ts(W("WR", 144, 144), W("WR", 0, 144), -32.0, ALU.mult)
    ts(W("WR", 288, 144), W("WR", 0, 144), 32.0, ALU.mult)
    BO = W("WB", 31 * 128, 128)
    ts(BO, V("idx", 144, 272), c1(5), ALU.is_equal, 32.0, ALU.mult)
    ms(W("C", 0, 64), -2.0)
    ms(W("C", 64, 64), -18.0)
    ms(HALF, 0.5)
    ms(C2K, 2048.0)
    ts(AT, HALF, -65536.0, ALU.mult)
    ts(CF, V("thi", 0, 1), 32.0, ALU.mult, HA + 30, ALU.add)
    ts(THR, V("thi", 0, 1), 32.0, ALU.mult, 30.0, ALU.add)
    ts(NTH, V("thi", 0, 1), -32.0, ALU.mult, -30.0, ALU.add)
    for h in range(2):
        cp(W("rl", 256 * h + 128, 64), W("nt", 0, 64))
        ts(W("rl", 256 * h + 192, 64), W("nt", 0, 64), 1.0, ALU.is_equal)
        for j in range(1, c["ZW"][h]):
            cp(W("zl", 512 * h + 128 * j, 128), W("zl", 512 * h, 128))
    if c["FIN"]:
        iota(V("cj", 32, 40), [[1, 8]], 0, 1)
        cp(c1(11), V("cj", 8, 9))
        ts(W("tf", 16, 8), W("idx", 0, 8), 16.0, ALU.mult)
        ts(V("cj", 40, 48), V("cj", 32, 40), 7, ALU.bitwise_and)
        ts(c1(12), c1(7), -1.0, ALU.mult, c1(0), ALU.add)
        ts(V("col", 16, 24), V("cj", 40, 48), c1(12), ALU.add)
    ops.append("head")

    def sel(src, dst, like):
        return wt(1, like, 16.0 * (src - dst), 1 + src)

    nb = [0]

    def stage():
        nb[0] += 1
        return 512 * (nb[0] % 3)

    def names_in(raw, o, dst, wide):
        a, b, st = W("h1", o, 256), W("h2", o, 256), stage()
        ts(a, V(raw, 0, 256), -2048.0, ALU.add)
        tr32(b, a)
        it = lin(W("S", st, 256), (1, C2K))
        for h in range(2):
            for k in range(8):
                for g1 in range(2):
                    it.append((V("S", st + 128 * h + k, st + 128 * h + 128, 8), sel(k & 1, g1, b),
                               W("h2", o + 128 * h + 32 * (k >> 1) + 16 * g1, 16)))
        mms(it)
        for h in range(2):
            ts(W(dst, wide * h, 128), W("S", st + 128 * h, 128), -2048.0, ALU.add)

    names_in("rawq", 0, "rl", 256)
    names_in("rawp", 256, "pn", 128)

    def runs(rows, n, col):
        out = []
        for r in rows:
            if out and out[-1][-1] + 1 == r and len(out[-1]) < n and col(out[-1][-1]) + 8 == col(r):
                out[-1].append(r)
            else:
                out.append([r])
        return out

    def fetch(plan, names, col, d0, sub, wide=1):
        srows = [r for r, k in enumerate(plan) if k == "s"]
        for i, r in enumerate(runs(srows, c["GC"], col)):
            act(W("G", d0 + 128 * r[0], 128 * len(r)), IND(XW, W(names, col(r[0]), 8 * len(r))), AF.Identity)
            call("g%d" % i)
        for i, r in enumerate(runs(srows, 4, lambda r: 8 * r)):
            st, n = stage(), 128 * len(r)
            it = lin(W("S", st, n), (1, W("G", d0 + 128 * r[0], n)))
            for j in range(len(r)):
                it += lin(W("S", st + 128 * j, 128), (-1, sub))
            mms(it)
            call("s%d" % i)
            act(W("AB", d0 + 128 * r[0], n), W("S", st, n), AF.Abs)
            call("a%d" % i)
        def fused(rows, name):
            for k in runs(rows, wide, col):
                n = len(k)
                tt(W("DD", d0 + 128 * k[0], 128 * n), IND(XW, W(names, col(k[0]), 8 * n)), W(sub[0], sub[1], 128 * n), ALU.subtract)
                call("v%d" % k[0])
        for i, r in enumerate(runs([r for r, k in enumerate(plan) if k == "a"], c["AC"], lambda r: 8 * r)):
            fused(r, "u%d" % i)
            act(W("AB", d0 + 128 * r[0], 128 * len(r)), W("DD", d0 + 128 * r[0], 128 * len(r)), AF.Abs)
            call("b%d" % i)
        for i, r in enumerate(runs([r for r, k in enumerate(plan) if k == "r"], c["RC"], lambda r: 8 * r)):
            fused(r, "v%d" % i)
            ts(W("AB", d0 + 128 * r[0], 128 * len(r)), W("DD", d0 + 128 * r[0], 128 * len(r)), 0.0, ALU.max, 2.0, ALU.mult)
            call("c%d" % i)

    def sums(o, w, buf, a0, n):
        return [(o, W("WR", w + 16 - a, 128), V(buf, a0 + a, a0 + n, 16)) for a in range(16)]

    def reduce(plan, bank, k0, d0, first):
        cut = []
        for r in runs([r for r, k in enumerate(plan) if k == "r"], 8, lambda r: 8 * r):
            cut += sums(W(bank, k0 + 8 * r[0], 8 * len(r)), 288, "DD", d0 + 128 * r[0], 128 * len(r))
        rest = sums(W(bank, k0, 64), 144, "AB", d0, 1024)
        if first and cut:
            mms(first + cut, stop=False)
            mms(rest, start=False)
        else:
            mms(first + rest + cut)

    def t64(name, h):
        return W(name, 64 * h, 64)

    def sums_d(s, h):
        K, P = "K%d" % h, "P%d" % h
        q0, n0 = 512 * s + 256 * h, 256 * s + 128 * h
        Z, NT = W("zl", 4 * n0, 128), W("rl", q0 + 128, 64)
        if s == 0 or not c["RU"]:
            ts(W("ru", n0, 128), W("rl", q0, 128), 2048.0, ALU.add)
        r1, r0, r9, r8 = W("rl", q0 + 8, 56), W("rl", q0, 8), W("rl", q0 + 72, 56), W("rl", q0 + 64, 8)
        k = -1 if s == 0 else 1
        mms(lin(W(K, 128, 56), (1, r9), (-1, r1)), lin(W(K, 184, 8), (k, r8), (-k, r0)),
            lin(W(K, 192, 64), (0.5, W("rl", q0 + 8, 64))) + lin(W(K, 192, 56), (0.5, r9)) + lin(W(K, 248, 8), (0.5, r0)))
        mms(lin(W(P, 128, 64), (1, W("pn", n0 + 64, 64)), (-1, W("pn", n0, 64))))
        plan = c["D" if s else "D0"][h]
        if s:
            fetch(plan, "ru", lambda r: n0 + 8 * ((r & 8) + ((r + 1) & 7)), 2048 * h, Z, c["ZW"][h])
        else:
            fetch(plan, "ru", lambda r: n0 + 8 * ((r + 1) & 15), 2048 * h, Z, c["ZW"][h])
        marks = (lin(W(K, 0, 64), (1, W("C", 0, 64)), (1, NT)),
                 lin(W(K, 64, 64), (1, W("C", 64, 64)), (1, NT)) + lin(W(K, 64, 56), (32, W("rl", q0 + 200, 56)))
                 + lin(W(K, 120, 8), (32, W("rl", q0 + 192, 8))))
        halves = (c["FIRST"][h], 1 - c["FIRST"][h])
        if c["CPS"][h] < 2:
            for k in halves:
                reduce(plan[8 * k:8 * k + 8], K, 64 * k, 2048 * h + 1024 * k, marks[k])
            return
        its = [sums(W(K, 64 * k, 64), 144, "AB", 2048 * h + 1024 * k, 1024) for k in halves]
        for r in runs([r for r, k in enumerate(plan) if k == "r"], 16, lambda r: 8 * r):
            its.insert(c["CUT"][h], sums(W(K, 8 * r[0], 8 * len(r)), 288, "DD", 2048 * h + 128 * r[0], 128 * len(r)))
        k = c["MK"][h]
        its[k] = marks[0][1:] + marks[1][1:] + its[k]
        its[0] = lin(W(K, 0, 128), (1, W("C", 0, 128))) + its[0]
        for i, it in enumerate(its):
            mms(it, start=i == 0, stop=i == len(its) - 1)
            call("k")

    def turn(s, h):
        last = s == ST - 1
        K, P = "K%d" % h, "P%d" % h
        q0, n0, t0 = 512 * s + 256 * h, 256 * s + 128 * h, 256 * h
        Z, NT = W("zl", 4 * n0, 128), W("rl", q0 + 128, 64)
        zw = c["ZW"][h] if c["ZS"] and not last else 1
        ZN, NTN, ZH = W("zs", 4 * n0, 128 * zw), W("rs", q0 + 128, 64), W("rs", q0 + 192, 64)
        U, M, T2, SG, DQ, DH, QA, PA, PU, YS = [t64(k, h) for k in ("U", "M", "T2", "sg", "dq", "dh", "qa", "pa", "pu", "ys")]
        DR, MID, XS, ZB = [W(K, 128 + 64 * j, 64) for j in range(4)]
        PAP, PBP, E, WW, E1 = [W(P, 64 * j, 64) for j in range(5)]
        PLO, PHI, KI = W("pn", n0, 64), W("pn", n0 + 64, 64), W("ki", 8 * h, 8)
        k = 64 * c["FIRST"][h]
        if c["CPS"][h] == 2:
            for b in range(8):
                red(W("ki", 8 * h + b, 1), V(K, b, 128, 8), ALU.max)
                call("ki")
        else:
            if c["CPS"][h]:
                act(W("tr", t0, 64), W(K, k, 64), AF.Identity)
            else:
                cp(W("tr", t0, 64), W(K, k, 64))
            tt(W("tr", t0 + 64, 64), W(K, 64 - k, 64), W("tr", t0, 64), ALU.max)
            tt(W("tr", t0 + 128, 32), W("tr", t0 + 64, 32), W("tr", t0 + 96, 32), ALU.max)
            tt(W("tr", t0 + 160, 16), W("tr", t0 + 128, 16), W("tr", t0 + 144, 16), ALU.max)
            tt(KI, W("tr", t0 + 160, 8), W("tr", t0 + 168, 8), ALU.max)
        tt(U, IND(KI, BC), NT, ALU.subtract)
        ts(M, U, 4, ALU.arith_shift_right, 1, ALU.bitwise_and)
        ts(T2, U, 14, ALU.bitwise_and)
        tt(E, E, M, ALU.mult)
        tt(PA, E, PLO, ALU.add)
        ts(PU, PA, 2048.0, ALU.add)
        ts(ZH, T2, 0.0, ALU.is_equal)
        tt(YS, ZH, PA, ALU.mult)
        YSUM, Y = W("MS", 336 + 8 * h, 8), W("y", 128 * h, 128)
        if c["YT"][h]:
            for n in (32, 16):
                tt(W("ys", 64 * h, n), W("ys", 64 * h, n), W("ys", 64 * h + n, n), ALU.add)
            if c["YT"][h] == 1:
                YSUM = W("ys", 64 * h, 8)
                tt(YSUM, YSUM, W("ys", 64 * h + 8, 8), ALU.add)
        if c["YT"][h] != 1:
            mms(lin(YSUM, *[(1, W("ys", 64 * h + 8 * r, 8)) for r in range(2 if c["YT"][h] else 8)]))
        ts(W("yu", 8 * h, 8), YSUM, 2048.0, ALU.add)
        if c["ZV"][h]:
            tt(W("yd", 128 * h, 128), IND(XW, W("yu", 8 * h, 8)), Z, ALU.subtract)
        cp(Y, IND(XW, W("yu", 8 * h, 8)))
        if c["ZV"][h]:
            act(ZN, W("yd", 128 * h, 128), AF.Abs)
        elif zw > 1:
            mms(*[lin(W("MS", 128 * j, 128), (1, Y), (-1, Z)) for j in range(zw)])
            act(ZN, W("MS", 0, 128 * zw), AF.Abs)
        else:
            mms(lin(W(P, 384, 128), (1, Y), (-1, Z)))
            act(ZN, W(P, 384, 128), AF.Abs)
        call("z")
        ts(NTN, T2, -1.0, ALU.mult, 1.0, ALU.add)
        if not last:
            send(W("zl", 4 * n0 + 1024, 128 * c["ZW"][h]), ZN, "az%d_%d" % (s + 1, h))
        else:
            store(T.yz[:, 128 * h:128 * h + 128], ZN, 2.5)
        if h or c["SC"] == 2:
            u0, n = (8 * h, 8) if c["SC"] == 2 else (0, 16)
            US = W("MS", 256 + u0, n)
            mms(sums(US, 0, "y", 16 * u0, 16 * n))
            ts(W("uh", u0, n), US, HU - 7.5, ALU.add)
            ts(W("uh", 16 + u0, n), US, -2048.0, ALU.add)
            mms(lin(US, (1, W("base", u0, n)), (-1, W("uh", u0, n)), (1, W("uh", 16 + u0, n))))
            ts(W("uu", u0, n), US, 2048.0 - 256 * u0, ALU.add)
        mms(lin(W(K, 384, 128), (1, Y), (1, Z)))
        ts(W("avg", 128 * h, 128), W(K, 384, 128), 0.5, ALU.mult, -0.25, ALU.add)
        SA, SB, k = W("ab", 128 * h, 64), W("ab", 128 * h + 64, 64), -1 if last else 1
        e = 1 if c["SGN"][h] else 2
        if c["SGN"][h]:
            act(W("ab", 128 * h, 128), W(K, 0, 128), AF.Sign, THR)
        else:
            ts(W("ab", 128 * h, 128), W(K, 0, 128), NTH, ALU.is_ge, -0.5, ALU.add)
        mms(lin(ZB, (e, SA), (-e, SB)))
        ts(SG, M, -0.5, ALU.add)
        tt(t64("w", h), ZB, M, ALU.mult)
        tt(DQ, DR, SG, ALU.mult)
        mms(lin(XS, (-k * e, SA), (k, t64("w", h))))
        tt(XS, XS, NTN, ALU.max)
        tt(QA, MID, DQ, ALU.add)
        tt(DH, XS, DQ, ALU.mult)
        tt(W("rs", q0, 64), MID, DH, ALU.add if last else ALU.subtract)
        tt(W("rs", q0 + 64, 64), MID, DH, ALU.subtract if last else ALU.add)
        if not last:
            if c["RU"]:
                ts(W("rv", n0, 128), W("rs", q0, 128), 2048.0, ALU.add)
                send(W("ru", n0 + 256, 128), W("rv", n0, 128), "au%d_%d" % (s + 1, h))
            send(W("rl", q0 + 512, 256), W("rs", q0, 256), "ar%d_%d" % (s + 1, h))
        mms(lin(PAP, (1, PA)), lin(PBP, (1, PLO), (1, PHI), (-1, PA)))
        if c["PV"] & 1:
            tt(E1, PBP, PA, ALU.subtract)
        else:
            mms(lin(E1, (1, PLO), (1, PHI), (-2, PA)))
        if not c["PV"] & 2:
            mms(lin(E, (1, PLO), (1, PHI), (-1, PA), (1, W("C", 192, 64))))
        mms(lin(WW, (2080, PA), (2048, QA), (2, AT)))
        tt(t64("p1", h), PAP, QA, ALU.mult)
        tt(t64("p2", h), WW, t64("p1", h), ALU.add)
        ts(t64("rem", h), t64("p2", h), 5, ALU.arith_shift_right, 4095, ALU.bitwise_and)
        if c["PV"] & 2:
            ts(t64("rc", h), t64("rem", h), -2048.0, ALU.add)
            tt(WW, t64("rc", h), PBP, ALU.subtract)
        else:
            tt(WW, t64("rem", h), E, ALU.subtract)

    def sums_f(s, h):
        plan = c["F" if s < ST - 1 else "FL"][h]
        fetch(plan, "pu", lambda r: 64 * h + 8 * r, 4096 + 1024 * h, W("y", 128 * h, 128))
        reduce(plan, "P%d" % h, 320, 4096 + 1024 * h, [])

    def left(s, h):
        P, n0 = "P%d" % h, 256 * s + 128 * h
        PAP, PBP, E, WW, E1, FK = [W(P, 64 * j, 64) for j in range(6)]
        LC, F1, F2 = t64("lc", h), W("f", 128 * h, 64), W("f", 128 * h + 64, 64)
        if c["SGN"] == (1, 1):
            ts(LC, FK, THR, ALU.add, 0.0, ALU.is_lt)
        else:
            ts(LC, FK, NTH, ALU.is_lt)
        tt(F1, E1, LC, ALU.mult)
        tt(F2, WW, LC, ALU.mult)
        tt(W("ps", n0, 64), PAP, F1, ALU.add)
        tt(W("ps", n0 + 64, 64), PBP, F2, ALU.add)
        if s < ST - 1:
            send(W("pn", n0 + 256, 128), W("ps", n0, 128), "ap%d_%d" % (s + 1, h))

    def limits():
        CNT = W("MS", 272, 64)
        mms([(CNT, BO, t64("lc", 0)), (CNT, BO, t64("lc", 1))])
        red(A, CNT, ALU.add)
        ts(HH, A, HA - 496, ALU.add)
        if 1 in c["SGN"]:
            ts(THR, A, HH, ALU.subtract, CF, ALU.add)
        if 0 in c["SGN"]:
            ts(NTH, HH, A, ALU.subtract, CF, ALU.subtract)
        ts(AT, HALF, A, ALU.mult, -32768.0, ALU.add)

    def names_out(x, bank, h, o):
        for i in range(3):
            n, m0, y, b0 = 8 << i, 1536 * (o // 256) + 768 * h + 256 * i, 128 * (i & 1), 384 * h + 128 * i
            for k in (0, 64):
                tt(W("rm", m0 + k, 64), W(bank, 128 - y + k, 64) if i else W(x[0], x[1] + k, 64), W("bit", b0, 64), ALU.mult)
            if i:
                for k in (0, 64):
                    tt(W("rm", m0 + 128 + k, 64), W(bank, 128 - y + k, 64), W("bit", b0 + 64, 64), ALU.mult)
                it = lin(W(bank, y, 128), (1, W("rm", m0 + 128, 128)))
            else:
                it = lin(W(bank, y, 128), (1, x), (-1, W("rm", m0, 128)))
            for k in (0, 64):
                it += lin(W(bank, y + k + n, 64 - n), (1, W("rm", m0 + k, 64 - n)))
                it += lin(W(bank, y + k, n), (1, W("rm", m0 + k + 64 - n, n)))
            mms(it)
        a, st = W("h1", o + 128 * h, 128), stage()
        cp(a, W(bank, 0, 128))
        it = lin(W("S", st, 128), (1, W("C", 192, 128)))
        for k in range(8):
            for g1 in range(2):
                it.append((W("S", st + 32 * (k >> 1) + 16 * g1, 16), sel(g1, k & 1, a), V("h1", a[1] + k, a[2], 8)))
        mms(it)
        tr32(W("fin", o + 128 * h, 128), W("S", st, 128))

    def names_turned(x, bank, h, o):
        a, b, v0 = W("h1", o + 128 * h, 128), W("h2", o + 128 * h, 128), 8 * o + 1024 * h
        it = lin(W(bank, 0, 128), (1, W("C", 192, 128)))
        for k in range(8):
            for g1 in range(2):
                it.append((W(bank, 32 * (k >> 1) + 16 * g1, 16), sel(g1, k & 1, x), V(x[0], x[1] + k, x[2], 8)))
        mms(it)
        ts(a, W(bank, 0, 128), -2048.0, ALU.add)
        tr32(b, a)
        for k in (0, 4):
            st = stage()
            mms(*[[(W("S", st + 128 * j, 128), wt(1, b, 0.0, 16 + k + j), b)] for j in range(4)])
            if c["EV"][2 * (o // 256) + h] > k:
                cp(W("var", v0 + 128 * k, 512), W("S", st, 512))
            else:
                act(W("var", v0 + 128 * k, 512), W("S", st, 512), AF.Identity)
        act(W("fin", o + 128 * h, 128), IND(W("var", v0, 1024), W("tu", 8 * h, 8)), AF.Identity, 2048.0)

    def finish(k):
        h = int(k[1])
        enter(ST - 1, k)
        if k[0] == "r":
            ts(W("tf", 8 * h, 8), W("T2", 64 * h, 8), 64.0, ALU.mult, c1(11), ALU.add)
            tt(W("tf", 8 * h, 8), W("tf", 8 * h, 8), W("tf", 16, 8), ALU.add)
            cp(W("tu", 8 * h, 8), W("tf", 8 * h, 8))
            names_turned(W("rs", 512 * (ST - 1) + 256 * h, 128), "K%d" % h, h, 0)
            store(T.yr[:, 128 * h:128 * h + 128], W("fin", 128 * h, 128), 2.6)
        else:
            left(ST - 1, h)
            names_turned(W("ps", 256 * (ST - 1) + 128 * h, 128), "P%d" % h, h, 256)
            store(T.yp[:, 128 * h:128 * h + 128], W("fin", 256 + 128 * h, 128), 2.6)

    for s in range(ST):
        last = s == ST - 1
        for h in range(2):
            enter(s, "d%d" % h)
            sums_d(s, h)
        for h in range(2):
            enter(s, "t%d" % h)
            turn(s, h)
            for k in c["END"].split()[:c["END"].split().index("f1")] if last and h else ():
                finish(k)
            enter(s, "f%d" % h)
            sums_f(s, h)
        enter(s, "x")
        XO = V("X2", 0, 4096) if last and c["X2"] else XW
        if c["SC"] == 1:
            cp(IND(XO, W("uu", 0, 16)), W("avg", 0, 256))
        for h in range(2 if c["SC"] == 2 else 0):
            cp(IND(W(XO[0], 2048 * h, 2048), W("uu", 8 * h, 8)), W("avg", 128 * h, 128))
        if s == ST - 2 and c["X2"]:
            load("sp", V("X2", 0, 4096), XW, "l2", 6.5, [XW])
        if last:
            for h in range(2):
                store(T.yx[:, 2048 * h:2048 * h + 2048], W(XO[0], 2048 * h, 2048), 4.4)
            enter(s, "e")
            break
        for h in range(2):
            left(s, h)
        limits()

    for k in c["END"].split()[c["END"].split().index("f1") + 1:]:
        finish(k)
    for h in range(0 if c["FIN"] else 2):
        for i in range(3):
            b0 = 384 * h + 128 * i
            ts(W("bit", b0, 64), IND(W("T2", 64 * h, 8), BC), i + 1, ALU.arith_shift_right, 1, ALU.bitwise_and)
            if i:
                ts(W("bit", b0 + 64, 64), W("bit", b0, 64), 0.0, ALU.is_equal)
        names_out(W("rs", 512 * (ST - 1) + 256 * h, 128), "K%d" % h, h, 0)
        store(T.yr[:, 128 * h:128 * h + 128], W("fin", 128 * h, 128), 2.6)
    for h in range(0 if c["FIN"] else 2):
        left(ST - 1, h)
        names_out(W("ps", 256 * (ST - 1) + 128 * h, 128), "P%d" % h, h, 256)
        store(T.yp[:, 128 * h:128 * h + 128], W("fin", 256 + 128 * h, 128), 2.6)
    k = ops.index("head")
    return ops[:k] + head + ops[k + 1:], nstore[0], nsent[0]


def conflicts(ops):
    hist, out = {}, []
    for n, o in enumerate(ops):
        deps = set()
        if o[0] == "far":
            deps.add(n - 1)
        else:
            for v, m in o[2]:
                for (k, a, b, w) in hist.get(v[0], []):
                    if a < v[2] and v[1] < b and (w != m or m == "w") and ops[k][3] != "":
                        deps.add(k)
        deps.discard(n)
        out.append(deps)
        for v, m in o[2]:
            if m == "w" and v[3] == 1:
                hist[v[0]] = [e for e in hist.get(v[0], []) if not (v[1] <= e[1] and e[2] <= v[2])]
        for v, m in o[2]:
            hist.setdefault(v[0], []).append((n, v[1], v[2], m))
    above = []
    for n, deps in enumerate(out):
        far = 0
        for k in deps:
            far |= above[k]
        above.append(far | sum(1 << k for k in deps))
        out[n] = {k for k in deps if not far >> k & 1}
    return out


def with_banks(ops, deps, order):
    seen, out = {}, [None] * len(ops)
    for j in order:
        d = set(deps[j])
        for b in ops[j][6]:
            s = seen.setdefault(b, {})
            d.update(k for q, k in s.items() if q != ops[j][0])
            s[ops[j][0]] = j
        out[j] = d
    return out


def figures(g, T):
    out, keep = [], dict(CFG)
    for m in keep["models"]:
        CFG.update(m)
        out.append(([o[5] for o in build(g, T, (0, 0), 0, 0)[0]], CFG["far"], CFG["wake"]))
        CFG.update(keep)
    return out


def replay(ops, deps, order, d, far, wake):
    free, seen, start, end, why = {}, {}, [0.0] * len(ops), [0.0] * len(ops), [None] * len(ops)
    for j in order:
        q = ops[j][0]
        t, w = free.get(q, (0.0, None))
        for k in deps[j]:
            p = ops[k][0]
            x = end[k] + ((0.0 if q == "pe" else wake + 0.1) if p == "pe" else 0.0 if q == "far" else wake)
            if x > t:
                t, w = x, k
        for b in ops[j][6]:
            s = seen.setdefault(b, {})
            for p, k in s.items():
                if p != q:
                    x = end[k] + wake + (0.1 if p == "pe" else 0.0)
                    if x > t:
                        t, w = x, k
            s[q] = j
        start[j], end[j], why[j] = t, t + d[j], w
        free[q] = (t + (d[j] - far if q == "far" else 0.05 if q == "sp" or q == "act" and ops[j][3] else d[j]), j)
    return start, end, why


def plan(ops, deps, others):
    c = CFG
    n = len(ops)
    kids = [[] for _ in ops]
    for j in range(n):
        for k in deps[j]:
            kids[k].append(j)

    def gap(k, j):
        if ops[k][0] == "pe":
            return 0.0 if ops[j][0] == "pe" else c["wake"] + 0.1
        return 0.0 if ops[j][0] == "far" else c["wake"]
    dur = [o[5] for o in ops]
    hold = [0.05 if o[3] is not None and o[0] in ("sp", "act") else o[5] - c["far"] if o[0] == "far" else o[5] for o in ops]
    lag = [c["wake"] + (0.1 if o[0] == "pe" else 0.0) for o in ops]
    pre = [[(k, gap(k, j)) for k in deps[j]] for j in range(n)]
    post = [[(k, gap(j, k)) for k in kids[j]] for j in range(n)]
    named = {}
    for j, o in enumerate(ops):
        named.setdefault(o[7][:2], []).append(j)
    for names in c["order"]:
        seq = [j for s in range(ST + 1) for k in names.split() for j in named.get((s - (k[0] == "-"), k.lstrip("-")), [])]
        for i, j in zip(seq, seq[1:]):
            pre[j].append((i, 0.0))
            post[i].append((j, 0.0))
    topo, left = [j for j in range(n) if not pre[j]], [len(p) for p in pre]
    for j in topo:
        for k, _ in post[j]:
            left[k] -= 1
            if not left[k]:
                topo.append(k)
    assert len(topo) == n

    def place(seq, back):
        busy, used, start = {}, {}, [0.0] * n
        for j in seq:
            if back:
                t = max([start[k] + hold[k] + d for k, d in post[j]] + [0.0]) + dur[j] - hold[j]
            else:
                t = max([start[k] + dur[k] + d for k, d in pre[j]] + [0.0])
            q, h = ops[j][0], hold[j]
            l = busy.setdefault(q, [])
            while True:
                i = len(l)
                while i > 0 and l[i - 1][1] > t + 1e-9:
                    i -= 1
                while i < len(l) and l[i][0] < t + h - 1e-9:
                    t = max(t, l[i][1])
                    i += 1
                t0 = t
                for b in ops[j][6]:
                    for (x, y, p) in used.get(b, ())[-24:]:
                        if ops[p][0] != q:
                            before, after = (lag[p], lag[j]) if back else (lag[j], lag[p])
                            if x < t + h + before - 1e-9 and t < y + after - 1e-9:
                                t = y + after
                if t == t0:
                    break
            l.insert(i, (t, t + h))
            for b in ops[j][6]:
                used.setdefault(b, []).append((t, t + h, j))
            start[j] = t
        return start

    def spans(start):
        seq = sorted(range(n), key=lambda j: (start[j], j))
        return [max(replay(ops, deps, seq, d, far, wake)[1]) for d, far, wake in others]
    prio = [0.0] * n
    for j in reversed(topo):
        prio[j] = dur[j] + max([prio[k] + d for k, d in post[j]] + [0.0])

    span = max(prio)
    for j in range(n):
        if dur[j] < c["short"] and ops[j][0] in ("dve", "pe"):
            prio[j] += c["bonus"]

    def settle(key):
        for j in topo:
            for k, _ in pre[j]:
                if key[k] >= key[j]:
                    key[j] = key[k] + 1e-6
        return place(sorted(range(n), key=lambda j: (key[j], j)), False)
    def pull(key):
        for j in reversed(topo):
            for k, _ in post[j]:
                if key[j] > key[k] - dur[j]:
                    key[j] = key[k] - dur[j]
        return settle(key)
    start = pull([-prio[j] for j in range(n)])
    base = spans(start)
    best = (float(len(base)), start)
    lead, keep, x = {}, {}, 777 + c["seed"]
    for it in range(c["blame"]):
        seq = sorted(range(n), key=lambda j: (start[j], j))
        runs = [replay(ops, deps, seq, d, far, wake) for d, far, wake in others]
        score = sum(max(r[1]) / b for r, b in zip(runs, base))
        if score < best[0]:
            best, keep = (score, start), dict(lead)
        elif it % c["back"] == 0:
            lead = dict(keep)
        x = (x * 1103515245 + 12345) % 2147483648
        t0, end, why = runs[(x >> 8) % len(runs)]
        j, late = max(range(n), key=lambda j: end[j]), {}
        while why[j] is not None:
            if why[j] not in deps[j]:
                late[ops[j][7][1:]] = (j, why[j])
            j = why[j]
        late = list(late.values())
        for _ in range(1 + (x >> 20) % 3):
            x = (x * 1103515245 + 12345) % 2147483648
            j, i = late[(x >> 8) % len(late)]
            k, d = (ops[j][7][1:], 1) if (x >> 6) % 2 else (ops[i][7][1:], -1)
            lead[k] = lead.get(k, 0.0) + d * c["step"] * ((x >> 16) % 16 + 1) / 8
        start = pull([-prio[j] - lead.get(ops[j][7][1:], 0.0) for j in range(n)])
    start = best[1]
    for _ in range(c["rounds"]):
        late = place(sorted(range(n), key=lambda j: (-start[j] - dur[j], -j)), True)
        start = place(sorted(range(n), key=lambda j: (-late[j] - hold[j], j)), False)
        score = sum(a / b for a, b in zip(spans(start), base))
        if score < best[0]:
            best = (score, start)
    first, cur = spans(best[1]), best
    tags = {}
    tag = np.array([tags.setdefault(o[7][1:], len(tags)) for o in ops])
    model = [j for j in range(n) if ops[j][7][0] == 2]
    x = np.arange(n, dtype=np.int64) * 7919 + c["seed"]
    for it in range(c["search"]):
        x = (x * 1103515245 + 12345) % 2147483648
        amp = c["jit"] * (0.2 + (int(x[1]) % 100) / 100)
        now, r = np.array(cur[1]), (x >> 8) / 8388608.0 - 0.5
        if it % 3 == 2:
            key = now + amp * r * (abs(now - now[int(x[0] >> 4) % n]) < c["win"])
        else:
            mid, hit = now[model[int(x[0] >> 4) % len(model)]], np.zeros(n)
            for j in model:
                hit[tag[j]] = abs(now[j] - mid) < c["win"]
            key = now + amp * (r * hit)[tag]
        start = settle(list(key))
        score = sum(a / b for a, b in zip(spans(start), base))
        if score <= cur[0] + c["heat"] * (1 - it / c["search"]) * (int(x[2] >> 8) % 100) / 100:
            cur = (score, start)
        if score <= best[0]:
            best = (score, start)
    loads = [j for j in range(n) if ops[j][3] and ops[j][0] != "far" and not deps[j]]
    order = loads + sorted(set(range(n)) - set(loads), key=lambda j: (best[1][j], j))

    same = {o[7]: j for j, o in enumerate(ops)}

    qs = [o[0] for o in ops]
    fast = []
    for d, far, wake in others:
        lagm = [wake + (0.1 if q == "pe" else 0.0) for q in qs]
        fast.append((d, [d[j] - far if qs[j] == "far" else hold[j] if hold[j] != dur[j] else d[j] for j in range(n)], lagm,
                     [[(k, 0.0 if qs[j] == "far" or qs[j] == qs[k] == "pe" else lagm[k]) for k in deps[j]] for j in range(n)]))

    def judge(seq):
        free, seen, links = {}, {}, []
        for j in seq:
            q, other = qs[j], ()
            if ops[j][6]:
                other = []
                for b in ops[j][6]:
                    s = seen.setdefault(b, {})
                    other += [k for p, k in s.items() if p != q]
                    s[q] = j
            links.append((j, free.get(q), other))
            free[q] = j
        runs = []
        for d, hd, lagm, before in fast:
            start, end, why = [0.0] * n, [0.0] * n, [None] * n
            for j, w, other in links:
                t = 0.0 if w is None else start[w] + hd[w]
                for k, x in before[j]:
                    x += end[k]
                    if x > t:
                        t, w = x, k
                for k in other:
                    x = end[k] + lagm[k]
                    if x > t:
                        t, w = x, k
                start[j], end[j], why[j] = t, t + d[j], w
            runs.append((start, end, why))
        return sum((max(r[1]) + c["mean"] * sum(r[1]) / n) / b for r, b in zip(runs, base)), runs

    def moved(seq, i, j, way):
        seq, done = list(seq), False
        steps = range(ST) if ops[i][7][0] >= 0 and way & 2 else [0]
        for s in steps:
            a, b = i, j
            if len(steps) > 1:
                a = same.get((s,) + ops[i][7][1:])
                b = same.get((s + ops[j][7][0] - ops[i][7][0],) + ops[j][7][1:])
                if a is None or b is None or ops[a][0] != ops[i][0] or ops[b][0] != ops[j][0]:
                    continue
            pa, pb = seq.index(a), seq.index(b)
            if pa > pb:
                continue
            part = seq[pa:pb + 1]
            if way & 1:
                take = {b}
                for k in reversed(part):
                    if k in take:
                        take.update(deps[k])
                if a in take:
                    continue
                seq[pa:pb + 1] = [k for k in part if k in take] + [k for k in part if k not in take]
            else:
                take = {a}
                for k in part:
                    if deps[k] & take:
                        take.add(k)
                if b in take:
                    continue
                seq[pa:pb + 1] = [k for k in part if k not in take] + [k for k in part if k in take]
            done = True
        return seq if done else None
    cur = (order,) + judge(order)
    best, x = cur, 12345 + c["seed"]
    for it in range(c["swaps"]):
        x = (x * 1103515245 + 12345) % 2147483648
        start, end, why = cur[2][(x >> 8) % len(others)]
        j, pairs = max(range(n), key=lambda j: end[j]) if it % 2 else (x >> 6) % n, []
        while why[j] is not None and (it % 2 or len(pairs) < 6):
            if why[j] not in deps[j] and why[j] not in loads:
                pairs.append((why[j], j))
            j = why[j]
        if not pairs:
            continue
        i, j = pairs[(x >> 12) % len(pairs)]
        if (x >> 20) % 2 and ops[i][0] == ops[j][0]:
            if (x >> 24) % 2:
                ready = max([end[k] for k in deps[j]] + [0.0]) if (x >> 5) % 2 else start[j] - c["reach"]
                can = [k for k in cur[0] if ops[k][0] == ops[j][0] and ready - 0.3 < start[k] < start[j] and k not in loads]
                i = can[(x >> 9) % len(can)] if can else i
            else:
                can = [k for k in cur[0] if ops[k][0] == ops[j][0] and start[j] <= start[k] < start[j] + 1.5]
                j = can[(x >> 9) % len(can)]
        seq = moved(cur[0], i, j, (x >> 24) % 4 | (2 if (x >> 28) % 2 else 0))
        if seq:
            new = (seq,) + judge(seq)
            if new[1] <= cur[1] + c["heat"] * (1 - it / c["swaps"]) * ((x >> 4) % 64) / 64:
                cur = new
                if new[1] < best[1]:
                    best = new
    c["span"] = [round(v, 1) for v in [span] + base + first + [max(r[1]) for r in best[2]]]
    return best[0]


def emit(g, T, ops, deps, order, nstore, nsent, neng):
    queues = {"pe": g.tensor, "dve": g.vector, "act": g.scalar, "pool": g, "sp": g.sync}
    known = {q: {} for q in queues}
    pos = {q: 0 for q in queues}
    rank = {j: i for i, j in enumerate(order)}
    clock, waits, sig, needed = {}, {}, {}, set()
    for n in order:
        q, sem = ops[n][0], ops[n][3]
        if sem:
            sig[n] = (sem, 1)
        elif sem is None:
            pos[q] += 1
            sig[n] = (q, pos[q])
        else:
            sig[n] = None
        mine, ck = [], {}
        if q != "far":
            kn = known[q]
            for k in sorted(deps[n], key=lambda k: -rank[k]):
                if q == "pe" and ops[k][0] == "pe":
                    continue
                s, p = sig[k]
                if kn.get(s, 0) >= p:
                    continue
                mine.append(k)
                needed.add(k)
                for s2, p2 in clock[k].items():
                    if kn.get(s2, 0) < p2:
                        kn[s2] = p2
            ck = dict(kn)
        if sig[n] is not None:
            ck[sig[n][0]] = max(ck.get(sig[n][0], 0), sig[n][1])
        clock[n], waits[n] = ck, mine
    count = {q: 0 for q in queues}
    value = {}
    for n in order:
        o = ops[n]
        if o[3] is None and n in needed:
            count[o[0]] += 1
            value[n] = count[o[0]]
        elif o[3]:
            value[n] = o[4]
    for n in order:
        o = ops[n]
        if o[0] == "far":
            continue
        for k in waits[n]:
            queues[o[0]].wait_ge(T.sem[sig[k][0]], value[k])
        ins = o[1]()
        if o[3] is None and n in needed:
            ins.then_inc(T.sem[o[0]], 1)
    g.sync.wait_ge(T.sem.stored, 16 * nstore)
    g.wait_ge(T.sem.sent, neng * nsent)


def rank_program(g, core, T, topo):
    rank = T.rank_of(core)
    if rank is None:
        return
    nxt = T.cores[(rank + 1) % len(T.cores)]
    neng = len(topo.engines(core, nxt))
    ops, nstore, nsent = build(g, T, topo.addr(nxt), topo.mask(core, nxt), neng)
    if not PLANS:
        deps = conflicts(ops)
        order = plan(ops, deps, figures(g, T))
        PLANS["it"] = (with_banks(ops, deps, order), order)
    emit(g, T, ops, PLANS["it"][0], PLANS["it"][1], nstore, nsent, neng)
